import numpy as np
import ml_dtypes


def mxq(x, axis, fmt="e4m3"):
    dtype, down = {"e4m3": (ml_dtypes.float8_e4m3fn, 7), "e5m2": (ml_dtypes.float8_e5m2, 14)}[fmt]
    v = np.moveaxis(np.asarray(x, np.float32).astype(ml_dtypes.bfloat16).astype(np.float64), axis, -1)
    blocks = v.reshape(v.shape[:-1] + (-1, 32))
    amax = np.abs(blocks).max(-1, keepdims=True)
    byte = np.maximum(np.where(amax > 0, np.frexp(amax)[1] - 1 + 127, 0) - down, 1)
    scale = np.exp2(byte - 127.0)
    codes = (blocks / scale).astype(np.float32).astype(dtype).astype(np.float64)
    return np.moveaxis((codes * scale).reshape(v.shape), -1, axis)


WIDE = False


def mx_kscale(k):
    if not WIDE:
        return np.ones(k)
    levels = np.array([30, -30])
    if k % 512:
        return np.exp2(np.random.permutation(np.resize(levels, k // 32))).repeat(32)
    a = np.empty((k // 512, 16))
    for p in range(k // 512):
        a[p, :8] = np.random.permutation(np.resize(levels, 8))
        for g in range(8):
            far = levels[np.abs(levels - a[p, g]) >= 10]
            a[p, g + 8] = far[np.random.randint(len(far))]
    return np.exp2(a.ravel()).repeat(32)


def f64(x):
    return np.asarray(x).astype(np.float64)


E2M1 = np.array([0.0, 0.5, 1.0, 1.5, 2.0, 3.0, 4.0, 6.0, -0.0, -0.5, -1.0, -1.5, -2.0, -3.0, -4.0, -6.0])


def pack_weight(w, fmt):
    k, n = w.shape
    w = f64(np.asarray(w, np.float32).astype(ml_dtypes.bfloat16)).reshape(k // 32, 32, n)
    amax = np.abs(w).max(1)
    if fmt == "e4m3":
        byte = np.frexp(amax)[1] - 1 + 127 - 7
    else:
        mant, ex = np.frexp(amax / 6.0)
        byte = np.where(mant > 0.5, ex, ex - 1) + 127
    byte = np.clip(np.where(amax > 0, byte, 1), 1, 254)
    scaled = (w * np.exp2(127.0 - byte)[:, None, :]).reshape(k, n).astype(np.float32)
    by_word = np.ascontiguousarray(scaled.reshape(k // 512, 128, 4, n).transpose(0, 1, 3, 2))
    if fmt == "e4m3":
        words = by_word.astype(ml_dtypes.float8_e4m3fn).view(np.uint8)
    else:
        c = by_word.astype(ml_dtypes.float4_e2m1fn).view(np.uint8) & 0xF
        words = (c[..., 0::2] | (c[..., 1::2] << 4)).reshape(k // 512, 128, 2 * n)
    return np.ascontiguousarray(words), np.ascontiguousarray(byte.astype(np.uint8).reshape(k // 512, 16, n))


def unpack_weight(words, scales, fmt):
    g, _, n = scales.shape
    words = np.ascontiguousarray(words).reshape(g, 128, n, -1)
    if fmt == "e4m3":
        vals = words.view(ml_dtypes.float8_e4m3fn).astype(np.float64)
    else:
        nib = np.empty((g, 128, n, 4), np.uint8)
        nib[..., 0::2] = words & 0xF
        nib[..., 1::2] = words >> 4
        vals = E2M1[nib]
    vals = vals * np.repeat(np.exp2(scales.astype(np.float64) - 127.0), 8, axis=1)[..., None]
    return vals.transpose(0, 1, 3, 2).reshape(g * 512, n)


K, N, T = 1024, 512, 1024


def setup_inputs():
    n = np.random.standard_normal
    s = mx_kscale(K)[:, None]
    m = np.exp(0.5 * n((1, T)))
    p_w4 = pack_weight(n((K, N)) / np.sqrt(K) / s, "e2m1")
    return {
        "g": (m * n((K, T)) * s).astype(np.float32),
        "w4_words": p_w4[0],
        "w4_scales": p_w4[1],
        "res": (n((N, T))).astype(np.float32),
        "ls": (np.random.uniform(0.25, 1.0, N)).astype(np.float32),
    }


def reference(g, w4_words, w4_scales, res, ls):
    g_q_ = mxq(f64(g), 0, "e5m2")
    g_r_ = mxq(f64(g) - g_q_, 0, "e4m3")
    w4_ = unpack_weight(w4_words, w4_scales, "e2m1")
    dx = w4_.T @ g_q_ + w4_.T @ g_r_
    return f64(res) + dx * f64(ls)[:, None]

@@ -1,0 +1,137 @@
+from contextlib import ExitStack
+
+import concourse.mybir as mybir
+from concourse.masks import make_identity
+
+K, N, T = 1024, 512, 1024
+FLOPS = 2 * 2 * K * N * T
+F32 = mybir.dt.float32
+BF16 = mybir.dt.bfloat16
+U32 = mybir.dt.uint32
+I32 = mybir.dt.int32
+U8 = mybir.dt.uint8
+E4 = mybir.dt.float8_e4m3fn_x4
+E5 = mybir.dt.float8_e5m2_x4
+E2 = mybir.dt.float4_e2m1fn_x4
+ALU = mybir.AluOpType
+P = 128
+W = 256
+ORDER = """Lg:0 Lg:1 Lg:2 Lg:3 Lg:4 Lg:5 Lg:6 Lg:7 Lw Lr:0 Lr:1
+AV:0 B:0 AS:1:0 AV:1:1 B:1 M:0:0:0 M:0:1:1 M:0:2:2 AS:2 AS:3 AS:4 AS:5
+C:0:0 M:0:3:0 B:2 C:0:1 C:0:2 B:3 M:1:0:1 M:1:1:2 C:0:3 M:1:2:0 DS:0 AS:6 AS:7
+C:1:0 M:1:3:1 B:4 C:1:1 C:1:2 B:5 M:2:0:2 M:2:1:0 C:1:3 M:2:2:1 DS:1 DS:2 DS:3 X:q:0:0:3 X:q:0:1:4 X:q:0:2:5 X:q:0:3:6
+C:2:0 M:2:3:2 E:0 C:2:1 X:q:1:0:3 X:q:1:1:4 B:6 C:2:2 B:7 M:3:0:0 M:3:1:1 C:2:3 M:3:2:2 X:q:1:2:5 X:q:1:3:6 DS:4 DS:5 
+C:3:0 M:3:3:0 E:1 X:r:0:0:3 X:r:0:1:4 X:r:0:2:5 X:r:0:3:6  C:3:1 E:2 C:3:2 C:3:3 DS:6 X:q:2:0:7 X:q:2:1:0 X:q:2:2:1  E:3 X:r:1:0:3 X:r:1:1:4 X:r:1:2:5 X:r:1:3:6 X:q:2:3:2 X:q:3:0:7 X:q:3:1:0 X:q:3:2:1 X:q:3:3:2 DV:7 F:0:0 E:4 F:0:1 E:7 E:5  X:r:2:0:7 X:r:2:1:0 X:r:2:2:1 X:r:2:3:2 F:0:2 E:6  X:r:3:0:7 X:r:3:1:0 X:r:3:2:1 X:r:3:3:2 F:0:3 F:1:0 F:1:1 F:1:2 F:1:3"""
+
+
+def tile_mix_tierg_ls_kernel(tc, g, w4_words, w4_scales, res, ls, out):
+    nc = tc.nc
+    with ExitStack() as ctx:
+        sb = ctx.enter_context(tc.tile_pool(name="sb", bufs=1))
+        psum = ctx.enter_context(tc.psum_pool(name="psum", bufs=1))
+        ctx.enter_context(tc.manual_schedule())
+
+        graw = [sb.tile([P, 2, 4, W], F32, name="graw%d" % c, align_bytes=64) for c in range(4)]
+        gb = [sb.tile([P, W, 4], BF16, name="gb%d" % i, align_bytes=64) for i in range(8)]
+        rb = [sb.tile([P, 2, 4, W], BF16, name="rb%d" % c, align_bytes=64) for c in range(4)]
+        ri = [sb.tile([P, W, 4], BF16, name="ri%d" % i, align_bytes=64) for i in range(8)]
+        qc = [sb.tile([P, 512], U32, name="qc%d" % c, align_bytes=64) for c in range(4)]
+        qs = [sb.tile([P, 512], U8, name="qs%d" % c, align_bytes=64) for c in range(4)]
+        rc = [sb.tile([P, 512], U32, name="rc%d" % c, align_bytes=64) for c in range(4)]
+        rs = [sb.tile([P, 512], U8, name="rs%d" % c, align_bytes=64) for c in range(4)]
+        w = sb.tile([P, 2, 2 * N], U8, name="w", align_bytes=64)
+        ws = sb.tile([P, 2, N], U8, name="ws", align_bytes=64)
+        lsc = sb.tile([P, 4], F32, name="lsc", align_bytes=64)
+        rt = [sb.tile([P, 4, 512], F32, name="rt%d" % h, align_bytes=64) for h in range(2)]
+        ot = [sb.tile([P, 512], F32, name="ot%d" % i, align_bytes=64) for i in range(8)]
+        eye = sb.tile([P, P], BF16, name="eye", align_bytes=64)
+        eye4 = sb.tile([P, 4, P, 4], BF16, name="eye4", align_bytes=64)
+        ic = sb.tile([P, 512], U32, name="ic", align_bytes=64)
+        isc = sb.tile([P, 512], U8, name="isc", align_bytes=64)
+
+        make_identity(nc, eye[:])
+        nc.vector.memset(eye4[:].rearrange("p j m i -> p (j m i)"), 0.0)
+        nc.vector.memset(ws[:].rearrange("p a n -> p (a n)").bitcast(I32), 0)
+        for j in range(4):
+            nc.scalar.copy(out=eye4[:, j, :, j], in_=eye[:])
+        nc.vector.quantize_mx(out=ic[:].bitcast(E4), scales=isc[:], in_=eye4[:].rearrange("p j m i -> p (j m i)"))
+
+        def interleave(eng, dst, src, p):
+            lo, hi = (0, W) if len(p) == 2 else (int(p[2]) * W // 2, (int(p[2]) + 1) * W // 2)
+            o = dst[:, lo:hi, :].rearrange("p (c i) t -> p c t i", i=4)
+            s = src[:, :, lo:hi].rearrange("p t (c i) -> p c t i", i=4)
+            if eng == "V":
+                nc.vector.tensor_copy(out=o, in_=s)
+            elif eng == "S":
+                nc.scalar.copy(out=o, in_=s)
+            else:
+                nc.gpsimd.tensor_scalar(out=o, in0=s, scalar1=1.0, scalar2=0.0, op0=ALU.mult, op1=ALU.add)
+
+        deq = {}
+        acc = {}
+        count = {}
+        for tok in ORDER.split():
+            p = tok.split(":")
+            k = p[0]
+            if k == "Lg":
+                i = int(p[1])
+                c, u = divmod(i, 2)
+                h, a = divmod(c, 2)
+                t0 = h * 512 + u * W
+                nc.sync.dma_start(out=graw[c][:, u, :, :], in_=g[a * 512:(a + 1) * 512, t0:t0 + W].rearrange("(p j) w -> p j w", j=4))
+            elif k == "Lw":
+                nc.sync.dma_start(out=w[:], in_=w4_words.rearrange("a p n -> p a n"))
+                for q in range(4):
+                    nc.sync.dma_start(out=ws[32 * q:32 * q + 4, :, :].bitcast(I32), in_=w4_scales[:, 4 * q:4 * q + 4, :].rearrange("a r n -> r a n").bitcast(I32))
+                with nc.allow_non_contiguous_dma("one factor a partition"):
+                    nc.sync.dma_start(out=lsc[:], in_=ls.rearrange("(c p) -> p c", p=P))
+            elif k == "Lr":
+                h = int(p[1])
+                nc.sync.dma_start(out=rt[h][:], in_=res[:, h * 512:(h + 1) * 512].rearrange("(c p) t -> p c t", p=P))
+            elif k[0] == "A":
+                i = int(p[1])
+                interleave(k[1], gb[i], graw[i // 2][:, i % 2, :, :], p)
+            elif k[0] == "D":
+                i = int(p[1])
+                interleave(k[1], ri[i], rb[i // 2][:, i % 2, :, :], p)
+            elif k == "B":
+                i = int(p[1])
+                cols = slice((i % 2) * W, (i % 2 + 1) * W)
+                nc.vector.quantize_mx(out=qc[i // 2][:, cols].bitcast(E5), scales=qs[i // 2][:, cols], in_=gb[i][:].rearrange("p w j -> p (w j)"))
+            elif k == "E":
+                i = int(p[1])
+                cols = slice((i % 2) * W, (i % 2 + 1) * W)
+                nc.vector.quantize_mx(out=rc[i // 2][:, cols].bitcast(E4), scales=rs[i // 2][:, cols], in_=ri[i][:].rearrange("p w j -> p (w j)"))
+            elif k == "M":
+                c, j, b = int(p[1]), int(p[2]), int(p[3])
+                bank = psum.tile([P, 512], F32, name="deq%d_%d" % (c, j), tag="bank%d" % b)
+                deq[(c, j)] = bank
+                cols = slice(j * P, (j + 1) * P)
+                nc.tensor.matmul_mx(out=bank[:], lhsT=ic[:, cols].bitcast(E4), lhsT_scale=isc[:, cols],
+                                    rhs=qc[c][:].bitcast(E5), rhs_scale=qs[c][:], start=True, stop=True)
+            elif k == "C":
+                c, j = int(p[1]), int(p[2])
+                nc.vector.tensor_tensor(out=rb[c][:, :, j, :], in0=graw[c][:, :, j, :],
+                                        in1=deq[(c, j)][:].rearrange("p (u w) -> p u w", u=2), op=ALU.subtract)
+            elif k == "H":
+                i, j = int(p[1]), int(p[2])
+                c, u = divmod(i, 2)
+                nc.vector.tensor_tensor(out=rb[c][:, u, j, :], in0=graw[c][:, u, j, :],
+                                        in1=deq[(c, j)][:, u * W:(u + 1) * W], op=ALU.subtract)
+            elif k == "X":
+                tier, c, n, b = p[1], int(p[2]), int(p[3]), int(p[4])
+                h, a = divmod(c, 2)
+                if (h, n) not in acc:
+                    acc[(h, n)] = psum.tile([P, 512], F32, name="acc%d_%d" % (h, n), tag="bank%d" % b)
+                    count[(h, n)] = 0
+                count[(h, n)] = count[(h, n)] + 1
+                codes, scales = (qc[c][:].bitcast(E5), qs[c][:]) if tier == "q" else (rc[c][:].bitcast(E4), rs[c][:])
+                nc.tensor.matmul_mx(out=acc[(h, n)][:], lhsT=w[:, a, 2 * P * n:2 * P * (n + 1)].bitcast(E2),
+                                    lhsT_scale=ws[:, a, P * n:P * (n + 1)], rhs=codes, rhs_scale=scales,
+                                    start=count[(h, n)] == 1, stop=count[(h, n)] == 4)
+            elif k == "F":
+                h, n = int(p[1]), int(p[2])
+                o = ot[4 * h + n]
+                nc.vector.scalar_tensor_tensor(out=o[:], in0=acc[(h, n)][:], scalar=lsc[:, n:n + 1], in1=rt[h][:, n, :],
+                                               op0=ALU.mult, op1=ALU.add)
+                nc.sync.dma_start(out=out[n * P:(n + 1) * P, h * 512:(h + 1) * 512], in_=o[:])

@@ -16,12 +16,12 @@ E2 = mybir.dt.float4_e2m1fn_x4
 ALU = mybir.AluOpType
 P = 128
 W = 256
-ORDER = """Lg:0 Lg:1 Lg:2 Lg:3 Lg:4 Lg:5 Lg:6 Lg:7 Lw Lr:0 Lr:1
-AV:0 B:0 AS:1:0 AV:1:1 B:1 M:0:0:0 M:0:1:1 M:0:2:2 AS:2 AS:3 AS:4 AS:5
-C:0:0 M:0:3:0 B:2 C:0:1 C:0:2 B:3 M:1:0:1 M:1:1:2 C:0:3 M:1:2:0 DS:0 AS:6 AS:7
-C:1:0 M:1:3:1 B:4 C:1:1 C:1:2 B:5 M:2:0:2 M:2:1:0 C:1:3 M:2:2:1 DS:1 DS:2 DS:3 X:q:0:0:3 X:q:0:1:4 X:q:0:2:5 X:q:0:3:6
-C:2:0 M:2:3:2 E:0 C:2:1 X:q:1:0:3 X:q:1:1:4 B:6 C:2:2 B:7 M:3:0:0 M:3:1:1 C:2:3 M:3:2:2 X:q:1:2:5 X:q:1:3:6 DS:4 DS:5 
-C:3:0 M:3:3:0 E:1 X:r:0:0:3 X:r:0:1:4 X:r:0:2:5 X:r:0:3:6  C:3:1 E:2 C:3:2 C:3:3 DS:6 X:q:2:0:7 X:q:2:1:0 X:q:2:2:1  E:3 X:r:1:0:3 X:r:1:1:4 X:r:1:2:5 X:r:1:3:6 X:q:2:3:2 X:q:3:0:7 X:q:3:1:0 X:q:3:2:1 X:q:3:3:2 DV:7 F:0:0 E:4 F:0:1 E:7 E:5  X:r:2:0:7 X:r:2:1:0 X:r:2:2:1 X:r:2:3:2 F:0:2 E:6  X:r:3:0:7 X:r:3:1:0 X:r:3:2:1 X:r:3:3:2 F:0:3 F:1:0 F:1:1 F:1:2 F:1:3"""
+ORDER = """Lg:0 Lg:1 Lg:2 Lg:3 Lg:4 Lg:5 Lw Lg:6 Lg:7 Lr:0 Lr:1
+AV:0 B:0 AS:1:0 AV:1:1 B:1 M:0:0:0 M:0:1:1 M:0:2:2 AS:2:0 AV:2:1 AS:3 AS:4 AS:5 B:2
+C:0:0 M:0:3:0 C:0:1 B:3 C:0:2 M:1:0:1 M:1:1:2 C:0:3 M:1:2:0 DS:0 AS:6 AS:7
+C:1:0 M:1:3:1 B:4 C:1:1 B:5 C:1:2 X:q:0:0:3 X:q:0:1:4 M:2:0:2 M:2:1:0 C:1:3 X:q:0:2:5 M:2:2:1 DS:1 DS:2 DS:3  X:q:0:3:6
+C:2:0 M:2:3:2 E:0 B:6 X:q:1:0:3 X:q:1:1:4 C:2:1 B:7  X:q:1:2:5 X:q:1:3:6 C:2:2  M:3:0:0 M:3:1:1 C:2:3 M:3:2:2  X:q:2:0:7 X:q:3:0:7 DS:4 DS:5 E:1
+C:3:0 M:3:3:0 X:r:0:0:3 X:r:0:1:4 X:r:0:2:5 X:r:0:3:6  C:3:1 E:2 X:q:2:1:1 X:q:3:1:1 C:3:2 E:3 X:r:1:0:3 X:r:1:1:4 X:r:1:2:5 X:r:1:3:6 C:3:3  DS:6 X:q:2:2:2 X:q:2:3:0 X:q:3:2:2 X:q:3:3:0 E:4  DV:7 E:5 X:r:2:0:7 X:r:2:1:1 X:r:2:2:2 X:r:2:3:0  F:0:0 E:7 F:0:1 E:6  X:r:3:0:7 X:r:3:1:1 X:r:3:2:2 X:r:3:3:0 F:0:2 F:0:3 F:1:0 F:1:1 F:1:2 F:1:3:0 F:1:3:1"""
 
 
 def tile_mix_tierg_ls_kernel(tc, g, w4_words, w4_scales, res, ls, out):
@@ -31,7 +31,8 @@ def tile_mix_tierg_ls_kernel(tc, g, w4_words, w4_scales, res, ls, out):
         psum = ctx.enter_context(tc.psum_pool(name="psum", bufs=1))
         ctx.enter_context(tc.manual_schedule())
 
-        graw = [sb.tile([P, 2, 4, W], F32, name="graw%d" % c, align_bytes=64) for c in range(4)]
+        gflat = [sb.tile([P, 8 * W], F32, name="graw%d" % c, align_bytes=64) for c in range(4)]
+        graw = [t[:].rearrange("p (u j w) -> p u j w", u=2, j=4) for t in gflat]
         gb = [sb.tile([P, W, 4], BF16, name="gb%d" % i, align_bytes=64) for i in range(8)]
         rb = [sb.tile([P, 2, 4, W], BF16, name="rb%d" % c, align_bytes=64) for c in range(4)]
         ri = [sb.tile([P, W, 4], BF16, name="ri%d" % i, align_bytes=64) for i in range(8)]
@@ -49,11 +50,15 @@ def tile_mix_tierg_ls_kernel(tc, g, w4_words, w4_scales, res, ls, out):
         ic = sb.tile([P, 512], U32, name="ic", align_bytes=64)
         isc = sb.tile([P, 512], U8, name="isc", align_bytes=64)
 
+        warm = sb.tile([P, 16], F32, name="warm", align_bytes=64)
+        warm2 = sb.tile([P, 16], F32, name="warm2", align_bytes=64)
+        nc.vector.memset(warm[:], 0.0)
+        nc.scalar.copy(out=warm2[:], in_=warm[:])
         make_identity(nc, eye[:])
-        nc.vector.memset(eye4[:].rearrange("p j m i -> p (j m i)"), 0.0)
-        nc.vector.memset(ws[:].rearrange("p a n -> p (a n)").bitcast(I32), 0)
+        nc.vector.memset(eye4[:].rearrange("p j m i -> p (j m i)").bitcast(I32), 0)
+        nc.gpsimd.memset(ws[:].rearrange("p a n -> p (a n)").bitcast(I32), 0)
         for j in range(4):
-            nc.scalar.copy(out=eye4[:, j, :, j], in_=eye[:])
+            nc.vector.tensor_copy(out=eye4[:, j, :, j], in_=eye[:])
         nc.vector.quantize_mx(out=ic[:].bitcast(E4), scales=isc[:], in_=eye4[:].rearrange("p j m i -> p (j m i)"))
 
         def interleave(eng, dst, src, p):
@@ -132,6 +137,7 @@ def tile_mix_tierg_ls_kernel(tc, g, w4_words, w4_scales, res, ls, out):
             elif k == "F":
                 h, n = int(p[1]), int(p[2])
                 o = ot[4 * h + n]
-                nc.vector.scalar_tensor_tensor(out=o[:], in0=acc[(h, n)][:], scalar=lsc[:, n:n + 1], in1=rt[h][:, n, :],
+                lo, hi = (0, 512) if len(p) == 3 else (int(p[3]) * W, (int(p[3]) + 1) * W)
+                nc.vector.scalar_tensor_tensor(out=o[:, lo:hi], in0=acc[(h, n)][:, lo:hi], scalar=lsc[:, n:n + 1], in1=rt[h][:, n, lo:hi],
                                                op0=ALU.mult, op1=ALU.add)
-                nc.sync.dma_start(out=out[n * P:(n + 1) * P, h * 512:(h + 1) * 512], in_=o[:])
+                nc.sync.dma_start(out=out[n * P:(n + 1) * P, h * 512 + lo:h * 512 + hi], in_=o[:, lo:hi])

@@ -16,12 +16,12 @@ E2 = mybir.dt.float4_e2m1fn_x4
 ALU = mybir.AluOpType
 P = 128
 W = 256
-ORDER = """Lg:0 Lg:1 Lg:2 Lg:3 Lg:4 Lg:5 Lw Lg:6 Lg:7 Lr:0 Lr:1
-AV:0 B:0 AS:1:0 AV:1:1 B:1 M:0:0:0 M:0:1:1 M:0:2:2 AS:2:0 AV:2:1 AS:3 AS:4 AS:5 B:2
-C:0:0 M:0:3:0 C:0:1 B:3 C:0:2 M:1:0:1 M:1:1:2 C:0:3 M:1:2:0 DS:0 AS:6 AS:7
-C:1:0 M:1:3:1 B:4 C:1:1 B:5 C:1:2 X:q:0:0:3 X:q:0:1:4 M:2:0:2 M:2:1:0 C:1:3 X:q:0:2:5 M:2:2:1 DS:1 DS:2 DS:3  X:q:0:3:6
-C:2:0 M:2:3:2 E:0 B:6 X:q:1:0:3 X:q:1:1:4 C:2:1 B:7  X:q:1:2:5 X:q:1:3:6 C:2:2  M:3:0:0 M:3:1:1 C:2:3 M:3:2:2  X:q:2:0:7 X:q:3:0:7 DS:4 DS:5 E:1
-C:3:0 M:3:3:0 X:r:0:0:3 X:r:0:1:4 X:r:0:2:5 X:r:0:3:6  C:3:1 E:2 X:q:2:1:1 X:q:3:1:1 C:3:2 E:3 X:r:1:0:3 X:r:1:1:4 X:r:1:2:5 X:r:1:3:6 C:3:3  DS:6 X:q:2:2:2 X:q:2:3:0 X:q:3:2:2 X:q:3:3:0 E:4  DV:7 E:5 X:r:2:0:7 X:r:2:1:1 X:r:2:2:2 X:r:2:3:0  F:0:0 E:7 F:0:1 E:6  X:r:3:0:7 X:r:3:1:1 X:r:3:2:2 X:r:3:3:0 F:0:2 F:0:3 F:1:0 F:1:1 F:1:2 F:1:3:0 F:1:3:1"""
+ORDER = """Lg:0 Lg:1 Ls Lg:2 Lg:3 Lg:4 Lg:5 Lw Lg:6 Lg:7 Lr:0 Ll Lr:1
+AV:0 B:0 AS:1:0 AV:1:1 B:1 M:0:0:0 M:0:1:1 M:0:2:2 AS:2:0 AV:2:1 AS:3:0 AS:4  B:2
+C:0:0 M:0:3:0 AV:3:1 C:0:1 B:3 M:1:0:1 AG:5 C:0:2 M:1:1:2 C:0:3 M:1:2:0 DS:0 DS:1 AS:6 
+C:1:0 M:1:3:1 X:q:0:0:3 X:q:0:1:4 X:q:0:2:5 X:q:0:3:6 C:1:1 B:4 B:5 M:2:0:2 AG:7 C:1:2 M:2:1:0 X:q:1:0:3 C:1:3  M:2:2:1 X:q:1:1:4 DS:2 DS:3  
+C:2:0 M:2:3:2 X:q:1:2:5 X:q:1:3:6 C:2:1 C:2:2 B:6 B:7 M:3:0:0 M:3:1:1 M:3:2:7 E:0 E:1 X:r:0:0:3 X:r:0:1:4 C:2:3 M:3:3:2 X:r:0:2:5 X:r:0:3:6 DS:4 E:2 E:3 DG:5 X:r:1:0:3 X:r:1:1:4 X:r:1:2:5 X:r:1:3:6
+H:6:0 H:6:1 H:6:2 H:6:3 DS:6 H:7:0 X:q:2:0:0 X:q:3:0:0 H:7:1 X:q:2:1:1 X:q:3:1:1 H:7:2 X:q:2:2:7 X:q:3:2:7 H:7:3 DS:7 E:4 E:5 X:r:2:0:0 X:r:2:1:1 X:r:2:2:7 X:q:2:3:2 X:q:3:3:2 F:0:0 E:6 F:0:1 E:7 X:r:3:0:0 X:r:3:1:1 X:r:2:3:2 X:r:3:2:7 X:r:3:3:2 F:0:2 F:0:3 F:1:0 F:1:1 F:1:2 F:1:3:0 F:1:3:1"""
 
 
 def tile_mix_tierg_ls_kernel(tc, g, w4_words, w4_scales, res, ls, out):
@@ -33,9 +33,9 @@ def tile_mix_tierg_ls_kernel(tc, g, w4_words, w4_scales, res, ls, out):
 
         gflat = [sb.tile([P, 8 * W], F32, name="graw%d" % c, align_bytes=64) for c in range(4)]
         graw = [t[:].rearrange("p (u j w) -> p u j w", u=2, j=4) for t in gflat]
-        gb = [sb.tile([P, W, 4], BF16, name="gb%d" % i, align_bytes=64) for i in range(8)]
+        gb = {}
         rb = [sb.tile([P, 2, 4, W], BF16, name="rb%d" % c, align_bytes=64) for c in range(4)]
-        ri = [sb.tile([P, W, 4], BF16, name="ri%d" % i, align_bytes=64) for i in range(8)]
+        ri = {}
         qc = [sb.tile([P, 512], U32, name="qc%d" % c, align_bytes=64) for c in range(4)]
         qs = [sb.tile([P, 512], U8, name="qs%d" % c, align_bytes=64) for c in range(4)]
         rc = [sb.tile([P, 512], U32, name="rc%d" % c, align_bytes=64) for c in range(4)]
@@ -70,7 +70,7 @@ def tile_mix_tierg_ls_kernel(tc, g, w4_words, w4_scales, res, ls, out):
             elif eng == "S":
                 nc.scalar.copy(out=o, in_=s)
             else:
-                nc.gpsimd.tensor_scalar(out=o, in0=s, scalar1=1.0, scalar2=0.0, op0=ALU.mult, op1=ALU.add)
+                nc.gpsimd.tensor_scalar(out=dst[:], in0=src.rearrange("p t w -> p w t"), scalar1=1.0, scalar2=0.0, op0=ALU.mult, op1=ALU.add)
 
         deq = {}
         acc = {}
@@ -86,8 +86,10 @@ def tile_mix_tierg_ls_kernel(tc, g, w4_words, w4_scales, res, ls, out):
                 nc.sync.dma_start(out=graw[c][:, u, :, :], in_=g[a * 512:(a + 1) * 512, t0:t0 + W].rearrange("(p j) w -> p j w", j=4))
             elif k == "Lw":
                 nc.sync.dma_start(out=w[:], in_=w4_words.rearrange("a p n -> p a n"))
+            elif k == "Ls":
                 for q in range(4):
-                    nc.sync.dma_start(out=ws[32 * q:32 * q + 4, :, :].bitcast(I32), in_=w4_scales[:, 4 * q:4 * q + 4, :].rearrange("a r n -> r a n").bitcast(I32))
+                    nc.scalar.dma_start(out=ws[32 * q:32 * q + 4, :, :].bitcast(I32), in_=w4_scales[:, 4 * q:4 * q + 4, :].rearrange("a r n -> r a n").bitcast(I32))
+            elif k == "Ll":
                 with nc.allow_non_contiguous_dma("one factor a partition"):
                     nc.sync.dma_start(out=lsc[:], in_=ls.rearrange("(c p) -> p c", p=P))
             elif k == "Lr":
@@ -95,9 +97,13 @@ def tile_mix_tierg_ls_kernel(tc, g, w4_words, w4_scales, res, ls, out):
                 nc.sync.dma_start(out=rt[h][:], in_=res[:, h * 512:(h + 1) * 512].rearrange("(c p) t -> p c t", p=P))
             elif k[0] == "A":
                 i = int(p[1])
+                if i not in gb:
+                    gb[i] = sb.tile([P, W, 4], BF16, name="gb%d" % i, tag="gbodd" if i in (3, 5, 7) else "gb%d" % i, align_bytes=64)
                 interleave(k[1], gb[i], graw[i // 2][:, i % 2, :, :], p)
             elif k[0] == "D":
                 i = int(p[1])
+                if i not in ri:
+                    ri[i] = sb.tile([P, W, 4], BF16, name="ri%d" % i, tag="riodd" if i in (3, 5) else "ri%d" % i, align_bytes=64)
                 interleave(k[1], ri[i], rb[i // 2][:, i % 2, :, :], p)
             elif k == "B":
                 i = int(p[1])

@@ -16,12 +16,12 @@ E2 = mybir.dt.float4_e2m1fn_x4
 ALU = mybir.AluOpType
 P = 128
 W = 256
-ORDER = """Lg:0 Lg:1 Ls Lg:2 Lg:3 Lg:4 Lg:5 Lw Lg:6 Lg:7 Lr:0 Ll Lr:1
-AV:0 B:0 AS:1:0 AV:1:1 B:1 M:0:0:0 M:0:1:1 M:0:2:2 AS:2:0 AV:2:1 AS:3:0 AS:4  B:2
-C:0:0 M:0:3:0 AV:3:1 C:0:1 B:3 M:1:0:1 AG:5 C:0:2 M:1:1:2 C:0:3 M:1:2:0 DS:0 DS:1 AS:6 
-C:1:0 M:1:3:1 X:q:0:0:3 X:q:0:1:4 X:q:0:2:5 X:q:0:3:6 C:1:1 B:4 B:5 M:2:0:2 AG:7 C:1:2 M:2:1:0 X:q:1:0:3 C:1:3  M:2:2:1 X:q:1:1:4 DS:2 DS:3  
-C:2:0 M:2:3:2 X:q:1:2:5 X:q:1:3:6 C:2:1 C:2:2 B:6 B:7 M:3:0:0 M:3:1:1 M:3:2:7 E:0 E:1 X:r:0:0:3 X:r:0:1:4 C:2:3 M:3:3:2 X:r:0:2:5 X:r:0:3:6 DS:4 E:2 E:3 DG:5 X:r:1:0:3 X:r:1:1:4 X:r:1:2:5 X:r:1:3:6
-H:6:0 H:6:1 H:6:2 H:6:3 DS:6 H:7:0 X:q:2:0:0 X:q:3:0:0 H:7:1 X:q:2:1:1 X:q:3:1:1 H:7:2 X:q:2:2:7 X:q:3:2:7 H:7:3 DS:7 E:4 E:5 X:r:2:0:0 X:r:2:1:1 X:r:2:2:7 X:q:2:3:2 X:q:3:3:2 F:0:0 E:6 F:0:1 E:7 X:r:3:0:0 X:r:3:1:1 X:r:2:3:2 X:r:3:2:7 X:r:3:3:2 F:0:2 F:0:3 F:1:0 F:1:1 F:1:2 F:1:3:0 F:1:3:1"""
+ORDER = """Lg:0 Lg:1 Lg:2 Lg:3 Lg:4 Lg:5 Lw Ls Lg:6 Lg:7 Lr:0 Ll Lr:1
+AV:0 B:0 AS:1:0 AV:1:1 B:1 M:0:0:0 M:0:1:1 M:0:2:2 AS:2:0 AV:2:1 AS:3:0 AS:4 AS:5 B:2
+C:0:0 M:0:3:0 AV:3:1 C:0:1 B:3 M:1:0:1 C:0:2 M:1:1:2 C:0:3 M:1:2:0 DS:0 AS:6 AS:7
+C:1:0 M:1:3:1 C:1:1 B:4 B:5 M:2:0:2 DG:1 X:q:0:0:3 C:1:2 M:2:1:0 X:q:0:1:4 C:1:3  M:2:2:1 X:q:0:2:5 DS:2 DS:3  
+C:2:0 M:2:3:2 X:q:0:3:6 X:q:1:0:3 X:q:1:1:4 X:q:1:2:5 X:q:1:3:6 C:2:1 C:2:2 E:0 E:1 X:r:0:0:3 X:r:0:1:4 B:6 B:7 M:3:0:0 M:3:1:1 M:3:2:7   C:2:3 M:3:3:2 X:r:0:2:5 X:r:0:3:6 DS:4 E:2 
+H:6:0 H:6:1 E:3 DG:5 X:r:1:0:3 X:r:1:1:4 X:r:1:2:5 X:r:1:3:6 H:6:2 H:6:3 DS:6 H:7:0 X:q:2:0:0 X:q:3:0:0 H:7:1 X:q:2:1:1 X:q:3:1:1 H:7:2 X:q:2:2:7 X:q:3:2:7 H:7:3 X:q:2:3:2 X:q:3:3:2 DS:7 F:0:0 F:0:1 E:4 E:5 X:r:2:0:0 X:r:2:1:1 E:6 E:7 X:r:3:0:0 X:r:3:1:1 X:r:2:2:7 X:r:3:2:7 X:r:2:3:2 X:r:3:3:2 F:0:2 F:0:3 F:1:0 F:1:1 F:1:2 F:1:3:0 F:1:3:1"""
 
 
 def tile_mix_tierg_ls_kernel(tc, g, w4_words, w4_scales, res, ls, out):
@@ -88,7 +88,7 @@ def tile_mix_tierg_ls_kernel(tc, g, w4_words, w4_scales, res, ls, out):
                 nc.sync.dma_start(out=w[:], in_=w4_words.rearrange("a p n -> p a n"))
             elif k == "Ls":
                 for q in range(4):
-                    nc.scalar.dma_start(out=ws[32 * q:32 * q + 4, :, :].bitcast(I32), in_=w4_scales[:, 4 * q:4 * q + 4, :].rearrange("a r n -> r a n").bitcast(I32))
+                    nc.sync.dma_start(out=ws[32 * q:32 * q + 4, :, :].bitcast(I32), in_=w4_scales[:, 4 * q:4 * q + 4, :].rearrange("a r n -> r a n").bitcast(I32))
             elif k == "Ll":
                 with nc.allow_non_contiguous_dma("one factor a partition"):
                     nc.sync.dma_start(out=lsc[:], in_=ls.rearrange("(c p) -> p c", p=P))
@@ -98,12 +98,12 @@ def tile_mix_tierg_ls_kernel(tc, g, w4_words, w4_scales, res, ls, out):
             elif k[0] == "A":
                 i = int(p[1])
                 if i not in gb:
-                    gb[i] = sb.tile([P, W, 4], BF16, name="gb%d" % i, tag="gbodd" if i in (3, 5, 7) else "gb%d" % i, align_bytes=64)
+                    gb[i] = sb.tile([P, W, 4], BF16, name="gb%d" % i, tag="slota" if i == 5 else "gb%d" % i, align_bytes=64)
                 interleave(k[1], gb[i], graw[i // 2][:, i % 2, :, :], p)
             elif k[0] == "D":
                 i = int(p[1])
                 if i not in ri:
-                    ri[i] = sb.tile([P, W, 4], BF16, name="ri%d" % i, tag="riodd" if i in (3, 5) else "ri%d" % i, align_bytes=64)
+                    ri[i] = sb.tile([P, W, 4], BF16, name="ri%d" % i, tag="riodd" if i in (3, 5) else "slota" if i == 1 else "ri%d" % i, align_bytes=64)
                 interleave(k[1], ri[i], rb[i // 2][:, i % 2, :, :], p)
             elif k == "B":
                 i = int(p[1])

@@ -5,23 +5,34 @@ from concourse.masks import make_identity
 
 K, N, T = 1024, 512, 1024
 FLOPS = 2 * 2 * K * N * T
+
 F32 = mybir.dt.float32
 BF16 = mybir.dt.bfloat16
 U32 = mybir.dt.uint32
 I32 = mybir.dt.int32
 U8 = mybir.dt.uint8
-E4 = mybir.dt.float8_e4m3fn_x4
-E5 = mybir.dt.float8_e5m2_x4
-E2 = mybir.dt.float4_e2m1fn_x4
+E4M3 = mybir.dt.float8_e4m3fn_x4
+E5M2 = mybir.dt.float8_e5m2_x4
+E2M1 = mybir.dt.float4_e2m1fn_x4
 ALU = mybir.AluOpType
+
 P = 128
-W = 256
-ORDER = """Lg:0 Lg:1 Lg:2 Lg:3 Lg:4 Lg:5 Lw Ls Lg:6 Lg:7 Lr:0 Ll Lr:1
-AV:0 B:0 AS:1:0 AV:1:1 B:1 M:0:0:0 M:0:1:1 M:0:2:2 AS:2:0 AV:2:1 AS:3:0 AS:4 AS:5 B:2
-C:0:0 M:0:3:0 AV:3:1 C:0:1 B:3 M:1:0:1 C:0:2 M:1:1:2 C:0:3 M:1:2:0 DS:0 AS:6 AS:7
-C:1:0 M:1:3:1 C:1:1 B:4 B:5 M:2:0:2 DG:1 X:q:0:0:3 C:1:2 M:2:1:0 X:q:0:1:4 C:1:3  M:2:2:1 X:q:0:2:5 DS:2 DS:3  
-C:2:0 M:2:3:2 X:q:0:3:6 X:q:1:0:3 X:q:1:1:4 X:q:1:2:5 X:q:1:3:6 C:2:1 C:2:2 E:0 E:1 X:r:0:0:3 X:r:0:1:4 B:6 B:7 M:3:0:0 M:3:1:1 M:3:2:7   C:2:3 M:3:3:2 X:r:0:2:5 X:r:0:3:6 DS:4 E:2 
-H:6:0 H:6:1 E:3 DG:5 X:r:1:0:3 X:r:1:1:4 X:r:1:2:5 X:r:1:3:6 H:6:2 H:6:3 DS:6 H:7:0 X:q:2:0:0 X:q:3:0:0 H:7:1 X:q:2:1:1 X:q:3:1:1 H:7:2 X:q:2:2:7 X:q:3:2:7 H:7:3 X:q:2:3:2 X:q:3:3:2 DS:7 F:0:0 F:0:1 E:4 E:5 X:r:2:0:0 X:r:2:1:1 E:6 E:7 X:r:3:0:0 X:r:3:1:1 X:r:2:2:7 X:r:3:2:7 X:r:2:3:2 X:r:3:3:2 F:0:2 F:0:3 F:1:0 F:1:1 F:1:2 F:1:3:0 F:1:3:1"""
+PACK = 4
+K_PASS = P * PACK
+CHUNK = 512
+PIECE = CHUNK // 2
+PASSES = K // K_PASS
+HALVES = T // CHUNK
+CHUNKS = PASSES * HALVES
+N_TILES = N // P
+LINE = 4
+SCALAR_SHARE_IDLE = 96
+SCALAR_SHARE_BUSY = 160
+WARM_PASSES = 4
+
+ROTATING_BANKS = 3
+FIRST_HALF_BANKS = (3, 4, 5, 6)
+LAST_CHUNK_BANKS = (0, 1, 7, 2)
 
 
 def tile_mix_tierg_ls_kernel(tc, g, w4_words, w4_scales, res, ls, out):
@@ -31,119 +42,290 @@ def tile_mix_tierg_ls_kernel(tc, g, w4_words, w4_scales, res, ls, out):
         psum = ctx.enter_context(tc.psum_pool(name="psum", bufs=1))
         ctx.enter_context(tc.manual_schedule())
 
-        gflat = [sb.tile([P, 8 * W], F32, name="graw%d" % c, align_bytes=64) for c in range(4)]
-        graw = [t[:].rearrange("p (u j w) -> p u j w", u=2, j=4) for t in gflat]
-        gb = {}
-        rb = [sb.tile([P, 2, 4, W], BF16, name="rb%d" % c, align_bytes=64) for c in range(4)]
-        ri = {}
-        qc = [sb.tile([P, 512], U32, name="qc%d" % c, align_bytes=64) for c in range(4)]
-        qs = [sb.tile([P, 512], U8, name="qs%d" % c, align_bytes=64) for c in range(4)]
-        rc = [sb.tile([P, 512], U32, name="rc%d" % c, align_bytes=64) for c in range(4)]
-        rs = [sb.tile([P, 512], U8, name="rs%d" % c, align_bytes=64) for c in range(4)]
-        w = sb.tile([P, 2, 2 * N], U8, name="w", align_bytes=64)
-        ws = sb.tile([P, 2, N], U8, name="ws", align_bytes=64)
-        lsc = sb.tile([P, 4], F32, name="lsc", align_bytes=64)
-        rt = [sb.tile([P, 4, 512], F32, name="rt%d" % h, align_bytes=64) for h in range(2)]
-        ot = [sb.tile([P, 512], F32, name="ot%d" % i, align_bytes=64) for i in range(8)]
-        eye = sb.tile([P, P], BF16, name="eye", align_bytes=64)
-        eye4 = sb.tile([P, 4, P, 4], BF16, name="eye4", align_bytes=64)
-        ic = sb.tile([P, 512], U32, name="ic", align_bytes=64)
-        isc = sb.tile([P, 512], U8, name="isc", align_bytes=64)
+        def tiles(name, count, shape, dtype):
+            return [sb.tile(shape, dtype, name="%s%d" % (name, i), align_bytes=64) for i in range(count)]
 
-        warm = sb.tile([P, 16], F32, name="warm", align_bytes=64)
-        warm2 = sb.tile([P, 16], F32, name="warm2", align_bytes=64)
-        nc.vector.memset(warm[:], 0.0)
-        nc.scalar.copy(out=warm2[:], in_=warm[:])
+        g_rows = [
+            t[:].rearrange("p (u j w) -> p u j w", u=2, j=PACK) for t in tiles("g_rows", CHUNKS, [P, PACK * CHUNK], F32)
+        ]
+        rest_rows = tiles("rest_rows", CHUNKS, [P, 2, PACK, PIECE], BF16)
+        q_codes = tiles("q_codes", CHUNKS, [P, CHUNK], U32)
+        q_scales = tiles("q_scales", CHUNKS, [P, CHUNK], U8)
+        r_codes = tiles("r_codes", CHUNKS, [P, CHUNK], U32)
+        r_scales = tiles("r_scales", CHUNKS, [P, CHUNK], U8)
+        w_words = sb.tile([P, PASSES, 2 * N], U8, align_bytes=64)
+        w_scales = sb.tile([P, PASSES, N], U8, align_bytes=64)
+        ls_cols = sb.tile([P, N_TILES], F32, align_bytes=64)
+        res_tiles = tiles("res", HALVES, [P, N_TILES, CHUNK], F32)
+        out_tiles = tiles("out", HALVES * N_TILES, [P, CHUNK], F32)
+        eye = sb.tile([P, P], BF16, align_bytes=64)
+        eye_words = sb.tile([P, PACK, P, PACK], BF16, align_bytes=64)
+        eye_codes = sb.tile([P, PACK * P], U32, align_bytes=64)
+        eye_scales = sb.tile([P, PACK * P], U8, align_bytes=64)
+
+        warm_in = sb.tile([P, 16], F32, align_bytes=64)
+        warm_out = sb.tile([P, 16], F32, align_bytes=64)
+        nc.vector.memset(warm_in[:], 0.0)
+        nc.scalar.copy(out=warm_out[:], in_=warm_in[:])
+
         make_identity(nc, eye[:])
-        nc.vector.memset(eye4[:].rearrange("p j m i -> p (j m i)").bitcast(I32), 0)
-        nc.gpsimd.memset(ws[:].rearrange("p a n -> p (a n)").bitcast(I32), 0)
-        for j in range(4):
-            nc.vector.tensor_copy(out=eye4[:, j, :, j], in_=eye[:])
-        nc.vector.quantize_mx(out=ic[:].bitcast(E4), scales=isc[:], in_=eye4[:].rearrange("p j m i -> p (j m i)"))
+        nc.vector.memset(eye_words[:].rearrange("p j m i -> p (j m i)").bitcast(I32), 0)
+        nc.gpsimd.memset(w_scales[:].rearrange("p a n -> p (a n)").bitcast(I32), 0)
+        for j in range(PACK):
+            nc.vector.tensor_copy(out=eye_words[:, j, :, j], in_=eye[:])
+        nc.vector.quantize_mx(
+            out=eye_codes[:].bitcast(E4M3), scales=eye_scales[:], in_=eye_words[:].rearrange("p j m i -> p (j m i)")
+        )
 
-        def interleave(eng, dst, src, p):
-            lo, hi = (0, W) if len(p) == 2 else (int(p[2]) * W // 2, (int(p[2]) + 1) * W // 2)
-            o = dst[:, lo:hi, :].rearrange("p (c i) t -> p c t i", i=4)
-            s = src[:, :, lo:hi].rearrange("p t (c i) -> p c t i", i=4)
-            if eng == "V":
-                nc.vector.tensor_copy(out=o, in_=s)
-            elif eng == "S":
-                nc.scalar.copy(out=o, in_=s)
-            else:
-                nc.gpsimd.tensor_scalar(out=dst[:], in0=src.rearrange("p t w -> p w t"), scalar1=1.0, scalar2=0.0, op0=ALU.mult, op1=ALU.add)
+        warm_bank = psum.tile([P, CHUNK], F32, tag="bank%d" % LAST_CHUNK_BANKS[2])
+        for j in range(WARM_PASSES):
+            nc.tensor.matmul_mx(
+                out=warm_bank[:],
+                lhsT=eye_codes[:, 0:P].bitcast(E4M3),
+                lhsT_scale=eye_scales[:, 0:P],
+                rhs=eye_codes[:].bitcast(E5M2),
+                rhs_scale=eye_scales[:],
+                start=True,
+                stop=True,
+            )
 
-        deq = {}
-        acc = {}
-        count = {}
-        for tok in ORDER.split():
-            p = tok.split(":")
-            k = p[0]
-            if k == "Lg":
-                i = int(p[1])
-                c, u = divmod(i, 2)
-                h, a = divmod(c, 2)
-                t0 = h * 512 + u * W
-                nc.sync.dma_start(out=graw[c][:, u, :, :], in_=g[a * 512:(a + 1) * 512, t0:t0 + W].rearrange("(p j) w -> p j w", j=4))
-            elif k == "Lw":
-                nc.sync.dma_start(out=w[:], in_=w4_words.rearrange("a p n -> p a n"))
-            elif k == "Ls":
-                for q in range(4):
-                    nc.sync.dma_start(out=ws[32 * q:32 * q + 4, :, :].bitcast(I32), in_=w4_scales[:, 4 * q:4 * q + 4, :].rearrange("a r n -> r a n").bitcast(I32))
-            elif k == "Ll":
-                with nc.allow_non_contiguous_dma("one factor a partition"):
-                    nc.sync.dma_start(out=lsc[:], in_=ls.rearrange("(c p) -> p c", p=P))
-            elif k == "Lr":
-                h = int(p[1])
-                nc.sync.dma_start(out=rt[h][:], in_=res[:, h * 512:(h + 1) * 512].rearrange("(c p) t -> p c t", p=P))
-            elif k[0] == "A":
-                i = int(p[1])
-                if i not in gb:
-                    gb[i] = sb.tile([P, W, 4], BF16, name="gb%d" % i, tag="slota" if i == 5 else "gb%d" % i, align_bytes=64)
-                interleave(k[1], gb[i], graw[i // 2][:, i % 2, :, :], p)
-            elif k[0] == "D":
-                i = int(p[1])
-                if i not in ri:
-                    ri[i] = sb.tile([P, W, 4], BF16, name="ri%d" % i, tag="riodd" if i in (3, 5) else "slota" if i == 1 else "ri%d" % i, align_bytes=64)
-                interleave(k[1], ri[i], rb[i // 2][:, i % 2, :, :], p)
-            elif k == "B":
-                i = int(p[1])
-                cols = slice((i % 2) * W, (i % 2 + 1) * W)
-                nc.vector.quantize_mx(out=qc[i // 2][:, cols].bitcast(E5), scales=qs[i // 2][:, cols], in_=gb[i][:].rearrange("p w j -> p (w j)"))
-            elif k == "E":
-                i = int(p[1])
-                cols = slice((i % 2) * W, (i % 2 + 1) * W)
-                nc.vector.quantize_mx(out=rc[i // 2][:, cols].bitcast(E4), scales=rs[i // 2][:, cols], in_=ri[i][:].rearrange("p w j -> p (w j)"))
-            elif k == "M":
-                c, j, b = int(p[1]), int(p[2]), int(p[3])
-                bank = psum.tile([P, 512], F32, name="deq%d_%d" % (c, j), tag="bank%d" % b)
-                deq[(c, j)] = bank
-                cols = slice(j * P, (j + 1) * P)
-                nc.tensor.matmul_mx(out=bank[:], lhsT=ic[:, cols].bitcast(E4), lhsT_scale=isc[:, cols],
-                                    rhs=qc[c][:].bitcast(E5), rhs_scale=qs[c][:], start=True, stop=True)
-            elif k == "C":
-                c, j = int(p[1]), int(p[2])
-                nc.vector.tensor_tensor(out=rb[c][:, :, j, :], in0=graw[c][:, :, j, :],
-                                        in1=deq[(c, j)][:].rearrange("p (u w) -> p u w", u=2), op=ALU.subtract)
-            elif k == "H":
-                i, j = int(p[1]), int(p[2])
-                c, u = divmod(i, 2)
-                nc.vector.tensor_tensor(out=rb[c][:, u, j, :], in0=graw[c][:, u, j, :],
-                                        in1=deq[(c, j)][:, u * W:(u + 1) * W], op=ALU.subtract)
-            elif k == "X":
-                tier, c, n, b = p[1], int(p[2]), int(p[3]), int(p[4])
-                h, a = divmod(c, 2)
-                if (h, n) not in acc:
-                    acc[(h, n)] = psum.tile([P, 512], F32, name="acc%d_%d" % (h, n), tag="bank%d" % b)
-                    count[(h, n)] = 0
-                count[(h, n)] = count[(h, n)] + 1
-                codes, scales = (qc[c][:].bitcast(E5), qs[c][:]) if tier == "q" else (rc[c][:].bitcast(E4), rs[c][:])
-                nc.tensor.matmul_mx(out=acc[(h, n)][:], lhsT=w[:, a, 2 * P * n:2 * P * (n + 1)].bitcast(E2),
-                                    lhsT_scale=ws[:, a, P * n:P * (n + 1)], rhs=codes, rhs_scale=scales,
-                                    start=count[(h, n)] == 1, stop=count[(h, n)] == 4)
-            elif k == "F":
-                h, n = int(p[1]), int(p[2])
-                o = ot[4 * h + n]
-                lo, hi = (0, 512) if len(p) == 3 else (int(p[3]) * W, (int(p[3]) + 1) * W)
-                nc.vector.scalar_tensor_tensor(out=o[:, lo:hi], in0=acc[(h, n)][:, lo:hi], scalar=lsc[:, n:n + 1], in1=rt[h][:, n, lo:hi],
-                                               op0=ALU.mult, op1=ALU.add)
-                nc.sync.dma_start(out=out[n * P:(n + 1) * P, h * 512 + lo:h * 512 + hi], in_=o[:, lo:hi])
+        g_words = {}
+        rest_words = {}
+        g_q = {}
+        sums = {}
+        passes_done = {}
+
+        def piece_cols(i):
+            return slice((i % 2) * PIECE, (i % 2 + 1) * PIECE)
+
+        def load_g(i):
+            h, a = divmod(i // 2, PASSES)
+            t0 = h * CHUNK + (i % 2) * PIECE
+            rows = g[a * K_PASS : (a + 1) * K_PASS, t0 : t0 + PIECE]
+            nc.sync.dma_start(out=g_rows[i // 2][:, i % 2, :, :], in_=rows.rearrange("(p j) w -> p j w", j=PACK))
+
+        def load_res(h):
+            cols = res[:, h * CHUNK : (h + 1) * CHUNK]
+            nc.sync.dma_start(out=res_tiles[h][:], in_=cols.rearrange("(c p) t -> p c t", p=P))
+
+        def interleave(copy, dst, src, lo, hi):
+            copy(
+                out=dst[:, lo:hi, :].rearrange("p (c i) j -> p c j i", i=LINE),
+                in_=src[:, :, lo:hi].rearrange("p j (c i) -> p c j i", i=LINE),
+            )
+
+        def round_g(copy, i, lo=0, hi=PIECE):
+            if i not in g_words:
+                name = "g_words%d" % i
+                g_words[i] = sb.tile([P, PIECE, PACK], BF16, name=name, tag=name, align_bytes=64)
+            interleave(copy, g_words[i], g_rows[i // 2][:, i % 2, :, :], lo, hi)
+
+        def interleave_rest_on_scalar(i):
+            name = "rest_words%d" % i
+            rest_words[i] = sb.tile([P, PIECE, PACK], BF16, name=name, tag=name, align_bytes=64)
+            interleave(nc.scalar.copy, rest_words[i], rest_rows[i // 2][:, i % 2, :, :], 0, PIECE)
+
+        def interleave_rest_on_gpsimd(i, slot):
+            rest_words[i] = sb.tile([P, PIECE, PACK], BF16, name="rest_words%d" % i, tag=slot, align_bytes=64)
+            nc.gpsimd.tensor_scalar(
+                out=rest_words[i][:],
+                in0=rest_rows[i // 2][:, i % 2, :, :].rearrange("p j w -> p w j"),
+                scalar1=1.0,
+                scalar2=0.0,
+                op0=ALU.mult,
+                op1=ALU.add,
+            )
+
+        def quantise_g(i):
+            nc.vector.quantize_mx(
+                out=q_codes[i // 2][:, piece_cols(i)].bitcast(E5M2),
+                scales=q_scales[i // 2][:, piece_cols(i)],
+                in_=g_words[i][:].rearrange("p w j -> p (w j)"),
+            )
+
+        def quantise_rest(i):
+            nc.vector.quantize_mx(
+                out=r_codes[i // 2][:, piece_cols(i)].bitcast(E4M3),
+                scales=r_scales[i // 2][:, piece_cols(i)],
+                in_=rest_words[i][:].rearrange("p w j -> p (w j)"),
+            )
+
+        def recover(c, j):
+            bank = LAST_CHUNK_BANKS[j] if c == CHUNKS - 1 else (PACK * c + j) % ROTATING_BANKS
+            g_q[(c, j)] = psum.tile([P, CHUNK], F32, name="g_q%d_%d" % (c, j), tag="bank%d" % bank)
+            cols = slice(j * P, (j + 1) * P)
+            nc.tensor.matmul_mx(
+                out=g_q[(c, j)][:],
+                lhsT=eye_codes[:, cols].bitcast(E4M3),
+                lhsT_scale=eye_scales[:, cols],
+                rhs=q_codes[c][:].bitcast(E5M2),
+                rhs_scale=q_scales[c][:],
+                start=True,
+                stop=True,
+            )
+
+        def subtract_chunk(c, j):
+            nc.vector.tensor_tensor(
+                out=rest_rows[c][:, :, j, :],
+                in0=g_rows[c][:, :, j, :],
+                in1=g_q[(c, j)][:].rearrange("p (u w) -> p u w", u=2),
+                op=ALU.subtract,
+            )
+
+        def subtract_piece(i, j):
+            nc.vector.tensor_tensor(
+                out=rest_rows[i // 2][:, i % 2, j, :],
+                in0=g_rows[i // 2][:, i % 2, j, :],
+                in1=g_q[(i // 2, j)][:, piece_cols(i)],
+                op=ALU.subtract,
+            )
+
+        def add_product(codes, scales, c, n):
+            h, a = divmod(c, PASSES)
+            if (h, n) not in sums:
+                bank = (FIRST_HALF_BANKS, LAST_CHUNK_BANKS)[h][n]
+                sums[(h, n)] = psum.tile([P, CHUNK], F32, name="sums%d_%d" % (h, n), tag="bank%d" % bank)
+                passes_done[(h, n)] = 0
+            passes_done[(h, n)] = passes_done[(h, n)] + 1
+            nc.tensor.matmul_mx(
+                out=sums[(h, n)][:],
+                lhsT=w_words[:, a, 2 * P * n : 2 * P * (n + 1)].bitcast(E2M1),
+                lhsT_scale=w_scales[:, a, P * n : P * (n + 1)],
+                rhs=codes,
+                rhs_scale=scales,
+                start=passes_done[(h, n)] == 1,
+                stop=passes_done[(h, n)] == 2 * PASSES,
+            )
+
+        def product_q(c, *n_tiles):
+            for n in n_tiles:
+                add_product(q_codes[c][:].bitcast(E5M2), q_scales[c][:], c, n)
+
+        def product_r(c, *n_tiles):
+            for n in n_tiles:
+                add_product(r_codes[c][:].bitcast(E4M3), r_scales[c][:], c, n)
+
+        def finish(h, n, lo=0, hi=CHUNK):
+            result = out_tiles[N_TILES * h + n]
+            nc.vector.scalar_tensor_tensor(
+                out=result[:, lo:hi],
+                in0=sums[(h, n)][:, lo:hi],
+                scalar=ls_cols[:, n : n + 1],
+                in1=res_tiles[h][:, n, lo:hi],
+                op0=ALU.mult,
+                op1=ALU.add,
+            )
+            nc.sync.dma_start(out=out[n * P : (n + 1) * P, h * CHUNK + lo : h * CHUNK + hi], in_=result[:, lo:hi])
+
+        on_scalar, on_vector = nc.scalar.copy, nc.vector.tensor_copy
+
+        for i in range(2 * (CHUNKS - 1)):
+            load_g(i)
+        nc.sync.dma_start(out=w_words[:], in_=w4_words.rearrange("a p n -> p a n"))
+        for quad in range(4):
+            nc.sync.dma_start(
+                out=w_scales[32 * quad : 32 * quad + 4, :, :].bitcast(I32),
+                in_=w4_scales[:, 4 * quad : 4 * quad + 4, :].rearrange("a r n -> r a n").bitcast(I32),
+            )
+        load_g(6)
+        load_g(7)
+        load_res(0)
+        with nc.allow_non_contiguous_dma("ls[128 c + p] goes to partition p"):
+            nc.sync.dma_start(out=ls_cols[:], in_=ls.rearrange("(c p) -> p c", p=P))
+        load_res(1)
+
+        round_g(on_vector, 0)
+        quantise_g(0)
+        round_g(on_scalar, 1, 0, SCALAR_SHARE_IDLE)
+        round_g(on_vector, 1, SCALAR_SHARE_IDLE, PIECE)
+        quantise_g(1)
+        for j in range(ROTATING_BANKS):
+            recover(0, j)
+        round_g(on_scalar, 2, 0, SCALAR_SHARE_IDLE)
+        round_g(on_vector, 2, SCALAR_SHARE_IDLE, PIECE)
+        round_g(on_scalar, 3, 0, SCALAR_SHARE_BUSY)
+        round_g(on_scalar, 4)
+        round_g(on_scalar, 5)
+        quantise_g(2)
+
+        subtract_chunk(0, 0)
+        recover(0, 3)
+        round_g(on_vector, 3, SCALAR_SHARE_BUSY, PIECE)
+        subtract_chunk(0, 1)
+        quantise_g(3)
+        recover(1, 0)
+        subtract_chunk(0, 2)
+        recover(1, 1)
+        subtract_chunk(0, 3)
+        recover(1, 2)
+        interleave_rest_on_scalar(0)
+        round_g(on_scalar, 6)
+        round_g(on_scalar, 7)
+
+        subtract_chunk(1, 0)
+        recover(1, 3)
+        quantise_g(4)
+        subtract_chunk(1, 1)
+        quantise_g(5)
+        recover(2, 0)
+        interleave_rest_on_gpsimd(1, "g_words5")
+        product_q(0, 0)
+        subtract_chunk(1, 2)
+        recover(2, 1)
+        product_q(0, 1)
+        subtract_chunk(1, 3)
+        recover(2, 2)
+        product_q(0, 2)
+        interleave_rest_on_scalar(2)
+        interleave_rest_on_scalar(3)
+
+        subtract_chunk(2, 0)
+        recover(2, 3)
+        product_q(0, 3)
+        product_q(1, 0, 1, 2, 3)
+        subtract_chunk(2, 1)
+        subtract_chunk(2, 2)
+        quantise_rest(0)
+        quantise_rest(1)
+        product_r(0, 0, 1)
+        quantise_g(6)
+        quantise_g(7)
+        for j in range(PACK - 1):
+            recover(3, j)
+        subtract_chunk(2, 3)
+        recover(3, 3)
+        product_r(0, 2, 3)
+        interleave_rest_on_scalar(4)
+        quantise_rest(2)
+
+        subtract_piece(6, 0)
+        subtract_piece(6, 1)
+        quantise_rest(3)
+        interleave_rest_on_gpsimd(5, "rest_words3")
+        product_r(1, 0, 1, 2, 3)
+        subtract_piece(6, 2)
+        subtract_piece(6, 3)
+        interleave_rest_on_scalar(6)
+        for j in range(PACK):
+            subtract_piece(7, j)
+            product_q(2, j)
+            product_q(3, j)
+        interleave_rest_on_scalar(7)
+
+        finish(0, 0)
+        finish(0, 1)
+        quantise_rest(4)
+        quantise_rest(5)
+        product_r(2, 0, 1)
+        quantise_rest(6)
+        quantise_rest(7)
+        product_r(3, 0, 1)
+        for n in (2, 3):
+            product_r(2, n)
+            product_r(3, n)
+        finish(0, 2)
+        finish(0, 3)
+        for n in range(N_TILES - 1):
+            finish(1, n)
+        finish(1, N_TILES - 1, 0, PIECE)
+        finish(1, N_TILES - 1, PIECE, CHUNK)

@@ -15,6 +15,7 @@ E4M3 = mybir.dt.float8_e4m3fn_x4
 E5M2 = mybir.dt.float8_e5m2_x4
 E2M1 = mybir.dt.float4_e2m1fn_x4
 ALU = mybir.AluOpType
+ACT = mybir.ActivationFunctionType
 
 P = 128
 PACK = 4
@@ -24,15 +25,15 @@ PIECE = CHUNK // 2
 PASSES = K // K_PASS
 HALVES = T // CHUNK
 CHUNKS = PASSES * HALVES
+PIECES = 2 * CHUNKS
 N_TILES = N // P
 LINE = 4
-SCALAR_SHARE_IDLE = 96
-SCALAR_SHARE_BUSY = 160
-WARM_PASSES = 4
-
-ROTATING_BANKS = 3
-FIRST_HALF_BANKS = (3, 4, 5, 6)
-LAST_CHUNK_BANKS = (0, 1, 7, 2)
+WARM_PASSES = 2
+GROUPS = ((0,), (1,), (2, 3), (4, 5), (6, 7))
+HALF = PIECE // 2
+SUM_BANKS = (0, 1, 2, 3)
+VALUE_BANKS = (4, 5, 6, 7)
+SECOND_BANKS = (0, 4, 5, 6)
 
 
 def tile_mix_tierg_ls_kernel(tc, g, w4_words, w4_scales, res, ls, out):
@@ -45,39 +46,46 @@ def tile_mix_tierg_ls_kernel(tc, g, w4_words, w4_scales, res, ls, out):
         def tiles(name, count, shape, dtype):
             return [sb.tile(shape, dtype, name="%s%d" % (name, i), align_bytes=64) for i in range(count)]
 
-        g_rows = [
-            t[:].rearrange("p (u j w) -> p u j w", u=2, j=PACK) for t in tiles("g_rows", CHUNKS, [P, PACK * CHUNK], F32)
-        ]
-        rest_rows = tiles("rest_rows", CHUNKS, [P, 2, PACK, PIECE], BF16)
-        q_codes = tiles("q_codes", CHUNKS, [P, CHUNK], U32)
-        q_scales = tiles("q_scales", CHUNKS, [P, CHUNK], U8)
+        g_rows = {}
+        rest_rows = tiles("rest_rows", CHUNKS, [P, PACK, CHUNK], BF16)
+        for group in GROUPS:
+            width = len(group) * PACK * PIECE
+            g_tile = sb.tile([P, width], F32, name="g_rows%d" % group[0], align_bytes=64)
+            g_rows[group] = g_tile[:].rearrange("p (u j w) -> p u j w", j=PACK, w=PIECE)
+
+        def of_piece(rows, i):
+            group = [group for group in GROUPS if i in group][0]
+            return rows[group][:, i - group[0], :, :]
+
+        q_codes = sb.tile([P, (PIECES + 1) * PIECE], U32, name="q_codes", align_bytes=64)
+        q_scales = sb.tile([P, (PIECES + 1) * PIECE], U8, name="q_scales", align_bytes=64)
         r_codes = tiles("r_codes", CHUNKS, [P, CHUNK], U32)
         r_scales = tiles("r_scales", CHUNKS, [P, CHUNK], U8)
-        w_words = sb.tile([P, PASSES, 2 * N], U8, align_bytes=64)
-        w_scales = sb.tile([P, PASSES, N], U8, align_bytes=64)
-        ls_cols = sb.tile([P, N_TILES], F32, align_bytes=64)
-        res_tiles = tiles("res", HALVES, [P, N_TILES, CHUNK], F32)
+        w_words = sb.tile([P, PASSES, 2 * N], U8, name="w_words", align_bytes=64)
+        w_scales = sb.tile([P, PASSES, N], U8, name="w_scales", align_bytes=64)
+        ls_cols = sb.tile([P, N_TILES], F32, name="ls_cols", align_bytes=64)
+        res_tiles = tiles("res", HALVES * N_TILES, [P, CHUNK], F32)
         out_tiles = tiles("out", HALVES * N_TILES, [P, CHUNK], F32)
-        eye = sb.tile([P, P], BF16, align_bytes=64)
-        eye_words = sb.tile([P, PACK, P, PACK], BF16, align_bytes=64)
-        eye_codes = sb.tile([P, PACK * P], U32, align_bytes=64)
-        eye_scales = sb.tile([P, PACK * P], U8, align_bytes=64)
+        eye = sb.tile([P, P], BF16, name="eye", align_bytes=64)
+        eye_words = sb.tile([P, PACK * (K_PASS + 1)], BF16, name="eye_words", align_bytes=64)
+        eye_codes = sb.tile([P, PACK * P], U32, name="eye_codes", align_bytes=64)
+        eye_scales = sb.tile([P, PACK * P], U8, name="eye_scales", align_bytes=64)
 
-        warm_in = sb.tile([P, 16], F32, align_bytes=64)
-        warm_out = sb.tile([P, 16], F32, align_bytes=64)
+        warm_in = sb.tile([P, 16], F32, name="warm_in", align_bytes=64)
+        warm_out = sb.tile([P, 16], F32, name="warm_out", align_bytes=64)
         nc.vector.memset(warm_in[:], 0.0)
         nc.scalar.copy(out=warm_out[:], in_=warm_in[:])
 
         make_identity(nc, eye[:])
-        nc.vector.memset(eye_words[:].rearrange("p j m i -> p (j m i)").bitcast(I32), 0)
+        nc.vector.memset(eye_words[:].bitcast(I32), 0)
         nc.gpsimd.memset(w_scales[:].rearrange("p a n -> p (a n)").bitcast(I32), 0)
-        for j in range(PACK):
-            nc.vector.tensor_copy(out=eye_words[:, j, :, j], in_=eye[:])
-        nc.vector.quantize_mx(
-            out=eye_codes[:].bitcast(E4M3), scales=eye_scales[:], in_=eye_words[:].rearrange("p j m i -> p (j m i)")
-        )
+        diagonal = eye_words[:].rearrange("p (j s) -> p j s", j=PACK)[:, :, 0:K_PASS:PACK]
+        nc.vector.tensor_copy(out=diagonal, in_=eye[:].unsqueeze(1).to_broadcast([P, PACK, P]))
+        nc.vector.quantize_mx(out=eye_codes[:].bitcast(E4M3), scales=eye_scales[:], in_=eye_words[:, 0 : PACK * K_PASS])
+        nc.gpsimd.memset(q_codes[:, 0:PIECE].bitcast(I32), 0)
+        nc.gpsimd.memset(q_scales[:, 0:PIECE].bitcast(I32), 0)
 
-        warm_bank = psum.tile([P, CHUNK], F32, tag="bank%d" % LAST_CHUNK_BANKS[2])
+        warm_bank = psum.tile([P, CHUNK], F32, name="warm_bank", tag="bank%d" % SUM_BANKS[0])
         for j in range(WARM_PASSES):
             nc.tensor.matmul_mx(
                 out=warm_bank[:],
@@ -91,6 +99,7 @@ def tile_mix_tierg_ls_kernel(tc, g, w4_words, w4_scales, res, ls, out):
 
         g_words = {}
         rest_words = {}
+        scaled = {}
         g_q = {}
         sums = {}
         passes_done = {}
@@ -98,15 +107,31 @@ def tile_mix_tierg_ls_kernel(tc, g, w4_words, w4_scales, res, ls, out):
         def piece_cols(i):
             return slice((i % 2) * PIECE, (i % 2 + 1) * PIECE)
 
+        def q_cols(i, count):
+            return slice((i + 1) * PIECE, (i + 1 + count) * PIECE)
+
         def load_g(i):
             h, a = divmod(i // 2, PASSES)
             t0 = h * CHUNK + (i % 2) * PIECE
             rows = g[a * K_PASS : (a + 1) * K_PASS, t0 : t0 + PIECE]
-            nc.sync.dma_start(out=g_rows[i // 2][:, i % 2, :, :], in_=rows.rearrange("(p j) w -> p j w", j=PACK))
+            nc.sync.dma_start(out=of_piece(g_rows, i), in_=rows.rearrange("(p j) w -> p j w", j=PACK))
 
-        def load_res(h):
-            cols = res[:, h * CHUNK : (h + 1) * CHUNK]
-            nc.sync.dma_start(out=res_tiles[h][:], in_=cols.rearrange("(c p) t -> p c t", p=P))
+        def load_weights():
+            nc.sync.dma_start(out=w_words[:], in_=w4_words.rearrange("a p n -> p a n"))
+            for quad in range(4):
+                nc.sync.dma_start(
+                    out=w_scales[32 * quad : 32 * quad + 4, :, :].bitcast(I32),
+                    in_=w4_scales[:, 4 * quad : 4 * quad + 4, :].rearrange("a r n -> r a n").bitcast(I32),
+                )
+
+        def load_ls():
+            with nc.allow_non_contiguous_dma("ls[128 c + p] goes to partition p"):
+                nc.sync.dma_start(out=ls_cols[:], in_=ls.rearrange("(c p) -> p c", p=P))
+
+        def load_res(h, n):
+            nc.sync.dma_start(
+                out=res_tiles[N_TILES * h + n][:], in_=res[n * P : (n + 1) * P, h * CHUNK : (h + 1) * CHUNK]
+            )
 
         def interleave(copy, dst, src, lo, hi):
             copy(
@@ -114,76 +139,75 @@ def tile_mix_tierg_ls_kernel(tc, g, w4_words, w4_scales, res, ls, out):
                 in_=src[:, :, lo:hi].rearrange("p j (c i) -> p c j i", i=LINE),
             )
 
-        def round_g(copy, i, lo=0, hi=PIECE):
-            if i not in g_words:
-                name = "g_words%d" % i
-                g_words[i] = sb.tile([P, PIECE, PACK], BF16, name=name, tag=name, align_bytes=64)
-            interleave(copy, g_words[i], g_rows[i // 2][:, i % 2, :, :], lo, hi)
+        def on_gpsimd(out, in_):
+            nc.gpsimd.tensor_scalar(out=out, in0=in_, scalar1=1.0, scalar2=0.0, op0=ALU.mult, op1=ALU.add)
 
-        def interleave_rest_on_scalar(i):
-            name = "rest_words%d" % i
-            rest_words[i] = sb.tile([P, PIECE, PACK], BF16, name=name, tag=name, align_bytes=64)
-            interleave(nc.scalar.copy, rest_words[i], rest_rows[i // 2][:, i % 2, :, :], 0, PIECE)
+        on_scalar, on_vector = nc.scalar.copy, nc.vector.tensor_copy
 
-        def interleave_rest_on_gpsimd(i, slot):
-            rest_words[i] = sb.tile([P, PIECE, PACK], BF16, name="rest_words%d" % i, tag=slot, align_bytes=64)
-            nc.gpsimd.tensor_scalar(
-                out=rest_words[i][:],
-                in0=rest_rows[i // 2][:, i % 2, :, :].rearrange("p j w -> p w j"),
-                scalar1=1.0,
-                scalar2=0.0,
-                op0=ALU.mult,
-                op1=ALU.add,
-            )
+        def words(store, name, i, slot):
+            if i not in store:
+                full = "%s%d" % (name, i)
+                store[i] = sb.tile([P, PIECE, PACK], BF16, name=full, tag=slot or full, align_bytes=64)
+            return store[i]
+
+        def round_g(copy, i, lo=0, hi=PIECE, slot=None):
+            interleave(copy, words(g_words, "g_words", i, slot), of_piece(g_rows, i), lo, hi)
+
+        def rest_tile(c, lo, hi, slot=None):
+            name = "rest_words%d_%d" % (c, lo)
+            rest_words[(c, lo, hi)] = sb.tile([P, hi - lo, PACK], BF16, name=name, tag=slot or name, align_bytes=64)
+
+        def mix_rest(copy, c, lo, hi):
+            key = [key for key in rest_words if key[0] == c and key[1] <= lo and hi <= key[2]][0]
+            dst = rest_words[key][:, lo - key[1] : hi - key[1], :]
+            src = rest_rows[c][:, :, lo:hi]
+            if copy is on_gpsimd:
+                copy(out=dst, in_=src.rearrange("p j w -> p w j"))
+            else:
+                interleave(copy, dst, src, 0, hi - lo)
 
         def quantise_g(i):
             nc.vector.quantize_mx(
-                out=q_codes[i // 2][:, piece_cols(i)].bitcast(E5M2),
-                scales=q_scales[i // 2][:, piece_cols(i)],
+                out=q_codes[:, q_cols(i, 1)].bitcast(E5M2),
+                scales=q_scales[:, q_cols(i, 1)],
                 in_=g_words[i][:].rearrange("p w j -> p (w j)"),
             )
 
-        def quantise_rest(i):
+        def quantise_rest(c, lo, hi):
             nc.vector.quantize_mx(
-                out=r_codes[i // 2][:, piece_cols(i)].bitcast(E4M3),
-                scales=r_scales[i // 2][:, piece_cols(i)],
-                in_=rest_words[i][:].rearrange("p w j -> p (w j)"),
+                out=r_codes[c][:, lo:hi].bitcast(E4M3),
+                scales=r_scales[c][:, lo:hi],
+                in_=rest_words[(c, lo, hi)][:].rearrange("p w j -> p (w j)"),
             )
 
-        def recover(c, j):
-            bank = LAST_CHUNK_BANKS[j] if c == CHUNKS - 1 else (PACK * c + j) % ROTATING_BANKS
-            g_q[(c, j)] = psum.tile([P, CHUNK], F32, name="g_q%d_%d" % (c, j), tag="bank%d" % bank)
+        def recover(i, j):
+            g_q[(i, j)] = psum.tile([P, CHUNK], F32, name="g_q%d_%d" % (i, j), tag="bank%d" % VALUE_BANKS[j])
             cols = slice(j * P, (j + 1) * P)
             nc.tensor.matmul_mx(
-                out=g_q[(c, j)][:],
+                out=g_q[(i, j)][:],
                 lhsT=eye_codes[:, cols].bitcast(E4M3),
                 lhsT_scale=eye_scales[:, cols],
-                rhs=q_codes[c][:].bitcast(E5M2),
-                rhs_scale=q_scales[c][:],
+                rhs=q_codes[:, q_cols(i - 1, 2)].bitcast(E5M2),
+                rhs_scale=q_scales[:, q_cols(i - 1, 2)],
                 start=True,
                 stop=True,
             )
 
-        def subtract_chunk(c, j):
+        def subtract(group, j, part=None):
+            values = g_q[(group[-1], j)][:].rearrange("p (u w) -> p u w", u=2)[:, 2 - len(group) :, :]
+            parts = slice(0, len(group)) if part is None else slice(part, part + 1)
+            first, count = group[0] % 2 + parts.start, parts.stop - parts.start
             nc.vector.tensor_tensor(
-                out=rest_rows[c][:, :, j, :],
-                in0=g_rows[c][:, :, j, :],
-                in1=g_q[(c, j)][:].rearrange("p (u w) -> p u w", u=2),
-                op=ALU.subtract,
-            )
-
-        def subtract_piece(i, j):
-            nc.vector.tensor_tensor(
-                out=rest_rows[i // 2][:, i % 2, j, :],
-                in0=g_rows[i // 2][:, i % 2, j, :],
-                in1=g_q[(i // 2, j)][:, piece_cols(i)],
+                out=rest_rows[group[0] // 2][:, j, :].rearrange("p (u w) -> p u w", u=2)[:, first : first + count, :],
+                in0=g_rows[group][:, parts, j, :],
+                in1=values[:, parts, :],
                 op=ALU.subtract,
             )
 
         def add_product(codes, scales, c, n):
             h, a = divmod(c, PASSES)
             if (h, n) not in sums:
-                bank = (FIRST_HALF_BANKS, LAST_CHUNK_BANKS)[h][n]
+                bank = (SUM_BANKS, SECOND_BANKS)[h][n]
                 sums[(h, n)] = psum.tile([P, CHUNK], F32, name="sums%d_%d" % (h, n), tag="bank%d" % bank)
                 passes_done[(h, n)] = 0
             passes_done[(h, n)] = passes_done[(h, n)] + 1
@@ -199,133 +223,143 @@ def tile_mix_tierg_ls_kernel(tc, g, w4_words, w4_scales, res, ls, out):
 
         def product_q(c, *n_tiles):
             for n in n_tiles:
-                add_product(q_codes[c][:].bitcast(E5M2), q_scales[c][:], c, n)
+                add_product(q_codes[:, q_cols(2 * c, 2)].bitcast(E5M2), q_scales[:, q_cols(2 * c, 2)], c, n)
 
         def product_r(c, *n_tiles):
             for n in n_tiles:
                 add_product(r_codes[c][:].bitcast(E4M3), r_scales[c][:], c, n)
 
-        def finish(h, n, lo=0, hi=CHUNK):
+        def store(h, n, lo, hi, queue=nc.sync):
             result = out_tiles[N_TILES * h + n]
+            queue.dma_start(out=out[n * P : (n + 1) * P, h * CHUNK + lo : h * CHUNK + hi], in_=result[:, lo:hi])
+
+        def finish(h, n, lo=0, hi=CHUNK):
             nc.vector.scalar_tensor_tensor(
-                out=result[:, lo:hi],
+                out=out_tiles[N_TILES * h + n][:, lo:hi],
                 in0=sums[(h, n)][:, lo:hi],
                 scalar=ls_cols[:, n : n + 1],
-                in1=res_tiles[h][:, n, lo:hi],
+                in1=res_tiles[N_TILES * h + n][:, lo:hi],
                 op0=ALU.mult,
                 op1=ALU.add,
             )
-            nc.sync.dma_start(out=out[n * P : (n + 1) * P, h * CHUNK + lo : h * CHUNK + hi], in_=result[:, lo:hi])
+            store(h, n, lo, hi)
 
-        on_scalar, on_vector = nc.scalar.copy, nc.vector.tensor_copy
+        def scale_on_scalar(h, n, slot=None):
+            name = "scaled%d_%d" % (h, n)
+            scaled[(h, n)] = sb.tile([P, CHUNK], F32, name=name, tag=slot or name, align_bytes=64)
+            nc.scalar.activation(out=scaled[(h, n)][:], in_=sums[(h, n)][:], func=ACT.Copy, scale=ls_cols[:, n : n + 1])
 
-        for i in range(2 * (CHUNKS - 1)):
-            load_g(i)
-        nc.sync.dma_start(out=w_words[:], in_=w4_words.rearrange("a p n -> p a n"))
-        for quad in range(4):
-            nc.sync.dma_start(
-                out=w_scales[32 * quad : 32 * quad + 4, :, :].bitcast(I32),
-                in_=w4_scales[:, 4 * quad : 4 * quad + 4, :].rearrange("a r n -> r a n").bitcast(I32),
+        def add_on_gpsimd(h, n, slot=None, lo=0, hi=CHUNK):
+            if slot:
+                out_tiles[N_TILES * h + n] = sb.tile([P, CHUNK], F32, name="late_out", tag=slot, align_bytes=64)
+            nc.gpsimd.tensor_tensor(
+                out=out_tiles[N_TILES * h + n][:, lo:hi],
+                in0=scaled[(h, n)][:, lo:hi],
+                in1=res_tiles[N_TILES * h + n][:, lo:hi],
+                op=ALU.add,
             )
-        load_g(6)
-        load_g(7)
-        load_res(0)
-        with nc.allow_non_contiguous_dma("ls[128 c + p] goes to partition p"):
-            nc.sync.dma_start(out=ls_cols[:], in_=ls.rearrange("(c p) -> p c", p=P))
-        load_res(1)
 
-        round_g(on_vector, 0)
+        for i in range(6):
+            load_g(i)
+        load_weights()
+        for i in range(6, 8):
+            load_g(i)
+        load_res(0, 0)
+        load_ls()
+        for n in range(1, N_TILES):
+            load_res(0, n)
+        for n in range(N_TILES):
+            load_res(1, n)
+
+        round_g(on_scalar, 0, 0, 96)
+        round_g(on_vector, 0, 96, PIECE)
         quantise_g(0)
-        round_g(on_scalar, 1, 0, SCALAR_SHARE_IDLE)
-        round_g(on_vector, 1, SCALAR_SHARE_IDLE, PIECE)
-        quantise_g(1)
-        for j in range(ROTATING_BANKS):
+        for j in range(PACK):
             recover(0, j)
-        round_g(on_scalar, 2, 0, SCALAR_SHARE_IDLE)
-        round_g(on_vector, 2, SCALAR_SHARE_IDLE, PIECE)
-        round_g(on_scalar, 3, 0, SCALAR_SHARE_BUSY)
+        round_g(on_scalar, 1, 0, 96)
+        round_g(on_vector, 1, 96, PIECE)
+        round_g(on_scalar, 2)
+        round_g(on_scalar, 3, 0, 96)
         round_g(on_scalar, 4)
         round_g(on_scalar, 5)
-        quantise_g(2)
-
-        subtract_chunk(0, 0)
-        recover(0, 3)
-        round_g(on_vector, 3, SCALAR_SHARE_BUSY, PIECE)
-        subtract_chunk(0, 1)
-        quantise_g(3)
+        subtract((0,), 0)
+        quantise_g(1)
         recover(1, 0)
-        subtract_chunk(0, 2)
-        recover(1, 1)
-        subtract_chunk(0, 3)
-        recover(1, 2)
-        interleave_rest_on_scalar(0)
+        for j in range(1, PACK):
+            subtract((0,), j)
+            recover(1, j)
+        subtract((1,), 0)
+        round_g(on_vector, 3, 96, PIECE)
+        quantise_g(2)
+        quantise_g(3)
+        recover(3, 0)
+        rest_tile(0, 0, PIECE, "g_words3")
+        mix_rest(on_gpsimd, 0, 0, PIECE)
+        for j in range(1, PACK):
+            subtract((1,), j)
+            recover(3, j)
+        rest_tile(0, PIECE, CHUNK)
+        mix_rest(on_gpsimd, 0, PIECE, PIECE + 96)
+        mix_rest(on_scalar, 0, PIECE + 96, CHUNK)
         round_g(on_scalar, 6)
         round_g(on_scalar, 7)
-
-        subtract_chunk(1, 0)
-        recover(1, 3)
+        for j in range(PACK - 1):
+            subtract((2, 3), j)
         quantise_g(4)
-        subtract_chunk(1, 1)
+        quantise_rest(0, 0, PIECE)
         quantise_g(5)
-        recover(2, 0)
-        interleave_rest_on_gpsimd(1, "g_words5")
-        product_q(0, 0)
-        subtract_chunk(1, 2)
-        recover(2, 1)
-        product_q(0, 1)
-        subtract_chunk(1, 3)
-        recover(2, 2)
-        product_q(0, 2)
-        interleave_rest_on_scalar(2)
-        interleave_rest_on_scalar(3)
-
-        subtract_chunk(2, 0)
-        recover(2, 3)
+        product_q(0, 0, 1, 2)
+        for j in range(PACK - 1):
+            recover(5, j)
+        subtract((2, 3), 3)
+        recover(5, 3)
+        quantise_rest(0, PIECE, CHUNK)
         product_q(0, 3)
         product_q(1, 0, 1, 2, 3)
-        subtract_chunk(2, 1)
-        subtract_chunk(2, 2)
-        quantise_rest(0)
-        quantise_rest(1)
-        product_r(0, 0, 1)
+        product_r(0, 0, 1, 2, 3)
+        rest_tile(1, 0, CHUNK)
+        mix_rest(on_gpsimd, 1, 0, 384)
+        mix_rest(on_scalar, 1, 384, CHUNK)
+        for j in range(PACK):
+            subtract((4, 5), j)
         quantise_g(6)
         quantise_g(7)
-        for j in range(PACK - 1):
-            recover(3, j)
-        subtract_chunk(2, 3)
-        recover(3, 3)
-        product_r(0, 2, 3)
-        interleave_rest_on_scalar(4)
-        quantise_rest(2)
-
-        subtract_piece(6, 0)
-        subtract_piece(6, 1)
-        quantise_rest(3)
-        interleave_rest_on_gpsimd(5, "rest_words3")
-        product_r(1, 0, 1, 2, 3)
-        subtract_piece(6, 2)
-        subtract_piece(6, 3)
-        interleave_rest_on_scalar(6)
         for j in range(PACK):
-            subtract_piece(7, j)
-            product_q(2, j)
-            product_q(3, j)
-        interleave_rest_on_scalar(7)
-
-        finish(0, 0)
+            recover(7, j)
+        quantise_rest(1, 0, CHUNK)
+        product_r(1, 0, 1, 2, 3)
+        rest_tile(2, 0, PIECE)
+        rest_tile(2, PIECE, CHUNK, "rest_words1_0")
+        mix_rest(on_scalar, 2, 0, PIECE)
+        mix_rest(on_scalar, 2, PIECE, PIECE + 112)
+        mix_rest(on_gpsimd, 2, PIECE + 112, CHUNK)
+        scale_on_scalar(0, 0)
+        for j in range(PACK):
+            subtract((6, 7), j, 0)
+        rest_tile(3, 0, CHUNK)
+        mix_rest(on_scalar, 3, 0, PIECE)
+        product_q(2, 0)
+        product_q(3, 0)
+        quantise_rest(2, 0, PIECE)
+        quantise_rest(2, PIECE, CHUNK)
+        add_on_gpsimd(0, 0, "rest_words2_0")
+        store(0, 0, 0, CHUNK)
+        product_r(2, 0)
+        for j in range(PACK):
+            subtract((6, 7), j, 1)
+            if j < 3:
+                product_q(2, 1 + j)
+                product_q(3, 1 + j)
+                product_r(2, 1 + j)
+        mix_rest(on_scalar, 3, PIECE, PIECE + 128)
+        mix_rest(on_gpsimd, 3, PIECE + 128, CHUNK)
         finish(0, 1)
-        quantise_rest(4)
-        quantise_rest(5)
-        product_r(2, 0, 1)
-        quantise_rest(6)
-        quantise_rest(7)
-        product_r(3, 0, 1)
-        for n in (2, 3):
-            product_r(2, n)
-            product_r(3, n)
         finish(0, 2)
+        quantise_rest(3, 0, CHUNK)
+        product_r(3, 0, 1, 2, 3)
         finish(0, 3)
-        for n in range(N_TILES - 1):
-            finish(1, n)
-        finish(1, N_TILES - 1, 0, PIECE)
-        finish(1, N_TILES - 1, PIECE, CHUNK)
+        finish(1, 0)
+        finish(1, 1)
+        finish(1, 2)
+        finish(1, 3, 0, PIECE)
+        finish(1, 3, PIECE, CHUNK)

@@ -33,7 +33,7 @@ GROUPS = ((0,), (1,), (2, 3), (4, 5), (6, 7))
 HALF = PIECE // 2
 SUM_BANKS = (0, 1, 2, 3)
 VALUE_BANKS = (4, 5, 6, 7)
-SECOND_BANKS = (0, 4, 5, 6)
+SECOND_BANKS = (4, 5, 6, 7)
 
 
 def tile_mix_tierg_ls_kernel(tc, g, w4_words, w4_scales, res, ls, out):
@@ -61,7 +61,7 @@ def tile_mix_tierg_ls_kernel(tc, g, w4_words, w4_scales, res, ls, out):
         q_scales = sb.tile([P, (PIECES + 1) * PIECE], U8, name="q_scales", align_bytes=64)
         r_codes = tiles("r_codes", CHUNKS, [P, CHUNK], U32)
         r_scales = tiles("r_scales", CHUNKS, [P, CHUNK], U8)
-        w_words = sb.tile([P, PASSES, 2 * N], U8, name="w_words", align_bytes=64)
+        w_words = tiles("w_words", PASSES, [P, 2 * N], U8)
         w_scales = sb.tile([P, PASSES, N], U8, name="w_scales", align_bytes=64)
         ls_cols = sb.tile([P, N_TILES], F32, name="ls_cols", align_bytes=64)
         res_tiles = tiles("res", HALVES * N_TILES, [P, CHUNK], F32)
@@ -78,12 +78,12 @@ def tile_mix_tierg_ls_kernel(tc, g, w4_words, w4_scales, res, ls, out):
 
         make_identity(nc, eye[:])
         nc.vector.memset(eye_words[:].bitcast(I32), 0)
-        nc.gpsimd.memset(w_scales[:].rearrange("p a n -> p (a n)").bitcast(I32), 0)
+        nc.vector.memset(w_scales[:].rearrange("p a n -> p (a n)").bitcast(I32), 0)
         diagonal = eye_words[:].rearrange("p (j s) -> p j s", j=PACK)[:, :, 0:K_PASS:PACK]
         nc.vector.tensor_copy(out=diagonal, in_=eye[:].unsqueeze(1).to_broadcast([P, PACK, P]))
+        nc.vector.memset(q_codes[:, 0:PIECE].bitcast(I32), 0)
+        nc.vector.memset(q_scales[:, 0:PIECE].bitcast(I32), 0)
         nc.vector.quantize_mx(out=eye_codes[:].bitcast(E4M3), scales=eye_scales[:], in_=eye_words[:, 0 : PACK * K_PASS])
-        nc.gpsimd.memset(q_codes[:, 0:PIECE].bitcast(I32), 0)
-        nc.gpsimd.memset(q_scales[:, 0:PIECE].bitcast(I32), 0)
 
         warm_bank = psum.tile([P, CHUNK], F32, name="warm_bank", tag="bank%d" % SUM_BANKS[0])
         for j in range(WARM_PASSES):
@@ -116,8 +116,10 @@ def tile_mix_tierg_ls_kernel(tc, g, w4_words, w4_scales, res, ls, out):
             rows = g[a * K_PASS : (a + 1) * K_PASS, t0 : t0 + PIECE]
             nc.sync.dma_start(out=of_piece(g_rows, i), in_=rows.rearrange("(p j) w -> p j w", j=PACK))
 
-        def load_weights():
-            nc.sync.dma_start(out=w_words[:], in_=w4_words.rearrange("a p n -> p a n"))
+        def load_words(a):
+            nc.sync.dma_start(out=w_words[a][:], in_=w4_words[a])
+
+        def load_scales():
             for quad in range(4):
                 nc.sync.dma_start(
                     out=w_scales[32 * quad : 32 * quad + 4, :, :].bitcast(I32),
@@ -193,14 +195,21 @@ def tile_mix_tierg_ls_kernel(tc, g, w4_words, w4_scales, res, ls, out):
                 stop=True,
             )
 
-        def subtract(group, j, part=None):
+        def subtract(group, j):
             values = g_q[(group[-1], j)][:].rearrange("p (u w) -> p u w", u=2)[:, 2 - len(group) :, :]
-            parts = slice(0, len(group)) if part is None else slice(part, part + 1)
-            first, count = group[0] % 2 + parts.start, parts.stop - parts.start
+            first = group[0] % 2
+            rest = rest_rows[group[0] // 2][:, j, :].rearrange("p (u w) -> p u w", u=2)
             nc.vector.tensor_tensor(
-                out=rest_rows[group[0] // 2][:, j, :].rearrange("p (u w) -> p u w", u=2)[:, first : first + count, :],
-                in0=g_rows[group][:, parts, j, :],
-                in1=values[:, parts, :],
+                out=rest[:, first : first + len(group), :], in0=g_rows[group][:, :, j, :], in1=values, op=ALU.subtract
+            )
+
+        def subtract_last(j, lo, hi):
+            group = GROUPS[-1]
+            u = lo // PIECE
+            nc.vector.tensor_tensor(
+                out=rest_rows[CHUNKS - 1][:, j, lo:hi],
+                in0=g_rows[group][:, u, j, lo - u * PIECE : hi - u * PIECE],
+                in1=g_q[(group[-1], j)][:, lo:hi],
                 op=ALU.subtract,
             )
 
@@ -213,7 +222,7 @@ def tile_mix_tierg_ls_kernel(tc, g, w4_words, w4_scales, res, ls, out):
             passes_done[(h, n)] = passes_done[(h, n)] + 1
             nc.tensor.matmul_mx(
                 out=sums[(h, n)][:],
-                lhsT=w_words[:, a, 2 * P * n : 2 * P * (n + 1)].bitcast(E2M1),
+                lhsT=w_words[a][:, 2 * P * n : 2 * P * (n + 1)].bitcast(E2M1),
                 lhsT_scale=w_scales[:, a, P * n : P * (n + 1)],
                 rhs=codes,
                 rhs_scale=scales,
@@ -251,7 +260,7 @@ def tile_mix_tierg_ls_kernel(tc, g, w4_words, w4_scales, res, ls, out):
 
         def add_on_gpsimd(h, n, slot=None, lo=0, hi=CHUNK):
             if slot:
-                out_tiles[N_TILES * h + n] = sb.tile([P, CHUNK], F32, name="late_out", tag=slot, align_bytes=64)
+                out_tiles[N_TILES * h + n] = sb.tile([P, CHUNK], F32, name="late_out%d" % n, tag=slot, align_bytes=64)
             nc.gpsimd.tensor_tensor(
                 out=out_tiles[N_TILES * h + n][:, lo:hi],
                 in0=scaled[(h, n)][:, lo:hi],
@@ -261,9 +270,11 @@ def tile_mix_tierg_ls_kernel(tc, g, w4_words, w4_scales, res, ls, out):
 
         for i in range(6):
             load_g(i)
-        load_weights()
-        for i in range(6, 8):
-            load_g(i)
+        load_words(0)
+        load_scales()
+        load_g(6)
+        load_g(7)
+        load_words(1)
         load_res(0, 0)
         load_ls()
         for n in range(1, N_TILES):
@@ -282,10 +293,8 @@ def tile_mix_tierg_ls_kernel(tc, g, w4_words, w4_scales, res, ls, out):
         round_g(on_scalar, 3, 0, 96)
         round_g(on_scalar, 4)
         round_g(on_scalar, 5)
-        subtract((0,), 0)
         quantise_g(1)
-        recover(1, 0)
-        for j in range(1, PACK):
+        for j in range(PACK):
             subtract((0,), j)
             recover(1, j)
         subtract((1,), 0)
@@ -306,59 +315,60 @@ def tile_mix_tierg_ls_kernel(tc, g, w4_words, w4_scales, res, ls, out):
         for j in range(PACK - 1):
             subtract((2, 3), j)
         quantise_g(4)
-        quantise_rest(0, 0, PIECE)
         quantise_g(5)
         product_q(0, 0, 1, 2)
         for j in range(PACK - 1):
             recover(5, j)
+        quantise_rest(0, 0, PIECE)
         subtract((2, 3), 3)
         recover(5, 3)
         quantise_rest(0, PIECE, CHUNK)
         product_q(0, 3)
-        product_q(1, 0, 1, 2, 3)
         product_r(0, 0, 1, 2, 3)
-        rest_tile(1, 0, CHUNK)
-        mix_rest(on_gpsimd, 1, 0, 384)
-        mix_rest(on_scalar, 1, 384, CHUNK)
-        for j in range(PACK):
+        product_q(1, 0, 1, 2)
+        rest_tile(1, 0, PIECE)
+        rest_tile(1, PIECE, CHUNK)
+        mix_rest(on_gpsimd, 1, 0, PIECE)
+        mix_rest(on_scalar, 1, PIECE, CHUNK)
+        for j in range(PACK - 1):
             subtract((4, 5), j)
         quantise_g(6)
         quantise_g(7)
-        for j in range(PACK):
+        for j in range(PACK - 1):
             recover(7, j)
-        quantise_rest(1, 0, CHUNK)
+        quantise_rest(1, 0, PIECE)
+        subtract((4, 5), 3)
+        recover(7, 3)
+        product_q(1, 3)
+        quantise_rest(1, PIECE, CHUNK)
         product_r(1, 0, 1, 2, 3)
-        rest_tile(2, 0, PIECE)
-        rest_tile(2, PIECE, CHUNK, "rest_words1_0")
-        mix_rest(on_scalar, 2, 0, PIECE)
-        mix_rest(on_scalar, 2, PIECE, PIECE + 112)
-        mix_rest(on_gpsimd, 2, PIECE + 112, CHUNK)
-        scale_on_scalar(0, 0)
+        rest_tile(2, 0, CHUNK)
+        mix_rest(on_scalar, 2, 0, 288)
+        mix_rest(on_gpsimd, 2, 288, CHUNK)
         for j in range(PACK):
-            subtract((6, 7), j, 0)
+            subtract_last(j, 0, PIECE)
         rest_tile(3, 0, CHUNK)
         mix_rest(on_scalar, 3, 0, PIECE)
-        product_q(2, 0)
-        product_q(3, 0)
-        quantise_rest(2, 0, PIECE)
-        quantise_rest(2, PIECE, CHUNK)
-        add_on_gpsimd(0, 0, "rest_words2_0")
-        store(0, 0, 0, CHUNK)
-        product_r(2, 0)
         for j in range(PACK):
-            subtract((6, 7), j, 1)
-            if j < 3:
-                product_q(2, 1 + j)
-                product_q(3, 1 + j)
-                product_r(2, 1 + j)
-        mix_rest(on_scalar, 3, PIECE, PIECE + 128)
-        mix_rest(on_gpsimd, 3, PIECE + 128, CHUNK)
+            subtract_last(j, PIECE, CHUNK)
+            product_q(2, j)
+            product_q(3, j)
+            if j == 1:
+                quantise_rest(2, 0, CHUNK)
+                product_r(2, 0, 1)
+        product_r(2, 2)
+        mix_rest(on_scalar, 3, PIECE, PIECE + 144)
+        mix_rest(on_gpsimd, 3, PIECE + 144, CHUNK)
+        finish(0, 0)
         finish(0, 1)
-        finish(0, 2)
         quantise_rest(3, 0, CHUNK)
-        product_r(3, 0, 1, 2, 3)
+        product_r(3, 0)
+        product_r(2, 3)
+        product_r(3, 1, 2, 3)
+        finish(0, 2)
         finish(0, 3)
-        finish(1, 0)
+        finish(1, 0, 0, PIECE)
+        finish(1, 0, PIECE, CHUNK)
         finish(1, 1)
         finish(1, 2)
         finish(1, 3, 0, PIECE)

@@ -242,7 +242,7 @@ def tile_mix_tierg_ls_kernel(tc, g, w4_words, w4_scales, res, ls, out):
             result = out_tiles[N_TILES * h + n]
             queue.dma_start(out=out[n * P : (n + 1) * P, h * CHUNK + lo : h * CHUNK + hi], in_=result[:, lo:hi])
 
-        def finish(h, n, lo=0, hi=CHUNK):
+        def finish(h, n, lo=0, hi=CHUNK, queue=nc.sync):
             nc.vector.scalar_tensor_tensor(
                 out=out_tiles[N_TILES * h + n][:, lo:hi],
                 in0=sums[(h, n)][:, lo:hi],
@@ -251,7 +251,7 @@ def tile_mix_tierg_ls_kernel(tc, g, w4_words, w4_scales, res, ls, out):
                 op0=ALU.mult,
                 op1=ALU.add,
             )
-            store(h, n, lo, hi)
+            store(h, n, lo, hi, queue)
 
         def scale_on_scalar(h, n, slot=None):
             name = "scaled%d_%d" % (h, n)
@@ -291,35 +291,38 @@ def tile_mix_tierg_ls_kernel(tc, g, w4_words, w4_scales, res, ls, out):
         round_g(on_vector, 1, 96, PIECE)
         round_g(on_scalar, 2)
         round_g(on_scalar, 3, 0, 96)
-        round_g(on_scalar, 4)
-        round_g(on_scalar, 5)
         quantise_g(1)
         for j in range(PACK):
             subtract((0,), j)
             recover(1, j)
+        rest_tile(0, 0, HALF)
+        mix_rest(on_scalar, 0, 0, HALF)
+        round_g(on_scalar, 4)
+        round_g(on_scalar, 5)
         subtract((1,), 0)
         round_g(on_vector, 3, 96, PIECE)
         quantise_g(2)
         quantise_g(3)
         recover(3, 0)
-        rest_tile(0, 0, PIECE, "g_words3")
-        mix_rest(on_gpsimd, 0, 0, PIECE)
+        rest_tile(0, HALF, PIECE, "g_words3")
+        mix_rest(on_gpsimd, 0, HALF, PIECE)
         for j in range(1, PACK):
             subtract((1,), j)
             recover(3, j)
         rest_tile(0, PIECE, CHUNK)
-        mix_rest(on_gpsimd, 0, PIECE, PIECE + 96)
-        mix_rest(on_scalar, 0, PIECE + 96, CHUNK)
+        mix_rest(on_gpsimd, 0, PIECE, PIECE + HALF)
+        mix_rest(on_scalar, 0, PIECE + HALF, CHUNK)
         round_g(on_scalar, 6)
         round_g(on_scalar, 7)
         for j in range(PACK - 1):
             subtract((2, 3), j)
         quantise_g(4)
+        quantise_rest(0, 0, HALF)
+        quantise_rest(0, HALF, PIECE)
         quantise_g(5)
         product_q(0, 0, 1, 2)
         for j in range(PACK - 1):
             recover(5, j)
-        quantise_rest(0, 0, PIECE)
         subtract((2, 3), 3)
         recover(5, 3)
         quantise_rest(0, PIECE, CHUNK)
@@ -343,8 +346,8 @@ def tile_mix_tierg_ls_kernel(tc, g, w4_words, w4_scales, res, ls, out):
         quantise_rest(1, PIECE, CHUNK)
         product_r(1, 0, 1, 2, 3)
         rest_tile(2, 0, CHUNK)
-        mix_rest(on_scalar, 2, 0, 288)
-        mix_rest(on_gpsimd, 2, 288, CHUNK)
+        mix_rest(on_scalar, 2, 0, 304)
+        mix_rest(on_gpsimd, 2, 304, CHUNK)
         for j in range(PACK):
             subtract_last(j, 0, PIECE)
         rest_tile(3, 0, CHUNK)
@@ -357,8 +360,8 @@ def tile_mix_tierg_ls_kernel(tc, g, w4_words, w4_scales, res, ls, out):
                 quantise_rest(2, 0, CHUNK)
                 product_r(2, 0, 1)
         product_r(2, 2)
-        mix_rest(on_scalar, 3, PIECE, PIECE + 144)
-        mix_rest(on_gpsimd, 3, PIECE + 144, CHUNK)
+        mix_rest(on_scalar, 3, PIECE, PIECE + 160)
+        mix_rest(on_gpsimd, 3, PIECE + 160, CHUNK)
         finish(0, 0)
         finish(0, 1)
         quantise_rest(3, 0, CHUNK)
@@ -366,10 +369,8 @@ def tile_mix_tierg_ls_kernel(tc, g, w4_words, w4_scales, res, ls, out):
         product_r(2, 3)
         product_r(3, 1, 2, 3)
         finish(0, 2)
-        finish(0, 3)
-        finish(1, 0, 0, PIECE)
-        finish(1, 0, PIECE, CHUNK)
-        finish(1, 1)
+        finish(0, 3, queue=nc.scalar)
+        finish(1, 0)
+        finish(1, 1, queue=nc.scalar)
         finish(1, 2)
-        finish(1, 3, 0, PIECE)
-        finish(1, 3, PIECE, CHUNK)
+        finish(1, 3, queue=nc.scalar)

@@ -270,8 +270,8 @@ def tile_mix_tierg_ls_kernel(tc, g, w4_words, w4_scales, res, ls, out):
 
         for i in range(6):
             load_g(i)
-        load_words(0)
         load_scales()
+        load_words(0)
         load_g(6)
         load_g(7)
         load_words(1)
@@ -350,24 +350,26 @@ def tile_mix_tierg_ls_kernel(tc, g, w4_words, w4_scales, res, ls, out):
         mix_rest(on_gpsimd, 2, 304, CHUNK)
         for j in range(PACK):
             subtract_last(j, 0, PIECE)
-        rest_tile(3, 0, CHUNK)
-        mix_rest(on_scalar, 3, 0, PIECE)
+        rest_tile(3, 0, PIECE)
+        rest_tile(3, PIECE, CHUNK)
+        mix_rest(on_scalar, 3, 0, 256)
         for j in range(PACK):
             subtract_last(j, PIECE, CHUNK)
             product_q(2, j)
             product_q(3, j)
-            if j == 1:
-                quantise_rest(2, 0, CHUNK)
-                product_r(2, 0, 1)
-        product_r(2, 2)
-        mix_rest(on_scalar, 3, PIECE, PIECE + 160)
-        mix_rest(on_gpsimd, 3, PIECE + 160, CHUNK)
+        mix_rest(on_scalar, 3, PIECE, PIECE + 192)
+        mix_rest(on_gpsimd, 3, PIECE + 192, CHUNK)
         finish(0, 0)
         finish(0, 1)
-        quantise_rest(3, 0, CHUNK)
-        product_r(3, 0)
+        quantise_rest(2, 0, CHUNK)
+        product_r(2, 0, 1)
+        quantise_rest(3, 0, PIECE)
+        quantise_rest(3, PIECE, CHUNK)
+        product_r(3, 0, 1)
+        product_r(2, 2)
+        product_r(3, 2)
         product_r(2, 3)
-        product_r(3, 1, 2, 3)
+        product_r(3, 3)
         finish(0, 2)
         finish(0, 3, queue=nc.scalar)
         finish(1, 0)

@@ -135,10 +135,10 @@ def tile_mix_tierg_ls_kernel(tc, g, w4_words, w4_scales, res, ls, out):
                 out=res_tiles[N_TILES * h + n][:], in_=res[n * P : (n + 1) * P, h * CHUNK : (h + 1) * CHUNK]
             )
 
-        def interleave(copy, dst, src, lo, hi):
+        def interleave(copy, dst, src, lo, hi, run=LINE):
             copy(
-                out=dst[:, lo:hi, :].rearrange("p (c i) j -> p c j i", i=LINE),
-                in_=src[:, :, lo:hi].rearrange("p j (c i) -> p c j i", i=LINE),
+                out=dst[:, lo:hi, :].rearrange("p (c i) j -> p c j i", i=run),
+                in_=src[:, :, lo:hi].rearrange("p j (c i) -> p c j i", i=run),
             )
 
         def on_gpsimd(out, in_):
@@ -153,7 +153,7 @@ def tile_mix_tierg_ls_kernel(tc, g, w4_words, w4_scales, res, ls, out):
             return store[i]
 
         def round_g(copy, i, lo=0, hi=PIECE, slot=None):
-            interleave(copy, words(g_words, "g_words", i, slot), of_piece(g_rows, i), lo, hi)
+            interleave(copy, words(g_words, "g_words", i, slot), of_piece(g_rows, i), lo, hi, 2)
 
         def rest_tile(c, lo, hi, slot=None):
             name = "rest_words%d_%d" % (c, lo)
@@ -270,8 +270,8 @@ def tile_mix_tierg_ls_kernel(tc, g, w4_words, w4_scales, res, ls, out):
 
         for i in range(6):
             load_g(i)
-        load_scales()
         load_words(0)
+        load_scales()
         load_g(6)
         load_g(7)
         load_words(1)
@@ -346,13 +346,14 @@ def tile_mix_tierg_ls_kernel(tc, g, w4_words, w4_scales, res, ls, out):
         quantise_rest(1, PIECE, CHUNK)
         product_r(1, 0, 1, 2, 3)
         rest_tile(2, 0, CHUNK)
-        mix_rest(on_scalar, 2, 0, 304)
-        mix_rest(on_gpsimd, 2, 304, CHUNK)
+        mix_rest(on_scalar, 2, 0, 256)
+        mix_rest(on_gpsimd, 2, 256, CHUNK)
         for j in range(PACK):
             subtract_last(j, 0, PIECE)
         rest_tile(3, 0, PIECE)
         rest_tile(3, PIECE, CHUNK)
-        mix_rest(on_scalar, 3, 0, 256)
+        mix_rest(on_scalar, 3, 0, 192)
+        mix_rest(on_gpsimd, 3, 192, PIECE)
         for j in range(PACK):
             subtract_last(j, PIECE, CHUNK)
             product_q(2, j)

@@ -20,20 +20,18 @@ ACT = mybir.ActivationFunctionType
 P = 128
 PACK = 4
 K_PASS = P * PACK
-CHUNK = 512
-PIECE = CHUNK // 2
+BANK = 512
+STRIP = BANK // PACK
+PIECE = 2 * STRIP
 PASSES = K // K_PASS
-HALVES = T // CHUNK
+HALVES = T // BANK
 CHUNKS = PASSES * HALVES
 PIECES = 2 * CHUNKS
+STRIPS = 2 * PIECES
 N_TILES = N // P
-LINE = 4
+PAIR = 2
 WARM_PASSES = 2
-GROUPS = ((0,), (1,), (2, 3), (4, 5), (6, 7))
-HALF = PIECE // 2
-SUM_BANKS = (0, 1, 2, 3)
-VALUE_BANKS = (4, 5, 6, 7)
-SECOND_BANKS = (4, 5, 6, 7)
+SUM_BANKS = ((0, 1, 2, 3), (6, 7, 0, 1))
 
 
 def tile_mix_tierg_ls_kernel(tc, g, w4_words, w4_scales, res, ls, out):
@@ -46,26 +44,17 @@ def tile_mix_tierg_ls_kernel(tc, g, w4_words, w4_scales, res, ls, out):
         def tiles(name, count, shape, dtype):
             return [sb.tile(shape, dtype, name="%s%d" % (name, i), align_bytes=64) for i in range(count)]
 
-        g_rows = {}
-        rest_rows = tiles("rest_rows", CHUNKS, [P, PACK, CHUNK], BF16)
-        for group in GROUPS:
-            width = len(group) * PACK * PIECE
-            g_tile = sb.tile([P, width], F32, name="g_rows%d" % group[0], align_bytes=64)
-            g_rows[group] = g_tile[:].rearrange("p (u j w) -> p u j w", j=PACK, w=PIECE)
-
-        def of_piece(rows, i):
-            group = [group for group in GROUPS if i in group][0]
-            return rows[group][:, i - group[0], :, :]
-
-        q_codes = sb.tile([P, (PIECES + 1) * PIECE], U32, name="q_codes", align_bytes=64)
-        q_scales = sb.tile([P, (PIECES + 1) * PIECE], U8, name="q_scales", align_bytes=64)
-        r_codes = tiles("r_codes", CHUNKS, [P, CHUNK], U32)
-        r_scales = tiles("r_scales", CHUNKS, [P, CHUNK], U8)
+        g_rows = tiles("g_rows", PIECES, [P, PACK, PIECE], F32)
+        g_words = tiles("g_words", PIECES, [P, PIECE * PACK], BF16)
+        rest_words = tiles("rest_words", PIECES, [P, PIECE * PACK], BF16)
+        q_codes = tiles("q_codes", CHUNKS, [P, BANK], U32)
+        q_scales = tiles("q_scales", CHUNKS, [P, BANK], U8)
+        r_codes = tiles("r_codes", CHUNKS, [P, BANK], U32)
+        r_scales = tiles("r_scales", CHUNKS, [P, BANK], U8)
         w_words = tiles("w_words", PASSES, [P, 2 * N], U8)
         w_scales = sb.tile([P, PASSES, N], U8, name="w_scales", align_bytes=64)
         ls_cols = sb.tile([P, N_TILES], F32, name="ls_cols", align_bytes=64)
-        res_tiles = tiles("res", HALVES * N_TILES, [P, CHUNK], F32)
-        out_tiles = tiles("out", HALVES * N_TILES, [P, CHUNK], F32)
+        res_tiles = tiles("res", HALVES * N_TILES, [P, BANK], F32)
         eye = sb.tile([P, P], BF16, name="eye", align_bytes=64)
         eye_words = sb.tile([P, PACK * (K_PASS + 1)], BF16, name="eye_words", align_bytes=64)
         eye_codes = sb.tile([P, PACK * P], U32, name="eye_codes", align_bytes=64)
@@ -81,11 +70,9 @@ def tile_mix_tierg_ls_kernel(tc, g, w4_words, w4_scales, res, ls, out):
         nc.vector.memset(w_scales[:].rearrange("p a n -> p (a n)").bitcast(I32), 0)
         diagonal = eye_words[:].rearrange("p (j s) -> p j s", j=PACK)[:, :, 0:K_PASS:PACK]
         nc.vector.tensor_copy(out=diagonal, in_=eye[:].unsqueeze(1).to_broadcast([P, PACK, P]))
-        nc.vector.memset(q_codes[:, 0:PIECE].bitcast(I32), 0)
-        nc.vector.memset(q_scales[:, 0:PIECE].bitcast(I32), 0)
         nc.vector.quantize_mx(out=eye_codes[:].bitcast(E4M3), scales=eye_scales[:], in_=eye_words[:, 0 : PACK * K_PASS])
 
-        warm_bank = psum.tile([P, CHUNK], F32, name="warm_bank", tag="bank%d" % SUM_BANKS[0])
+        warm_bank = psum.tile([P, BANK], F32, name="warm_bank", tag="bank0")
         for j in range(WARM_PASSES):
             nc.tensor.matmul_mx(
                 out=warm_bank[:],
@@ -97,24 +84,16 @@ def tile_mix_tierg_ls_kernel(tc, g, w4_words, w4_scales, res, ls, out):
                 stop=True,
             )
 
-        g_words = {}
-        rest_words = {}
-        scaled = {}
-        g_q = {}
+        values = {}
         sums = {}
-        passes_done = {}
-
-        def piece_cols(i):
-            return slice((i % 2) * PIECE, (i % 2 + 1) * PIECE)
-
-        def q_cols(i, count):
-            return slice((i + 1) * PIECE, (i + 1 + count) * PIECE)
+        scaled = {}
+        results = {}
 
         def load_g(i):
             h, a = divmod(i // 2, PASSES)
-            t0 = h * CHUNK + (i % 2) * PIECE
+            t0 = h * BANK + (i % 2) * PIECE
             rows = g[a * K_PASS : (a + 1) * K_PASS, t0 : t0 + PIECE]
-            nc.sync.dma_start(out=of_piece(g_rows, i), in_=rows.rearrange("(p j) w -> p j w", j=PACK))
+            nc.sync.dma_start(out=g_rows[i][:], in_=rows.rearrange("(p j) w -> p j w", j=PACK))
 
         def load_words(a):
             nc.sync.dma_start(out=w_words[a][:], in_=w4_words[a])
@@ -132,248 +111,217 @@ def tile_mix_tierg_ls_kernel(tc, g, w4_words, w4_scales, res, ls, out):
 
         def load_res(h, n):
             nc.sync.dma_start(
-                out=res_tiles[N_TILES * h + n][:], in_=res[n * P : (n + 1) * P, h * CHUNK : (h + 1) * CHUNK]
+                out=res_tiles[N_TILES * h + n][:], in_=res[n * P : (n + 1) * P, h * BANK : (h + 1) * BANK]
             )
 
-        def interleave(copy, dst, src, lo, hi, run=LINE):
-            copy(
-                out=dst[:, lo:hi, :].rearrange("p (c i) j -> p c j i", i=run),
-                in_=src[:, :, lo:hi].rearrange("p j (c i) -> p c j i", i=run),
-            )
+        def as_words(tile, s, count):
+            lo = (s % 2) * STRIP * PACK
+            return tile[:, lo : lo + count * STRIP * PACK]
 
-        def on_gpsimd(out, in_):
-            nc.gpsimd.tensor_scalar(out=out, in0=in_, scalar1=1.0, scalar2=0.0, op0=ALU.mult, op1=ALU.add)
+        def walk_words(words):
+            return words.rearrange("p (c i j) -> p c j i", i=PAIR, j=PACK)
 
-        on_scalar, on_vector = nc.scalar.copy, nc.vector.tensor_copy
+        def walk_rows(rows):
+            return rows.rearrange("p j (c i) -> p c j i", i=PAIR)
 
-        def words(store, name, i, slot):
-            if i not in store:
-                full = "%s%d" % (name, i)
-                store[i] = sb.tile([P, PIECE, PACK], BF16, name=full, tag=slot or full, align_bytes=64)
-            return store[i]
+        def rows_of(s, count):
+            lo = (s % 2) * STRIP
+            return g_rows[s // 2][:, :, lo : lo + count * STRIP]
 
-        def round_g(copy, i, lo=0, hi=PIECE, slot=None):
-            interleave(copy, words(g_words, "g_words", i, slot), of_piece(g_rows, i), lo, hi, 2)
+        def chunk_cols(s, count):
+            lo = (s % 4) * STRIP
+            return slice(lo, lo + count * STRIP)
 
-        def rest_tile(c, lo, hi, slot=None):
-            name = "rest_words%d_%d" % (c, lo)
-            rest_words[(c, lo, hi)] = sb.tile([P, hi - lo, PACK], BF16, name=name, tag=slot or name, align_bytes=64)
+        def round_g(copy, s, count):
+            copy(out=walk_words(as_words(g_words[s // 2], s, count)), in_=walk_rows(rows_of(s, count)))
 
-        def mix_rest(copy, c, lo, hi):
-            key = [key for key in rest_words if key[0] == c and key[1] <= lo and hi <= key[2]][0]
-            dst = rest_words[key][:, lo - key[1] : hi - key[1], :]
-            src = rest_rows[c][:, :, lo:hi]
-            if copy is on_gpsimd:
-                copy(out=dst, in_=src.rearrange("p j w -> p w j"))
-            else:
-                interleave(copy, dst, src, 0, hi - lo)
-
-        def quantise_g(i):
+        def quantise_g(s, count):
             nc.vector.quantize_mx(
-                out=q_codes[:, q_cols(i, 1)].bitcast(E5M2),
-                scales=q_scales[:, q_cols(i, 1)],
-                in_=g_words[i][:].rearrange("p w j -> p (w j)"),
+                out=q_codes[s // 4][:, chunk_cols(s, count)].bitcast(E5M2),
+                scales=q_scales[s // 4][:, chunk_cols(s, count)],
+                in_=as_words(g_words[s // 2], s, count),
             )
 
-        def quantise_rest(c, lo, hi):
+        def quantise_rest(s, count):
             nc.vector.quantize_mx(
-                out=r_codes[c][:, lo:hi].bitcast(E4M3),
-                scales=r_scales[c][:, lo:hi],
-                in_=rest_words[(c, lo, hi)][:].rearrange("p w j -> p (w j)"),
+                out=r_codes[s // 4][:, chunk_cols(s, count)].bitcast(E4M3),
+                scales=r_scales[s // 4][:, chunk_cols(s, count)],
+                in_=as_words(rest_words[s // 2], s, count),
             )
 
-        def recover(i, j):
-            g_q[(i, j)] = psum.tile([P, CHUNK], F32, name="g_q%d_%d" % (i, j), tag="bank%d" % VALUE_BANKS[j])
-            cols = slice(j * P, (j + 1) * P)
-            nc.tensor.matmul_mx(
-                out=g_q[(i, j)][:],
-                lhsT=eye_codes[:, cols].bitcast(E4M3),
-                lhsT_scale=eye_scales[:, cols],
-                rhs=q_codes[:, q_cols(i - 1, 2)].bitcast(E5M2),
-                rhs_scale=q_scales[:, q_cols(i - 1, 2)],
-                start=True,
-                stop=True,
-            )
+        def recover(s):
+            bank = 4 + s % (4 if s < STRIPS // 2 else 2)
+            values[s] = psum.tile([P, PACK, STRIP], F32, name="values%d" % s, tag="bank%d" % bank)
+            for j in range(PACK):
+                cols = slice(j * P, (j + 1) * P)
+                nc.tensor.matmul_mx(
+                    out=values[s][:, j, :],
+                    lhsT=eye_codes[:, cols].bitcast(E4M3),
+                    lhsT_scale=eye_scales[:, cols],
+                    rhs=q_codes[s // 4][:, chunk_cols(s, 1)].bitcast(E5M2),
+                    rhs_scale=q_scales[s // 4][:, chunk_cols(s, 1)],
+                    start=True,
+                    stop=True,
+                )
 
-        def subtract(group, j):
-            values = g_q[(group[-1], j)][:].rearrange("p (u w) -> p u w", u=2)[:, 2 - len(group) :, :]
-            first = group[0] % 2
-            rest = rest_rows[group[0] // 2][:, j, :].rearrange("p (u w) -> p u w", u=2)
+        def subtract(s):
             nc.vector.tensor_tensor(
-                out=rest[:, first : first + len(group), :], in0=g_rows[group][:, :, j, :], in1=values, op=ALU.subtract
-            )
-
-        def subtract_last(j, lo, hi):
-            group = GROUPS[-1]
-            u = lo // PIECE
-            nc.vector.tensor_tensor(
-                out=rest_rows[CHUNKS - 1][:, j, lo:hi],
-                in0=g_rows[group][:, u, j, lo - u * PIECE : hi - u * PIECE],
-                in1=g_q[(group[-1], j)][:, lo:hi],
+                out=walk_words(as_words(rest_words[s // 2], s, 1)),
+                in0=walk_rows(rows_of(s, 1)),
+                in1=walk_rows(values[s][:]),
                 op=ALU.subtract,
             )
 
-        def add_product(codes, scales, c, n):
+        def product(codes, scales, c, n, lo=0, hi=BANK, stop=False):
             h, a = divmod(c, PASSES)
-            if (h, n) not in sums:
-                bank = (SUM_BANKS, SECOND_BANKS)[h][n]
-                sums[(h, n)] = psum.tile([P, CHUNK], F32, name="sums%d_%d" % (h, n), tag="bank%d" % bank)
-                passes_done[(h, n)] = 0
-            passes_done[(h, n)] = passes_done[(h, n)] + 1
+            start = (h, n) not in sums
+            if start:
+                sums[(h, n)] = psum.tile([P, BANK], F32, name="sums%d_%d" % (h, n), tag="bank%d" % SUM_BANKS[h][n])
             nc.tensor.matmul_mx(
-                out=sums[(h, n)][:],
+                out=sums[(h, n)][:, lo:hi],
                 lhsT=w_words[a][:, 2 * P * n : 2 * P * (n + 1)].bitcast(E2M1),
                 lhsT_scale=w_scales[:, a, P * n : P * (n + 1)],
                 rhs=codes,
                 rhs_scale=scales,
-                start=passes_done[(h, n)] == 1,
-                stop=passes_done[(h, n)] == 2 * PASSES,
+                start=start,
+                stop=stop,
             )
 
         def product_q(c, *n_tiles):
             for n in n_tiles:
-                add_product(q_codes[:, q_cols(2 * c, 2)].bitcast(E5M2), q_scales[:, q_cols(2 * c, 2)], c, n)
+                product(q_codes[c][:].bitcast(E5M2), q_scales[c][:], c, n)
 
-        def product_r(c, *n_tiles):
+        def product_r(c, n_tiles, lo=0, hi=BANK):
             for n in n_tiles:
-                add_product(r_codes[c][:].bitcast(E4M3), r_scales[c][:], c, n)
+                last = c % PASSES == PASSES - 1 and hi == BANK
+                product(r_codes[c][:, lo:hi].bitcast(E4M3), r_scales[c][:, lo:hi], c, n, lo, hi, last)
 
-        def store(h, n, lo, hi, queue=nc.sync):
-            result = out_tiles[N_TILES * h + n]
-            queue.dma_start(out=out[n * P : (n + 1) * P, h * CHUNK + lo : h * CHUNK + hi], in_=result[:, lo:hi])
+        def result(h, n, slot=None):
+            if (h, n) not in results:
+                name = "result%d_%d" % (h, n)
+                results[(h, n)] = sb.tile([P, BANK], F32, name=name, tag=slot or name, align_bytes=64)
+            return results[(h, n)]
 
-        def finish(h, n, lo=0, hi=CHUNK, queue=nc.sync):
+        def store(h, n, queue=nc.sync):
+            queue.dma_start(out=out[n * P : (n + 1) * P, h * BANK : (h + 1) * BANK], in_=results[(h, n)][:])
+
+        def finish(h, n, lo=0, hi=BANK):
             nc.vector.scalar_tensor_tensor(
-                out=out_tiles[N_TILES * h + n][:, lo:hi],
+                out=result(h, n)[:, lo:hi],
                 in0=sums[(h, n)][:, lo:hi],
                 scalar=ls_cols[:, n : n + 1],
                 in1=res_tiles[N_TILES * h + n][:, lo:hi],
                 op0=ALU.mult,
                 op1=ALU.add,
             )
-            store(h, n, lo, hi, queue)
 
-        def scale_on_scalar(h, n, slot=None):
-            name = "scaled%d_%d" % (h, n)
-            scaled[(h, n)] = sb.tile([P, CHUNK], F32, name=name, tag=slot or name, align_bytes=64)
+        def scale(h, n):
+            scaled[(h, n)] = sb.tile([P, BANK], F32, name="scaled%d_%d" % (h, n), align_bytes=64)
             nc.scalar.activation(out=scaled[(h, n)][:], in_=sums[(h, n)][:], func=ACT.Copy, scale=ls_cols[:, n : n + 1])
 
-        def add_on_gpsimd(h, n, slot=None, lo=0, hi=CHUNK):
-            if slot:
-                out_tiles[N_TILES * h + n] = sb.tile([P, CHUNK], F32, name="late_out%d" % n, tag=slot, align_bytes=64)
-            nc.gpsimd.tensor_tensor(
-                out=out_tiles[N_TILES * h + n][:, lo:hi],
-                in0=scaled[(h, n)][:, lo:hi],
-                in1=res_tiles[N_TILES * h + n][:, lo:hi],
-                op=ALU.add,
+        def add_res(engine, h, n, slot=None):
+            engine.tensor_tensor(
+                out=result(h, n, slot)[:], in0=scaled[(h, n)][:], in1=res_tiles[N_TILES * h + n][:], op=ALU.add
             )
 
-        for i in range(6):
+        for i in range(3):
             load_g(i)
         load_words(0)
         load_scales()
-        load_g(6)
-        load_g(7)
+        load_g(3)
+        load_g(4)
         load_words(1)
-        load_res(0, 0)
+        for i in range(5, PIECES):
+            load_g(i)
         load_ls()
-        for n in range(1, N_TILES):
-            load_res(0, n)
-        for n in range(N_TILES):
-            load_res(1, n)
+        for h in range(HALVES):
+            for n in range(N_TILES):
+                load_res(h, n)
 
-        round_g(on_scalar, 0, 0, 96)
-        round_g(on_vector, 0, 96, PIECE)
-        quantise_g(0)
-        for j in range(PACK):
-            recover(0, j)
-        round_g(on_scalar, 1, 0, 96)
-        round_g(on_vector, 1, 96, PIECE)
-        round_g(on_scalar, 2)
-        round_g(on_scalar, 3, 0, 96)
-        quantise_g(1)
-        for j in range(PACK):
-            subtract((0,), j)
-            recover(1, j)
-        rest_tile(0, 0, HALF)
-        mix_rest(on_scalar, 0, 0, HALF)
-        round_g(on_scalar, 4)
-        round_g(on_scalar, 5)
-        subtract((1,), 0)
-        round_g(on_vector, 3, 96, PIECE)
-        quantise_g(2)
-        quantise_g(3)
-        recover(3, 0)
-        rest_tile(0, HALF, PIECE, "g_words3")
-        mix_rest(on_gpsimd, 0, HALF, PIECE)
-        for j in range(1, PACK):
-            subtract((1,), j)
-            recover(3, j)
-        rest_tile(0, PIECE, CHUNK)
-        mix_rest(on_gpsimd, 0, PIECE, PIECE + HALF)
-        mix_rest(on_scalar, 0, PIECE + HALF, CHUNK)
-        round_g(on_scalar, 6)
-        round_g(on_scalar, 7)
-        for j in range(PACK - 1):
-            subtract((2, 3), j)
-        quantise_g(4)
-        quantise_rest(0, 0, HALF)
-        quantise_rest(0, HALF, PIECE)
-        quantise_g(5)
-        product_q(0, 0, 1, 2)
-        for j in range(PACK - 1):
-            recover(5, j)
-        subtract((2, 3), 3)
-        recover(5, 3)
-        quantise_rest(0, PIECE, CHUNK)
-        product_q(0, 3)
-        product_r(0, 0, 1, 2, 3)
-        product_q(1, 0, 1, 2)
-        rest_tile(1, 0, PIECE)
-        rest_tile(1, PIECE, CHUNK)
-        mix_rest(on_gpsimd, 1, 0, PIECE)
-        mix_rest(on_scalar, 1, PIECE, CHUNK)
-        for j in range(PACK - 1):
-            subtract((4, 5), j)
-        quantise_g(6)
-        quantise_g(7)
-        for j in range(PACK - 1):
-            recover(7, j)
-        quantise_rest(1, 0, PIECE)
-        subtract((4, 5), 3)
-        recover(7, 3)
-        product_q(1, 3)
-        quantise_rest(1, PIECE, CHUNK)
-        product_r(1, 0, 1, 2, 3)
-        rest_tile(2, 0, CHUNK)
-        mix_rest(on_scalar, 2, 0, 256)
-        mix_rest(on_gpsimd, 2, 256, CHUNK)
-        for j in range(PACK):
-            subtract_last(j, 0, PIECE)
-        rest_tile(3, 0, PIECE)
-        rest_tile(3, PIECE, CHUNK)
-        mix_rest(on_scalar, 3, 0, 192)
-        mix_rest(on_gpsimd, 3, 192, PIECE)
-        for j in range(PACK):
-            subtract_last(j, PIECE, CHUNK)
-            product_q(2, j)
-            product_q(3, j)
-        mix_rest(on_scalar, 3, PIECE, PIECE + 192)
-        mix_rest(on_gpsimd, 3, PIECE + 192, CHUNK)
-        finish(0, 0)
-        finish(0, 1)
-        quantise_rest(2, 0, CHUNK)
-        product_r(2, 0, 1)
-        quantise_rest(3, 0, PIECE)
-        quantise_rest(3, PIECE, CHUNK)
-        product_r(3, 0, 1)
-        product_r(2, 2)
-        product_r(3, 2)
-        product_r(2, 3)
-        product_r(3, 3)
-        finish(0, 2)
-        finish(0, 3, queue=nc.scalar)
-        finish(1, 0)
-        finish(1, 1, queue=nc.scalar)
-        finish(1, 2)
-        finish(1, 3, queue=nc.scalar)
+        round_g(nc.vector.tensor_copy, 0, 1)
+        for s in range(1, 4):
+            round_g(nc.scalar.copy, s, 1)
+        for i in range(2, PIECES - 1):
+            round_g(nc.scalar.copy, 2 * i, 2)
+
+        quantise_g(0, 1)
+        recover(0)
+        quantise_g(1, 1)
+        recover(1)
+        subtract(0)
+        quantise_g(2, 1)
+        recover(2)
+        subtract(1)
+        quantise_g(3, 1)
+        recover(3)
+        quantise_rest(0, 2)
+        subtract(2)
+        quantise_g(4, 2)
+        product_q(0, 0, 1)
+        recover(4)
+        recover(5)
+        subtract(3)
+        quantise_g(6, 2)
+        quantise_rest(2, 2)
+        product_q(0, 2, 3)
+        recover(6)
+        recover(7)
+        subtract(4)
+        subtract(5)
+        product_r(0, (0, 1, 2, 3))
+        quantise_g(8, 2)
+        quantise_rest(4, 2)
+        recover(8)
+        recover(9)
+        product_q(1, 0, 1, 2, 3)
+        subtract(6)
+        subtract(7)
+        quantise_g(10, 2)
+        quantise_rest(6, 2)
+        product_r(1, (0, 1))
+        subtract(8)
+        recover(10)
+        product_r(1, (2,))
+        subtract(9)
+        recover(11)
+        product_r(1, (3,))
+        scale(0, 0)
+        round_g(nc.scalar.copy, 14, 2)
+        scale(0, 1)
+        scale(0, 2)
+        product_q(2, 0, 1)
+        quantise_g(12, 2)
+        quantise_rest(8, 2)
+        subtract(10)
+        recover(12)
+        product_q(2, 2)
+        subtract(11)
+        recover(13)
+        product_q(2, 3)
+        quantise_g(14, 2)
+        quantise_rest(10, 2)
+        product_r(2, (0, 1))
+        subtract(12)
+        recover(14)
+        product_r(2, (2,))
+        subtract(13)
+        recover(15)
+        product_r(2, (3,))
+        product_q(3, 0, 1, 2, 3)
+        add_res(nc.vector, 0, 0)
+        store(0, 0)
+        quantise_rest(12, 2)
+        product_r(3, (0, 1, 2, 3), 0, PIECE)
+        subtract(14)
+        subtract(15)
+        add_res(nc.vector, 0, 1)
+        store(0, 1)
+        quantise_rest(14, 2)
+        product_r(3, (0, 1, 2, 3), PIECE, BANK)
+        add_res(nc.vector, 0, 2)
+        store(0, 2)
+        finish(0, 3)
+        store(0, 3, nc.scalar)
+        for n in range(N_TILES):
+            finish(1, n)
+            store(1, n, (nc.sync, nc.scalar)[n % 2])

@@ -31,7 +31,10 @@ STRIPS = 2 * PIECES
 N_TILES = N // P
 PAIR = 2
 WARM_PASSES = 2
-SUM_BANKS = ((0, 1, 2, 3), (6, 7, 0, 1))
+STRETCHES = ((0, BANK, (0, 1, 2, 3)), (BANK, PIECE, (6, 7)), (BANK + PIECE, PIECE, (0, 1)))
+PIECE_AT = tuple(
+    (a, t0 + lo) for t0, width, banks in STRETCHES for a in range(PASSES) for lo in range(0, width, PIECE)
+)
 
 
 def tile_mix_tierg_ls_kernel(tc, g, w4_words, w4_scales, res, ls, out):
@@ -45,16 +48,24 @@ def tile_mix_tierg_ls_kernel(tc, g, w4_words, w4_scales, res, ls, out):
             return [sb.tile(shape, dtype, name="%s%d" % (name, i), align_bytes=64) for i in range(count)]
 
         g_rows = tiles("g_rows", PIECES, [P, PACK, PIECE], F32)
-        g_words = tiles("g_words", PIECES, [P, PIECE * PACK], BF16)
-        rest_words = tiles("rest_words", PIECES, [P, PIECE * PACK], BF16)
-        q_codes = tiles("q_codes", CHUNKS, [P, BANK], U32)
-        q_scales = tiles("q_scales", CHUNKS, [P, BANK], U8)
-        r_codes = tiles("r_codes", CHUNKS, [P, BANK], U32)
-        r_scales = tiles("r_scales", CHUNKS, [P, BANK], U8)
+        g_words = [
+            sb.tile([P, PIECE * PACK], BF16, name="g_words%d" % i, tag="g_words%d" % i, align_bytes=64)
+            for i in range(PIECES)
+        ]
+        rest_words = [
+            sb.tile([P, PIECE * PACK], BF16, name="rest_words%d" % i, tag="rest_words%d" % i, align_bytes=64)
+            for i in range(PIECES)
+        ]
+        q_codes = tiles("q_codes", PASSES, [P, T], U32)
+        q_scales = tiles("q_scales", PASSES, [P, T], U8)
+        r_codes = tiles("r_codes", PASSES, [P, T], U32)
+        r_scales = tiles("r_scales", PASSES, [P, T], U8)
         w_words = tiles("w_words", PASSES, [P, 2 * N], U8)
         w_scales = sb.tile([P, PASSES, N], U8, name="w_scales", align_bytes=64)
         ls_cols = sb.tile([P, N_TILES], F32, name="ls_cols", align_bytes=64)
-        res_tiles = tiles("res", HALVES * N_TILES, [P, BANK], F32)
+        res_half = tiles("res_half", N_TILES, [P, BANK], F32)
+        res_quarter = tiles("res_quarter", 2, [P, N_TILES, PIECE], F32)
+        out_quarter = tiles("out_quarter", 4, [P, 2, PIECE], F32)
         eye = sb.tile([P, P], BF16, name="eye", align_bytes=64)
         eye_words = sb.tile([P, PACK * (K_PASS + 1)], BF16, name="eye_words", align_bytes=64)
         eye_codes = sb.tile([P, PACK * P], U32, name="eye_codes", align_bytes=64)
@@ -87,11 +98,9 @@ def tile_mix_tierg_ls_kernel(tc, g, w4_words, w4_scales, res, ls, out):
         values = {}
         sums = {}
         scaled = {}
-        results = {}
 
         def load_g(i):
-            h, a = divmod(i // 2, PASSES)
-            t0 = h * BANK + (i % 2) * PIECE
+            a, t0 = PIECE_AT[i]
             rows = g[a * K_PASS : (a + 1) * K_PASS, t0 : t0 + PIECE]
             nc.sync.dma_start(out=g_rows[i][:], in_=rows.rearrange("(p j) w -> p j w", j=PACK))
 
@@ -109,10 +118,12 @@ def tile_mix_tierg_ls_kernel(tc, g, w4_words, w4_scales, res, ls, out):
             with nc.allow_non_contiguous_dma("ls[128 c + p] goes to partition p"):
                 nc.sync.dma_start(out=ls_cols[:], in_=ls.rearrange("(c p) -> p c", p=P))
 
-        def load_res(h, n):
-            nc.sync.dma_start(
-                out=res_tiles[N_TILES * h + n][:], in_=res[n * P : (n + 1) * P, h * BANK : (h + 1) * BANK]
-            )
+        def load_res_half(n):
+            nc.sync.dma_start(out=res_half[n][:], in_=res[n * P : (n + 1) * P, 0:BANK])
+
+        def load_res_quarter(b):
+            t0 = STRETCHES[b][0]
+            nc.sync.dma_start(out=res_quarter[b - 1][:], in_=res[:, t0 : t0 + PIECE].rearrange("(c p) w -> p c w", p=P))
 
         def as_words(tile, s, count):
             lo = (s % 2) * STRIP * PACK
@@ -128,24 +139,25 @@ def tile_mix_tierg_ls_kernel(tc, g, w4_words, w4_scales, res, ls, out):
             lo = (s % 2) * STRIP
             return g_rows[s // 2][:, :, lo : lo + count * STRIP]
 
-        def chunk_cols(s, count):
-            lo = (s % 4) * STRIP
-            return slice(lo, lo + count * STRIP)
+        def strip_cols(rows, s, count):
+            a, t0 = PIECE_AT[s // 2]
+            lo = t0 + (s % 2) * STRIP
+            return rows[a][:, lo : lo + count * STRIP]
 
         def round_g(copy, s, count):
             copy(out=walk_words(as_words(g_words[s // 2], s, count)), in_=walk_rows(rows_of(s, count)))
 
         def quantise_g(s, count):
             nc.vector.quantize_mx(
-                out=q_codes[s // 4][:, chunk_cols(s, count)].bitcast(E5M2),
-                scales=q_scales[s // 4][:, chunk_cols(s, count)],
+                out=strip_cols(q_codes, s, count).bitcast(E5M2),
+                scales=strip_cols(q_scales, s, count),
                 in_=as_words(g_words[s // 2], s, count),
             )
 
         def quantise_rest(s, count):
             nc.vector.quantize_mx(
-                out=r_codes[s // 4][:, chunk_cols(s, count)].bitcast(E4M3),
-                scales=r_scales[s // 4][:, chunk_cols(s, count)],
+                out=strip_cols(r_codes, s, count).bitcast(E4M3),
+                scales=strip_cols(r_scales, s, count),
                 in_=as_words(rest_words[s // 2], s, count),
             )
 
@@ -158,8 +170,8 @@ def tile_mix_tierg_ls_kernel(tc, g, w4_words, w4_scales, res, ls, out):
                     out=values[s][:, j, :],
                     lhsT=eye_codes[:, cols].bitcast(E4M3),
                     lhsT_scale=eye_scales[:, cols],
-                    rhs=q_codes[s // 4][:, chunk_cols(s, 1)].bitcast(E5M2),
-                    rhs_scale=q_scales[s // 4][:, chunk_cols(s, 1)],
+                    rhs=strip_cols(q_codes, s, 1).bitcast(E5M2),
+                    rhs_scale=strip_cols(q_scales, s, 1),
                     start=True,
                     stop=True,
                 )
@@ -172,57 +184,58 @@ def tile_mix_tierg_ls_kernel(tc, g, w4_words, w4_scales, res, ls, out):
                 op=ALU.subtract,
             )
 
-        def product(codes, scales, c, n, lo=0, hi=BANK, stop=False):
-            h, a = divmod(c, PASSES)
-            start = (h, n) not in sums
-            if start:
-                sums[(h, n)] = psum.tile([P, BANK], F32, name="sums%d_%d" % (h, n), tag="bank%d" % SUM_BANKS[h][n])
+        def sum_of(b, n):
+            t0, width, banks = STRETCHES[b]
+            share = BANK // width
+            if (b, n // share) not in sums:
+                name = "sums%d_%d" % (b, n // share)
+                sums[(b, n // share)] = psum.tile([P, share, width], F32, name=name, tag="bank%d" % banks[n // share])
+            return sums[(b, n // share)][:, n % share, :]
+
+        def product(codes, scales, fmt, b, a, n, first, last):
+            t0, width, banks = STRETCHES[b]
+            share = BANK // width
             nc.tensor.matmul_mx(
-                out=sums[(h, n)][:, lo:hi],
+                out=sum_of(b, n),
                 lhsT=w_words[a][:, 2 * P * n : 2 * P * (n + 1)].bitcast(E2M1),
                 lhsT_scale=w_scales[:, a, P * n : P * (n + 1)],
-                rhs=codes,
-                rhs_scale=scales,
-                start=start,
-                stop=stop,
+                rhs=codes[a][:, t0 : t0 + width].bitcast(fmt),
+                rhs_scale=scales[a][:, t0 : t0 + width],
+                start=first and n % share == 0,
+                stop=last and n % share == share - 1,
             )
 
-        def product_q(c, *n_tiles):
+        def product_q(b, a, *n_tiles):
             for n in n_tiles:
-                product(q_codes[c][:].bitcast(E5M2), q_scales[c][:], c, n)
+                product(q_codes, q_scales, E5M2, b, a, n, a == 0, False)
 
-        def product_r(c, n_tiles, lo=0, hi=BANK):
+        def product_r(b, a, *n_tiles):
             for n in n_tiles:
-                last = c % PASSES == PASSES - 1 and hi == BANK
-                product(r_codes[c][:, lo:hi].bitcast(E4M3), r_scales[c][:, lo:hi], c, n, lo, hi, last)
+                product(r_codes, r_scales, E4M3, b, a, n, False, a == PASSES - 1)
 
-        def result(h, n, slot=None):
-            if (h, n) not in results:
-                name = "result%d_%d" % (h, n)
-                results[(h, n)] = sb.tile([P, BANK], F32, name=name, tag=slot or name, align_bytes=64)
-            return results[(h, n)]
+        def scale(n):
+            scaled[n] = sb.tile([P, BANK], F32, name="scaled%d" % n, align_bytes=64)
+            nc.scalar.activation(out=scaled[n][:], in_=sum_of(0, n), func=ACT.Copy, scale=ls_cols[:, n : n + 1])
 
-        def store(h, n, queue=nc.sync):
-            queue.dma_start(out=out[n * P : (n + 1) * P, h * BANK : (h + 1) * BANK], in_=results[(h, n)][:])
+        def add_res(n, slot):
+            result = sb.tile([P, BANK], F32, name="out_half%d" % n, tag=slot, align_bytes=64)
+            nc.gpsimd.tensor_tensor(out=result[:], in0=scaled[n][:], in1=res_half[n][:], op=ALU.add)
+            nc.sync.dma_start(out=out[n * P : (n + 1) * P, 0:BANK], in_=result[:])
 
-        def finish(h, n, lo=0, hi=BANK):
+        def finish(b, n):
             nc.vector.scalar_tensor_tensor(
-                out=result(h, n)[:, lo:hi],
-                in0=sums[(h, n)][:, lo:hi],
+                out=out_quarter[2 * (b - 1) + n // 2][:, n % 2, :],
+                in0=sum_of(b, n),
                 scalar=ls_cols[:, n : n + 1],
-                in1=res_tiles[N_TILES * h + n][:, lo:hi],
+                in1=res_quarter[b - 1][:, n, :],
                 op0=ALU.mult,
                 op1=ALU.add,
             )
 
-        def scale(h, n):
-            scaled[(h, n)] = sb.tile([P, BANK], F32, name="scaled%d_%d" % (h, n), align_bytes=64)
-            nc.scalar.activation(out=scaled[(h, n)][:], in_=sums[(h, n)][:], func=ACT.Copy, scale=ls_cols[:, n : n + 1])
-
-        def add_res(engine, h, n, slot=None):
-            engine.tensor_tensor(
-                out=result(h, n, slot)[:], in0=scaled[(h, n)][:], in1=res_tiles[N_TILES * h + n][:], op=ALU.add
-            )
+        def store(b, pair, queue):
+            t0 = STRETCHES[b][0]
+            rows = out[2 * pair * P : 2 * (pair + 1) * P, t0 : t0 + PIECE]
+            queue.dma_start(out=rows.rearrange("(c p) w -> p c w", p=P), in_=out_quarter[2 * (b - 1) + pair][:])
 
         for i in range(3):
             load_g(i)
@@ -231,12 +244,16 @@ def tile_mix_tierg_ls_kernel(tc, g, w4_words, w4_scales, res, ls, out):
         load_g(3)
         load_g(4)
         load_words(1)
-        for i in range(5, PIECES):
-            load_g(i)
+        load_g(5)
+        load_g(6)
         load_ls()
-        for h in range(HALVES):
-            for n in range(N_TILES):
-                load_res(h, n)
+        load_g(7)
+        load_res_half(0)
+        load_res_half(1)
+        load_res_quarter(1)
+        load_res_half(2)
+        load_res_half(3)
+        load_res_quarter(2)
 
         round_g(nc.vector.tensor_copy, 0, 1)
         for s in range(1, 4):
@@ -257,71 +274,78 @@ def tile_mix_tierg_ls_kernel(tc, g, w4_words, w4_scales, res, ls, out):
         quantise_rest(0, 2)
         subtract(2)
         quantise_g(4, 2)
-        product_q(0, 0, 1)
+        product_q(0, 0, 0, 1)
         recover(4)
         recover(5)
         subtract(3)
         quantise_g(6, 2)
         quantise_rest(2, 2)
-        product_q(0, 2, 3)
+        product_q(0, 0, 2, 3)
         recover(6)
         recover(7)
         subtract(4)
         subtract(5)
-        product_r(0, (0, 1, 2, 3))
+        product_r(0, 0, 0, 1, 2, 3)
         quantise_g(8, 2)
         quantise_rest(4, 2)
         recover(8)
         recover(9)
-        product_q(1, 0, 1, 2, 3)
+        product_q(0, 1, 0, 1, 2, 3)
         subtract(6)
         subtract(7)
         quantise_g(10, 2)
         quantise_rest(6, 2)
-        product_r(1, (0, 1))
+        product_r(0, 1, 0, 1)
         subtract(8)
         recover(10)
-        product_r(1, (2,))
+        product_r(0, 1, 2)
         subtract(9)
         recover(11)
-        product_r(1, (3,))
-        scale(0, 0)
+        product_r(0, 1, 3)
+        scale(0)
         round_g(nc.scalar.copy, 14, 2)
-        scale(0, 1)
-        scale(0, 2)
-        product_q(2, 0, 1)
+        scale(1)
+        scale(2)
+        scale(3)
+        product_q(1, 0, 0, 1, 2, 3)
         quantise_g(12, 2)
+        add_res(0, "g_words6")
         quantise_rest(8, 2)
         subtract(10)
         recover(12)
-        product_q(2, 2)
+        product_q(1, 1, 0, 1)
         subtract(11)
         recover(13)
-        product_q(2, 3)
+        product_q(1, 1, 2, 3)
+        product_r(1, 0, 0, 1, 2, 3)
         quantise_g(14, 2)
+        add_res(1, "g_words7")
         quantise_rest(10, 2)
-        product_r(2, (0, 1))
+        product_r(1, 1, 0, 1)
         subtract(12)
         recover(14)
-        product_r(2, (2,))
+        product_r(1, 1, 2, 3)
         subtract(13)
         recover(15)
-        product_r(2, (3,))
-        product_q(3, 0, 1, 2, 3)
-        add_res(nc.vector, 0, 0)
-        store(0, 0)
+        product_q(2, 0, 0, 1, 2, 3)
+        product_q(2, 1, 0, 1, 2, 3)
+        finish(1, 0)
         quantise_rest(12, 2)
-        product_r(3, (0, 1, 2, 3), 0, PIECE)
+        add_res(2, "rest_words6")
+        product_r(2, 0, 0, 1, 2, 3)
         subtract(14)
         subtract(15)
-        add_res(nc.vector, 0, 1)
-        store(0, 1)
+        finish(1, 1)
+        store(1, 0, nc.scalar)
         quantise_rest(14, 2)
-        product_r(3, (0, 1, 2, 3), PIECE, BANK)
-        add_res(nc.vector, 0, 2)
-        store(0, 2)
-        finish(0, 3)
-        store(0, 3, nc.scalar)
-        for n in range(N_TILES):
-            finish(1, n)
-            store(1, n, (nc.sync, nc.scalar)[n % 2])
+        add_res(3, "rest_words7")
+        product_r(2, 1, 0, 1, 2, 3)
+        finish(1, 2)
+        finish(1, 3)
+        store(1, 1, nc.scalar)
+        finish(2, 0)
+        finish(2, 1)
+        store(2, 0, nc.scalar)
+        finish(2, 2)
+        finish(2, 3)
+        store(2, 1, nc.scalar)

@@ -1,7 +1,6 @@
 from contextlib import ExitStack
 
 import concourse.mybir as mybir
-from concourse.masks import make_identity
 
 K, N, T = 1024, 512, 1024
 FLOPS = 2 * 2 * K * N * T
@@ -31,6 +30,7 @@ STRIPS = 2 * PIECES
 N_TILES = N // P
 PAIR = 2
 WARM_PASSES = 2
+BF16_ONE = 0x3F80
 STRETCHES = ((0, BANK, (0, 1, 2, 3)), (BANK, PIECE, (6, 7)), (BANK + PIECE, PIECE, (0, 1)))
 PIECE_AT = tuple(
     (a, t0 + lo) for t0, width, banks in STRETCHES for a in range(PASSES) for lo in range(0, width, PIECE)
@@ -66,22 +66,33 @@ def tile_mix_tierg_ls_kernel(tc, g, w4_words, w4_scales, res, ls, out):
         res_half = tiles("res_half", N_TILES, [P, BANK], F32)
         res_quarter = tiles("res_quarter", 2, [P, N_TILES, PIECE], F32)
         out_quarter = tiles("out_quarter", 4, [P, 2, PIECE], F32)
-        eye = sb.tile([P, P], BF16, name="eye", align_bytes=64)
-        eye_words = sb.tile([P, PACK * (K_PASS + 1)], BF16, name="eye_words", align_bytes=64)
+        ramp = sb.tile([P, 2 * P], I32, name="ramp", align_bytes=64)
+        eye_pairs = sb.tile([P, PACK, 2 * P], I32, name="eye_pairs", align_bytes=64)
         eye_codes = sb.tile([P, PACK * P], U32, name="eye_codes", align_bytes=64)
         eye_scales = sb.tile([P, PACK * P], U8, name="eye_scales", align_bytes=64)
+
+        nc.gpsimd.iota(ramp[:], pattern=[[1, 2 * P]], base=0, channel_multiplier=-2)
 
         warm_in = sb.tile([P, 16], F32, name="warm_in", align_bytes=64)
         warm_out = sb.tile([P, 16], F32, name="warm_out", align_bytes=64)
         nc.vector.memset(warm_in[:], 0.0)
         nc.scalar.copy(out=warm_out[:], in_=warm_in[:])
 
-        make_identity(nc, eye[:])
-        nc.vector.memset(eye_words[:].bitcast(I32), 0)
         nc.vector.memset(w_scales[:].rearrange("p a n -> p (a n)").bitcast(I32), 0)
-        diagonal = eye_words[:].rearrange("p (j s) -> p j s", j=PACK)[:, :, 0:K_PASS:PACK]
-        nc.vector.tensor_copy(out=diagonal, in_=eye[:].unsqueeze(1).to_broadcast([P, PACK, P]))
-        nc.vector.quantize_mx(out=eye_codes[:].bitcast(E4M3), scales=eye_scales[:], in_=eye_words[:, 0 : PACK * K_PASS])
+        for j in range(PACK):
+            nc.vector.tensor_scalar(
+                out=eye_pairs[:, j, :],
+                in0=ramp[:],
+                scalar1=float(j // 2),
+                scalar2=float(BF16_ONE << (16 * (j % 2))),
+                op0=ALU.is_equal,
+                op1=ALU.mult,
+            )
+        nc.vector.quantize_mx(
+            out=eye_codes[:].bitcast(E4M3),
+            scales=eye_scales[:],
+            in_=eye_pairs[:].rearrange("p j w -> p (j w)").bitcast(BF16),
+        )
 
         warm_bank = psum.tile([P, BANK], F32, name="warm_bank", tag="bank0")
         for j in range(WARM_PASSES):
@@ -222,6 +233,24 @@ def tile_mix_tierg_ls_kernel(tc, g, w4_words, w4_scales, res, ls, out):
             nc.gpsimd.tensor_tensor(out=result[:], in0=scaled[n][:], in1=res_half[n][:], op=ALU.add)
             nc.sync.dma_start(out=out[n * P : (n + 1) * P, 0:BANK], in_=result[:])
 
+        def finish_half(n):
+            result = sb.tile([P, BANK], F32, name="out_half%d" % n, align_bytes=64)
+            nc.vector.scalar_tensor_tensor(
+                out=result[:],
+                in0=sum_of(0, n),
+                scalar=ls_cols[:, n : n + 1],
+                in1=res_half[n][:],
+                op0=ALU.mult,
+                op1=ALU.add,
+            )
+            nc.sync.dma_start(out=out[n * P : (n + 1) * P, 0:BANK], in_=result[:])
+
+        def store_tile(b, n, queue):
+            t0 = STRETCHES[b][0]
+            queue.dma_start(
+                out=out[n * P : (n + 1) * P, t0 : t0 + PIECE], in_=out_quarter[2 * (b - 1) + n // 2][:, n % 2, :]
+            )
+
         def finish(b, n):
             nc.vector.scalar_tensor_tensor(
                 out=out_quarter[2 * (b - 1) + n // 2][:, n % 2, :],
@@ -248,104 +277,102 @@ def tile_mix_tierg_ls_kernel(tc, g, w4_words, w4_scales, res, ls, out):
         load_g(6)
         load_ls()
         load_g(7)
-        load_res_half(0)
-        load_res_half(1)
+        for n in (0, 2, 1, 3):
+            load_res_half(n)
         load_res_quarter(1)
-        load_res_half(2)
-        load_res_half(3)
         load_res_quarter(2)
 
         round_g(nc.vector.tensor_copy, 0, 1)
-        for s in range(1, 4):
-            round_g(nc.scalar.copy, s, 1)
-        for i in range(2, PIECES - 1):
-            round_g(nc.scalar.copy, 2 * i, 2)
-
+        round_g(nc.scalar.copy, 1, 1)
         quantise_g(0, 1)
         recover(0)
         quantise_g(1, 1)
         recover(1)
+        round_g(nc.vector.tensor_copy, 2, 1)
+        round_g(nc.scalar.copy, 3, 1)
+        round_g(nc.scalar.copy, 4, 2)
+        round_g(nc.scalar.copy, 6, 1)
+        round_g(nc.scalar.copy, 7, 1)
+        for i in range(4, PIECES - 1):
+            round_g(nc.scalar.copy, 2 * i, 2)
         subtract(0)
-        quantise_g(2, 1)
+        quantise_g(2, 2)
         recover(2)
-        subtract(1)
-        quantise_g(3, 1)
         recover(3)
-        quantise_rest(0, 2)
+        subtract(1)
+        product_q(0, 0, 0, 1)
         subtract(2)
         quantise_g(4, 2)
-        product_q(0, 0, 0, 1)
         recover(4)
         recover(5)
+        quantise_rest(0, 2)
         subtract(3)
-        quantise_g(6, 2)
-        quantise_rest(2, 2)
         product_q(0, 0, 2, 3)
-        recover(6)
-        recover(7)
         subtract(4)
-        subtract(5)
+        quantise_g(6, 1)
+        recover(6)
+        quantise_rest(2, 2)
+        quantise_g(7, 1)
+        recover(7)
         product_r(0, 0, 0, 1, 2, 3)
+        subtract(5)
+        subtract(6)
         quantise_g(8, 2)
-        quantise_rest(4, 2)
         recover(8)
+        quantise_rest(4, 2)
         recover(9)
         product_q(0, 1, 0, 1, 2, 3)
-        subtract(6)
         subtract(7)
+        subtract(8)
         quantise_g(10, 2)
+        recover(10)
         quantise_rest(6, 2)
         product_r(0, 1, 0, 1)
-        subtract(8)
-        recover(10)
-        product_r(0, 1, 2)
         subtract(9)
         recover(11)
-        product_r(0, 1, 3)
+        product_r(0, 1, 2, 3)
         scale(0)
         round_g(nc.scalar.copy, 14, 2)
         scale(1)
-        scale(2)
-        scale(3)
-        product_q(1, 0, 0, 1, 2, 3)
+        subtract(10)
         quantise_g(12, 2)
+        recover(12)
         add_res(0, "g_words6")
         quantise_rest(8, 2)
-        subtract(10)
-        recover(12)
-        product_q(1, 1, 0, 1)
+        product_q(1, 0, 0, 1, 2, 3)
         subtract(11)
         recover(13)
-        product_q(1, 1, 2, 3)
+        product_q(1, 1, 0, 1, 2, 3)
         product_r(1, 0, 0, 1, 2, 3)
+        subtract(12)
+        finish_half(2)
         quantise_g(14, 2)
+        recover(14)
         add_res(1, "g_words7")
         quantise_rest(10, 2)
         product_r(1, 1, 0, 1)
-        subtract(12)
-        recover(14)
-        product_r(1, 1, 2, 3)
         subtract(13)
         recover(15)
+        product_r(1, 1, 2, 3)
         product_q(2, 0, 0, 1, 2, 3)
         product_q(2, 1, 0, 1, 2, 3)
-        finish(1, 0)
-        quantise_rest(12, 2)
-        add_res(2, "rest_words6")
-        product_r(2, 0, 0, 1, 2, 3)
         subtract(14)
+        finish_half(3)
+        quantise_rest(12, 2)
+        product_r(2, 0, 0, 1, 2, 3)
         subtract(15)
+        finish(1, 0)
+        quantise_rest(14, 2)
+        product_r(2, 1, 0, 1, 2, 3)
         finish(1, 1)
         store(1, 0, nc.scalar)
-        quantise_rest(14, 2)
-        add_res(3, "rest_words7")
-        product_r(2, 1, 0, 1, 2, 3)
         finish(1, 2)
         finish(1, 3)
-        store(1, 1, nc.scalar)
+        store(1, 1, nc.sync)
         finish(2, 0)
         finish(2, 1)
         store(2, 0, nc.scalar)
         finish(2, 2)
+        store_tile(2, 2, nc.sync)
         finish(2, 3)
-        store(2, 1, nc.scalar)
+        store_tile(2, 3, nc.scalar)

@@ -119,10 +119,10 @@ def tile_mix_tierg_ls_kernel(tc, g, w4_words, w4_scales, res, ls, out):
             nc.sync.dma_start(out=w_words[a][:], in_=w4_words[a])
 
         def load_scales():
-            for quad in range(4):
+            for r in range(4):
                 nc.sync.dma_start(
-                    out=w_scales[32 * quad : 32 * quad + 4, :, :].bitcast(I32),
-                    in_=w4_scales[:, 4 * quad : 4 * quad + 4, :].rearrange("a r n -> r a n").bitcast(I32),
+                    out=w_scales[r:P:32, :, :].bitcast(I32),
+                    in_=w4_scales[:, r:16:4, :].rearrange("a q n -> q a n").bitcast(I32),
                 )
 
         def load_ls():
@@ -289,46 +289,50 @@ def tile_mix_tierg_ls_kernel(tc, g, w4_words, w4_scales, res, ls, out):
         quantise_g(1, 1)
         recover(1)
         round_g(nc.vector.tensor_copy, 2, 1)
-        round_g(nc.scalar.copy, 3, 1)
-        round_g(nc.scalar.copy, 4, 2)
-        round_g(nc.scalar.copy, 6, 1)
-        round_g(nc.scalar.copy, 7, 1)
-        for i in range(4, PIECES - 1):
-            round_g(nc.scalar.copy, 2 * i, 2)
+        for s in range(3, 12):
+            round_g(nc.scalar.copy, s, 1)
+        round_g(nc.scalar.copy, 12, 2)
         subtract(0)
-        quantise_g(2, 2)
+        quantise_g(2, 1)
         recover(2)
+        quantise_g(3, 1)
         recover(3)
         subtract(1)
         product_q(0, 0, 0, 1)
         subtract(2)
-        quantise_g(4, 2)
+        quantise_g(4, 1)
         recover(4)
-        recover(5)
         quantise_rest(0, 2)
+        product_q(0, 0, 2)
         subtract(3)
-        product_q(0, 0, 2, 3)
+        quantise_g(5, 1)
+        recover(5)
+        product_q(0, 0, 3)
         subtract(4)
         quantise_g(6, 1)
         recover(6)
         quantise_rest(2, 2)
+        product_r(0, 0, 0, 1)
+        subtract(5)
         quantise_g(7, 1)
         recover(7)
-        product_r(0, 0, 0, 1, 2, 3)
-        subtract(5)
+        product_r(0, 0, 2, 3)
         subtract(6)
-        quantise_g(8, 2)
+        quantise_g(8, 1)
         recover(8)
         quantise_rest(4, 2)
-        recover(9)
-        product_q(0, 1, 0, 1, 2, 3)
+        product_q(0, 1, 0, 1)
         subtract(7)
+        quantise_g(9, 1)
+        recover(9)
+        product_q(0, 1, 2, 3)
         subtract(8)
-        quantise_g(10, 2)
+        quantise_g(10, 1)
         recover(10)
         quantise_rest(6, 2)
         product_r(0, 1, 0, 1)
         subtract(9)
+        quantise_g(11, 1)
         recover(11)
         product_r(0, 1, 2, 3)
         scale(0)

@@ -29,7 +29,9 @@ PIECES = 2 * CHUNKS
 STRIPS = 2 * PIECES
 N_TILES = N // P
 PAIR = 2
-WARM_PASSES = 2
+G_GROUPS = ((0,), (1,), (2,), (3,), (4,), (5,), (6,), (7,))
+REST_GROUPS = ((0,), (1,), (2,), (3,), (4,), (5,), (6, 7))
+LAST_BANK = 3
 BF16_ONE = 0x3F80
 STRETCHES = ((0, BANK, (0, 1, 2, 3)), (BANK, PIECE, (6, 7)), (BANK + PIECE, PIECE, (0, 1)))
 PIECE_AT = tuple(
@@ -48,22 +50,26 @@ def tile_mix_tierg_ls_kernel(tc, g, w4_words, w4_scales, res, ls, out):
             return [sb.tile(shape, dtype, name="%s%d" % (name, i), align_bytes=64) for i in range(count)]
 
         g_rows = tiles("g_rows", PIECES, [P, PACK, PIECE], F32)
-        g_words = [
-            sb.tile([P, PIECE * PACK], BF16, name="g_words%d" % i, tag="g_words%d" % i, align_bytes=64)
-            for i in range(PIECES)
-        ]
-        rest_words = [
-            sb.tile([P, PIECE * PACK], BF16, name="rest_words%d" % i, tag="rest_words%d" % i, align_bytes=64)
-            for i in range(PIECES)
-        ]
-        q_codes = tiles("q_codes", PASSES, [P, T], U32)
-        q_scales = tiles("q_scales", PASSES, [P, T], U8)
-        r_codes = tiles("r_codes", PASSES, [P, T], U32)
-        r_scales = tiles("r_scales", PASSES, [P, T], U8)
+        def word_tiles(name, groups):
+            found = {}
+            for group in groups:
+                full = "%s%d" % (name, group[0])
+                tile = sb.tile([P, len(group) * PIECE * PACK], BF16, name=full, tag=full, align_bytes=64)
+                for i in group:
+                    found[i] = (tile, group[0])
+            return found
+
+        g_words = word_tiles("g_words", G_GROUPS)
+        rest_words = word_tiles("rest_words", REST_GROUPS)
+        q_codes = sb.tile([P, PIECES * PIECE], U32, name="q_codes", align_bytes=64)
+        q_scales = sb.tile([P, PIECES * PIECE], U8, name="q_scales", align_bytes=64)
+        r_codes = sb.tile([P, PIECES * PIECE], U32, name="r_codes", align_bytes=64)
+        r_scales = sb.tile([P, PIECES * PIECE], U8, name="r_scales", align_bytes=64)
         w_words = tiles("w_words", PASSES, [P, 2 * N], U8)
         w_scales = sb.tile([P, PASSES, N], U8, name="w_scales", align_bytes=64)
         ls_cols = sb.tile([P, N_TILES], F32, name="ls_cols", align_bytes=64)
-        res_half = tiles("res_half", N_TILES, [P, BANK], F32)
+        res_half = sb.tile([P, N_TILES * BANK], F32, name="res_half", align_bytes=64)
+        scaled = sb.tile([P, N_TILES * BANK], F32, name="scaled", align_bytes=64)
         res_quarter = tiles("res_quarter", 2, [P, N_TILES, PIECE], F32)
         out_quarter = tiles("out_quarter", 4, [P, 2, PIECE], F32)
         ramp = sb.tile([P, 2 * P], I32, name="ramp", align_bytes=64)
@@ -95,25 +101,26 @@ def tile_mix_tierg_ls_kernel(tc, g, w4_words, w4_scales, res, ls, out):
         )
 
         warm_bank = psum.tile([P, BANK], F32, name="warm_bank", tag="bank0")
-        for j in range(WARM_PASSES):
-            nc.tensor.matmul_mx(
-                out=warm_bank[:],
-                lhsT=eye_codes[:, 0:P].bitcast(E4M3),
-                lhsT_scale=eye_scales[:, 0:P],
-                rhs=eye_codes[:].bitcast(E5M2),
-                rhs_scale=eye_scales[:],
-                start=True,
-                stop=True,
-            )
+
+        def warm_tensor(passes):
+            for count in range(passes):
+                nc.tensor.matmul_mx(
+                    out=warm_bank[:],
+                    lhsT=eye_codes[:, 0:P].bitcast(E4M3),
+                    lhsT_scale=eye_scales[:, 0:P],
+                    rhs=eye_codes[:].bitcast(E5M2),
+                    rhs_scale=eye_scales[:],
+                    start=True,
+                    stop=True,
+                )
 
         values = {}
         sums = {}
-        scaled = {}
 
-        def load_g(i):
+        def load_g(i, lo=0, hi=PIECE):
             a, t0 = PIECE_AT[i]
-            rows = g[a * K_PASS : (a + 1) * K_PASS, t0 : t0 + PIECE]
-            nc.sync.dma_start(out=g_rows[i][:], in_=rows.rearrange("(p j) w -> p j w", j=PACK))
+            rows = g[a * K_PASS : (a + 1) * K_PASS, t0 + lo : t0 + hi]
+            nc.sync.dma_start(out=g_rows[i][:, :, lo:hi], in_=rows.rearrange("(p j) w -> p j w", j=PACK))
 
         def load_words(a):
             nc.sync.dma_start(out=w_words[a][:], in_=w4_words[a])
@@ -130,14 +137,15 @@ def tile_mix_tierg_ls_kernel(tc, g, w4_words, w4_scales, res, ls, out):
                 nc.sync.dma_start(out=ls_cols[:], in_=ls.rearrange("(c p) -> p c", p=P))
 
         def load_res_half(n):
-            nc.sync.dma_start(out=res_half[n][:], in_=res[n * P : (n + 1) * P, 0:BANK])
+            nc.sync.dma_start(out=res_half[:, n * BANK : (n + 1) * BANK], in_=res[n * P : (n + 1) * P, 0:BANK])
 
         def load_res_quarter(b):
             t0 = STRETCHES[b][0]
             nc.sync.dma_start(out=res_quarter[b - 1][:], in_=res[:, t0 : t0 + PIECE].rearrange("(c p) w -> p c w", p=P))
 
-        def as_words(tile, s, count):
-            lo = (s % 2) * STRIP * PACK
+        def as_words(words, s, count):
+            tile, first = words[s // 2]
+            lo = (s - 2 * first) * STRIP * PACK
             return tile[:, lo : lo + count * STRIP * PACK]
 
         def walk_words(words):
@@ -151,29 +159,27 @@ def tile_mix_tierg_ls_kernel(tc, g, w4_words, w4_scales, res, ls, out):
             return g_rows[s // 2][:, :, lo : lo + count * STRIP]
 
         def strip_cols(rows, s, count):
-            a, t0 = PIECE_AT[s // 2]
-            lo = t0 + (s % 2) * STRIP
-            return rows[a][:, lo : lo + count * STRIP]
+            return rows[:, s * STRIP : (s + count) * STRIP]
 
         def round_g(copy, s, count):
-            copy(out=walk_words(as_words(g_words[s // 2], s, count)), in_=walk_rows(rows_of(s, count)))
+            copy(out=walk_words(as_words(g_words, s, count)), in_=walk_rows(rows_of(s, count)))
 
         def quantise_g(s, count):
             nc.vector.quantize_mx(
                 out=strip_cols(q_codes, s, count).bitcast(E5M2),
                 scales=strip_cols(q_scales, s, count),
-                in_=as_words(g_words[s // 2], s, count),
+                in_=as_words(g_words, s, count),
             )
 
         def quantise_rest(s, count):
             nc.vector.quantize_mx(
                 out=strip_cols(r_codes, s, count).bitcast(E4M3),
                 scales=strip_cols(r_scales, s, count),
-                in_=as_words(rest_words[s // 2], s, count),
+                in_=as_words(rest_words, s, count),
             )
 
         def recover(s):
-            bank = 4 + s % (4 if s < STRIPS // 2 else 2)
+            bank = LAST_BANK if s == STRIPS - 1 else 4 + s % (4 if s < STRIPS // 2 else 2)
             values[s] = psum.tile([P, PACK, STRIP], F32, name="values%d" % s, tag="bank%d" % bank)
             for j in range(PACK):
                 cols = slice(j * P, (j + 1) * P)
@@ -189,7 +195,7 @@ def tile_mix_tierg_ls_kernel(tc, g, w4_words, w4_scales, res, ls, out):
 
         def subtract(s):
             nc.vector.tensor_tensor(
-                out=walk_words(as_words(rest_words[s // 2], s, 1)),
+                out=walk_words(as_words(rest_words, s, 1)),
                 in0=walk_rows(rows_of(s, 1)),
                 in1=walk_rows(values[s][:]),
                 op=ALU.subtract,
@@ -206,12 +212,13 @@ def tile_mix_tierg_ls_kernel(tc, g, w4_words, w4_scales, res, ls, out):
         def product(codes, scales, fmt, b, a, n, first, last):
             t0, width, banks = STRETCHES[b]
             share = BANK // width
+            lo = PIECE_AT.index((a, t0)) * PIECE
             nc.tensor.matmul_mx(
                 out=sum_of(b, n),
                 lhsT=w_words[a][:, 2 * P * n : 2 * P * (n + 1)].bitcast(E2M1),
                 lhsT_scale=w_scales[:, a, P * n : P * (n + 1)],
-                rhs=codes[a][:, t0 : t0 + width].bitcast(fmt),
-                rhs_scale=scales[a][:, t0 : t0 + width],
+                rhs=codes[:, lo : lo + width].bitcast(fmt),
+                rhs_scale=scales[:, lo : lo + width],
                 start=first and n % share == 0,
                 stop=last and n % share == share - 1,
             )
@@ -224,26 +231,38 @@ def tile_mix_tierg_ls_kernel(tc, g, w4_words, w4_scales, res, ls, out):
             for n in n_tiles:
                 product(r_codes, r_scales, E4M3, b, a, n, False, a == PASSES - 1)
 
-        def scale(n):
-            scaled[n] = sb.tile([P, BANK], F32, name="scaled%d" % n, align_bytes=64)
-            nc.scalar.activation(out=scaled[n][:], in_=sum_of(0, n), func=ACT.Copy, scale=ls_cols[:, n : n + 1])
+        def scale(n, width=BANK):
+            nc.scalar.activation(
+                out=scaled[:, n * BANK : n * BANK + width],
+                in_=sum_of(0, n)[:, 0:width],
+                func=ACT.Copy,
+                scale=ls_cols[:, n : n + 1],
+            )
 
-        def add_res(n, slot):
-            result = sb.tile([P, BANK], F32, name="out_half%d" % n, tag=slot, align_bytes=64)
-            nc.gpsimd.tensor_tensor(out=result[:], in0=scaled[n][:], in1=res_half[n][:], op=ALU.add)
-            nc.sync.dma_start(out=out[n * P : (n + 1) * P, 0:BANK], in_=result[:])
+        def store_half(result, lo, hi):
+            for n in range(lo // BANK, (hi - 1) // BANK + 1):
+                first, last = max(lo, n * BANK), min(hi, (n + 1) * BANK)
+                nc.sync.dma_start(
+                    out=out[n * P : (n + 1) * P, first - n * BANK : last - n * BANK],
+                    in_=result[:, first - lo : last - lo],
+                )
 
-        def finish_half(n):
-            result = sb.tile([P, BANK], F32, name="out_half%d" % n, align_bytes=64)
+        def add_res(lo, hi, slot):
+            result = sb.tile([P, hi - lo], F32, name="added%d" % lo, tag=slot, align_bytes=64)
+            nc.gpsimd.tensor_tensor(out=result[:], in0=scaled[:, lo:hi], in1=res_half[:, lo:hi], op=ALU.add)
+            store_half(result, lo, hi)
+
+        def finish_half(n, lo=0, hi=BANK):
+            result = sb.tile([P, hi - lo], F32, name="out_half%d_%d" % (n, lo), align_bytes=64)
             nc.vector.scalar_tensor_tensor(
                 out=result[:],
-                in0=sum_of(0, n),
+                in0=sum_of(0, n)[:, lo:hi],
                 scalar=ls_cols[:, n : n + 1],
-                in1=res_half[n][:],
+                in1=res_half[:, n * BANK + lo : n * BANK + hi],
                 op0=ALU.mult,
                 op1=ALU.add,
             )
-            nc.sync.dma_start(out=out[n * P : (n + 1) * P, 0:BANK], in_=result[:])
+            store_half(result, n * BANK + lo, n * BANK + hi)
 
         def store_tile(b, n, queue):
             t0 = STRETCHES[b][0]
@@ -266,8 +285,9 @@ def tile_mix_tierg_ls_kernel(tc, g, w4_words, w4_scales, res, ls, out):
             rows = out[2 * pair * P : 2 * (pair + 1) * P, t0 : t0 + PIECE]
             queue.dma_start(out=rows.rearrange("(c p) w -> p c w", p=P), in_=out_quarter[2 * (b - 1) + pair][:])
 
-        for i in range(3):
-            load_g(i)
+        load_g(0)
+        load_g(1)
+        load_g(2)
         load_words(0)
         load_scales()
         load_g(3)
@@ -277,11 +297,12 @@ def tile_mix_tierg_ls_kernel(tc, g, w4_words, w4_scales, res, ls, out):
         load_g(6)
         load_ls()
         load_g(7)
-        for n in (0, 2, 1, 3):
+        for n in (0, 3, 1, 2):
             load_res_half(n)
         load_res_quarter(1)
         load_res_quarter(2)
 
+        warm_tensor(2)
         round_g(nc.vector.tensor_copy, 0, 1)
         round_g(nc.scalar.copy, 1, 1)
         quantise_g(0, 1)
@@ -292,9 +313,9 @@ def tile_mix_tierg_ls_kernel(tc, g, w4_words, w4_scales, res, ls, out):
         for s in range(3, 12):
             round_g(nc.scalar.copy, s, 1)
         round_g(nc.scalar.copy, 12, 2)
-        subtract(0)
         quantise_g(2, 1)
         recover(2)
+        subtract(0)
         quantise_g(3, 1)
         recover(3)
         subtract(1)
@@ -338,45 +359,45 @@ def tile_mix_tierg_ls_kernel(tc, g, w4_words, w4_scales, res, ls, out):
         scale(0)
         round_g(nc.scalar.copy, 14, 2)
         scale(1)
+        scale(2, 128)
         subtract(10)
         quantise_g(12, 2)
         recover(12)
-        add_res(0, "g_words6")
+        add_res(0, BANK, "g_words6")
         quantise_rest(8, 2)
         product_q(1, 0, 0, 1, 2, 3)
         subtract(11)
         recover(13)
         product_q(1, 1, 0, 1, 2, 3)
-        product_r(1, 0, 0, 1, 2, 3)
+        product_r(1, 0, 0, 1)
         subtract(12)
-        finish_half(2)
+        finish_half(3)
         quantise_g(14, 2)
         recover(14)
-        add_res(1, "g_words7")
-        quantise_rest(10, 2)
-        product_r(1, 1, 0, 1)
-        subtract(13)
         recover(15)
-        product_r(1, 1, 2, 3)
+        add_res(BANK, 2 * BANK + 128, "g_words7")
+        quantise_rest(10, 2)
+        product_r(1, 0, 2, 3)
+        subtract(13)
+        product_r(1, 1, 0, 1, 2, 3)
         product_q(2, 0, 0, 1, 2, 3)
         product_q(2, 1, 0, 1, 2, 3)
         subtract(14)
-        finish_half(3)
-        quantise_rest(12, 2)
-        product_r(2, 0, 0, 1, 2, 3)
         subtract(15)
-        finish(1, 0)
-        quantise_rest(14, 2)
-        product_r(2, 1, 0, 1, 2, 3)
-        finish(1, 1)
-        store(1, 0, nc.scalar)
-        finish(1, 2)
-        finish(1, 3)
-        store(1, 1, nc.sync)
+        finish_half(2, 128, BANK)
+        quantise_rest(12, 4)
+        product_r(2, 0, 0, 1)
+        product_r(2, 1, 0, 1)
+        product_r(2, 0, 2, 3)
+        product_r(2, 1, 2, 3)
+        for n in range(N_TILES):
+            finish(1, n)
+            store_tile(1, n, (nc.scalar, nc.sync)[n % 2])
         finish(2, 0)
+        store_tile(2, 0, nc.scalar)
         finish(2, 1)
-        store(2, 0, nc.scalar)
+        store_tile(2, 1, nc.sync)
         finish(2, 2)
-        store_tile(2, 2, nc.sync)
+        store_tile(2, 2, nc.scalar)
         finish(2, 3)
-        store_tile(2, 3, nc.scalar)
+        store_tile(2, 3, nc.sync)

@@ -32,6 +32,7 @@ PAIR = 2
 G_GROUPS = ((0,), (1,), (2,), (3,), (4,), (5,), (6,), (7,))
 REST_GROUPS = ((0,), (1,), (2,), (3,), (4,), (5,), (6, 7))
 LAST_BANK = 3
+LOADS = ((0,), (1, 2), (3,), (4, 5), (6, 7), (8, 9), (10, 11), (12, 13), (14, 15))
 BF16_ONE = 0x3F80
 STRETCHES = ((0, BANK, (0, 1, 2, 3)), (BANK, PIECE, (6, 7)), (BANK + PIECE, PIECE, (0, 1)))
 PIECE_AT = tuple(
@@ -49,7 +50,11 @@ def tile_mix_tierg_ls_kernel(tc, g, w4_words, w4_scales, res, ls, out):
         def tiles(name, count, shape, dtype):
             return [sb.tile(shape, dtype, name="%s%d" % (name, i), align_bytes=64) for i in range(count)]
 
-        g_rows = tiles("g_rows", PIECES, [P, PACK, PIECE], F32)
+        g_rows = {}
+        for strips in LOADS:
+            tile = sb.tile([P, PACK, len(strips) * STRIP], F32, name="g_rows%d" % strips[0], align_bytes=64)
+            for s in strips:
+                g_rows[s] = (tile, strips[0])
         def word_tiles(name, groups):
             found = {}
             for group in groups:
@@ -117,10 +122,12 @@ def tile_mix_tierg_ls_kernel(tc, g, w4_words, w4_scales, res, ls, out):
         values = {}
         sums = {}
 
-        def load_g(i, lo=0, hi=PIECE):
-            a, t0 = PIECE_AT[i]
-            rows = g[a * K_PASS : (a + 1) * K_PASS, t0 + lo : t0 + hi]
-            nc.sync.dma_start(out=g_rows[i][:, :, lo:hi], in_=rows.rearrange("(p j) w -> p j w", j=PACK))
+        def load_g(i):
+            strips = LOADS[i]
+            a, t0 = PIECE_AT[strips[0] // 2]
+            t0 = t0 + (strips[0] % 2) * STRIP
+            rows = g[a * K_PASS : (a + 1) * K_PASS, t0 : t0 + len(strips) * STRIP]
+            nc.sync.dma_start(out=g_rows[strips[0]][0][:], in_=rows.rearrange("(p j) w -> p j w", j=PACK))
 
         def load_words(a):
             nc.sync.dma_start(out=w_words[a][:], in_=w4_words[a])
@@ -155,8 +162,8 @@ def tile_mix_tierg_ls_kernel(tc, g, w4_words, w4_scales, res, ls, out):
             return rows.rearrange("p j (c i) -> p c j i", i=PAIR)
 
         def rows_of(s, count):
-            lo = (s % 2) * STRIP
-            return g_rows[s // 2][:, :, lo : lo + count * STRIP]
+            tile, first = g_rows[s]
+            return tile[:, :, (s - first) * STRIP : (s - first + count) * STRIP]
 
         def strip_cols(rows, s, count):
             return rows[:, s * STRIP : (s + count) * STRIP]
@@ -209,12 +216,14 @@ def tile_mix_tierg_ls_kernel(tc, g, w4_words, w4_scales, res, ls, out):
                 sums[(b, n // share)] = psum.tile([P, share, width], F32, name=name, tag="bank%d" % banks[n // share])
             return sums[(b, n // share)][:, n % share, :]
 
-        def product(codes, scales, fmt, b, a, n, first, last):
+        def product(codes, scales, fmt, b, a, n, first, last, part=None):
             t0, width, banks = STRETCHES[b]
             share = BANK // width
-            lo = PIECE_AT.index((a, t0)) * PIECE
+            start = 0 if part is None else part * PIECE
+            width = width if part is None else PIECE
+            lo = PIECE_AT.index((a, t0)) * PIECE + start
             nc.tensor.matmul_mx(
-                out=sum_of(b, n),
+                out=sum_of(b, n)[:, start : start + width],
                 lhsT=w_words[a][:, 2 * P * n : 2 * P * (n + 1)].bitcast(E2M1),
                 lhsT_scale=w_scales[:, a, P * n : P * (n + 1)],
                 rhs=codes[:, lo : lo + width].bitcast(fmt),
@@ -230,6 +239,10 @@ def tile_mix_tierg_ls_kernel(tc, g, w4_words, w4_scales, res, ls, out):
         def product_r(b, a, *n_tiles):
             for n in n_tiles:
                 product(r_codes, r_scales, E4M3, b, a, n, False, a == PASSES - 1)
+
+        def product_r_piece(a, part, *n_tiles):
+            for n in n_tiles:
+                product(r_codes, r_scales, E4M3, 0, a, n, False, a == PASSES - 1 and part == 1, part)
 
         def scale(n, width=BANK):
             nc.scalar.activation(
@@ -288,15 +301,16 @@ def tile_mix_tierg_ls_kernel(tc, g, w4_words, w4_scales, res, ls, out):
         load_g(0)
         load_g(1)
         load_g(2)
+        load_g(3)
         load_words(0)
         load_scales()
-        load_g(3)
         load_g(4)
-        load_words(1)
         load_g(5)
+        load_words(1)
         load_g(6)
-        load_ls()
         load_g(7)
+        load_ls()
+        load_g(8)
         for n in (0, 3, 1, 2):
             load_res_half(n)
         load_res_quarter(1)
@@ -304,15 +318,14 @@ def tile_mix_tierg_ls_kernel(tc, g, w4_words, w4_scales, res, ls, out):
 
         warm_tensor(2)
         round_g(nc.vector.tensor_copy, 0, 1)
-        round_g(nc.scalar.copy, 1, 1)
         quantise_g(0, 1)
         recover(0)
-        quantise_g(1, 1)
-        recover(1)
-        round_g(nc.vector.tensor_copy, 2, 1)
-        for s in range(3, 12):
+        round_g(nc.vector.tensor_copy, 1, 1)
+        for s in range(2, 12):
             round_g(nc.scalar.copy, s, 1)
         round_g(nc.scalar.copy, 12, 2)
+        quantise_g(1, 1)
+        recover(1)
         quantise_g(2, 1)
         recover(2)
         subtract(0)
@@ -324,20 +337,21 @@ def tile_mix_tierg_ls_kernel(tc, g, w4_words, w4_scales, res, ls, out):
         quantise_g(4, 1)
         recover(4)
         quantise_rest(0, 2)
-        product_q(0, 0, 2)
+        product_q(0, 0, 2, 3)
         subtract(3)
         quantise_g(5, 1)
         recover(5)
-        product_q(0, 0, 3)
+        product_r_piece(0, 0, 0, 1)
         subtract(4)
         quantise_g(6, 1)
         recover(6)
         quantise_rest(2, 2)
-        product_r(0, 0, 0, 1)
+        product_r_piece(0, 0, 2, 3)
+        product_r_piece(0, 1, 0, 1)
         subtract(5)
         quantise_g(7, 1)
         recover(7)
-        product_r(0, 0, 2, 3)
+        product_r_piece(0, 1, 2, 3)
         subtract(6)
         quantise_g(8, 1)
         recover(8)
@@ -346,7 +360,7 @@ def tile_mix_tierg_ls_kernel(tc, g, w4_words, w4_scales, res, ls, out):
         subtract(7)
         quantise_g(9, 1)
         recover(9)
-        product_q(0, 1, 2, 3)
+        product_q(0, 1, 3, 2)
         subtract(8)
         quantise_g(10, 1)
         recover(10)
@@ -355,21 +369,22 @@ def tile_mix_tierg_ls_kernel(tc, g, w4_words, w4_scales, res, ls, out):
         subtract(9)
         quantise_g(11, 1)
         recover(11)
-        product_r(0, 1, 2, 3)
+        product_r(0, 1, 3)
         scale(0)
         round_g(nc.scalar.copy, 14, 2)
         scale(1)
-        scale(2, 128)
         subtract(10)
         quantise_g(12, 2)
         recover(12)
         add_res(0, BANK, "g_words6")
         quantise_rest(8, 2)
-        product_q(1, 0, 0, 1, 2, 3)
+        product_r(0, 1, 2)
+        scale(2, 128)
+        product_q(1, 0, 0, 1)
         subtract(11)
         recover(13)
+        product_q(1, 0, 2, 3)
         product_q(1, 1, 0, 1, 2, 3)
-        product_r(1, 0, 0, 1)
         subtract(12)
         finish_half(3)
         quantise_g(14, 2)
@@ -377,17 +392,19 @@ def tile_mix_tierg_ls_kernel(tc, g, w4_words, w4_scales, res, ls, out):
         recover(15)
         add_res(BANK, 2 * BANK + 128, "g_words7")
         quantise_rest(10, 2)
-        product_r(1, 0, 2, 3)
         subtract(13)
+        product_r(1, 0, 0, 1, 2, 3)
         product_r(1, 1, 0, 1, 2, 3)
-        product_q(2, 0, 0, 1, 2, 3)
-        product_q(2, 1, 0, 1, 2, 3)
+        product_q(2, 0, 0, 1)
+        product_q(2, 1, 0, 1)
+        product_q(2, 0, 2, 3)
         subtract(14)
         subtract(15)
         finish_half(2, 128, BANK)
         quantise_rest(12, 4)
         product_r(2, 0, 0, 1)
         product_r(2, 1, 0, 1)
+        product_q(2, 1, 2, 3)
         product_r(2, 0, 2, 3)
         product_r(2, 1, 2, 3)
         for n in range(N_TILES):

@@ -84,11 +84,6 @@ def tile_mix_tierg_ls_kernel(tc, g, w4_words, w4_scales, res, ls, out):
 
         nc.gpsimd.iota(ramp[:], pattern=[[1, 2 * P]], base=0, channel_multiplier=-2)
 
-        warm_in = sb.tile([P, 16], F32, name="warm_in", align_bytes=64)
-        warm_out = sb.tile([P, 16], F32, name="warm_out", align_bytes=64)
-        nc.vector.memset(warm_in[:], 0.0)
-        nc.scalar.copy(out=warm_out[:], in_=warm_in[:])
-
         nc.vector.memset(w_scales[:].rearrange("p a n -> p (a n)").bitcast(I32), 0)
         for j in range(PACK):
             nc.vector.tensor_scalar(

@@ -29,6 +29,7 @@ PIECES = 2 * CHUNKS
 STRIPS = 2 * PIECES
 N_TILES = N // P
 PAIR = 2
+LINE = 4
 G_GROUPS = ((0,), (1,), (2,), (3,), (4,), (5,), (6,), (7,))
 REST_GROUPS = ((0,), (1,), (2,), (3,), (4,), (5,), (6, 7))
 LAST_BANK = 3
@@ -116,6 +117,7 @@ def tile_mix_tierg_ls_kernel(tc, g, w4_words, w4_scales, res, ls, out):
 
         values = {}
         sums = {}
+        shared = {}
 
         def load_g(i):
             strips = LOADS[i]
@@ -150,11 +152,11 @@ def tile_mix_tierg_ls_kernel(tc, g, w4_words, w4_scales, res, ls, out):
             lo = (s - 2 * first) * STRIP * PACK
             return tile[:, lo : lo + count * STRIP * PACK]
 
-        def walk_words(words):
-            return words.rearrange("p (c i j) -> p c j i", i=PAIR, j=PACK)
+        def walk_words(words, run=PAIR):
+            return words.rearrange("p (c i j) -> p c j i", i=run, j=PACK)
 
-        def walk_rows(rows):
-            return rows.rearrange("p j (c i) -> p c j i", i=PAIR)
+        def walk_rows(rows, run=PAIR):
+            return rows.rearrange("p j (c i) -> p c j i", i=run)
 
         def rows_of(s, count):
             tile, first = g_rows[s]
@@ -197,9 +199,9 @@ def tile_mix_tierg_ls_kernel(tc, g, w4_words, w4_scales, res, ls, out):
 
         def subtract(s):
             nc.vector.tensor_tensor(
-                out=walk_words(as_words(rest_words, s, 1)),
-                in0=walk_rows(rows_of(s, 1)),
-                in1=walk_rows(values[s][:]),
+                out=walk_words(as_words(rest_words, s, 1), LINE),
+                in0=walk_rows(rows_of(s, 1), LINE),
+                in1=walk_rows(values[s][:], LINE),
                 op=ALU.subtract,
             )
 
@@ -256,21 +258,25 @@ def tile_mix_tierg_ls_kernel(tc, g, w4_words, w4_scales, res, ls, out):
                 )
 
         def add_res(lo, hi, slot):
-            result = sb.tile([P, hi - lo], F32, name="added%d" % lo, tag=slot, align_bytes=64)
-            nc.gpsimd.tensor_tensor(out=result[:], in0=scaled[:, lo:hi], in1=res_half[:, lo:hi], op=ALU.add)
-            store_half(result, lo, hi)
+            whole = (hi + BANK - 1) // BANK * BANK
+            result = sb.tile([P, whole - lo], F32, name="added%d" % lo, tag=slot, align_bytes=64)
+            nc.gpsimd.tensor_tensor(out=result[:, 0 : hi - lo], in0=scaled[:, lo:hi], in1=res_half[:, lo:hi], op=ALU.add)
+            store_half(result, lo, lo + BANK)
+            if hi < whole:
+                shared[hi // BANK] = result[:, whole - BANK - lo : whole - lo]
 
         def finish_half(n, lo=0, hi=BANK):
-            result = sb.tile([P, hi - lo], F32, name="out_half%d_%d" % (n, lo), align_bytes=64)
+            if n not in shared:
+                shared[n] = sb.tile([P, BANK], F32, name="out_half%d" % n, align_bytes=64)[:]
             nc.vector.scalar_tensor_tensor(
-                out=result[:],
+                out=shared[n][:, lo:hi],
                 in0=sum_of(0, n)[:, lo:hi],
                 scalar=ls_cols[:, n : n + 1],
                 in1=res_half[:, n * BANK + lo : n * BANK + hi],
                 op0=ALU.mult,
                 op1=ALU.add,
             )
-            store_half(result, n * BANK + lo, n * BANK + hi)
+            store_half(shared[n], n * BANK, (n + 1) * BANK)
 
         def store_tile(b, n, queue):
             t0 = STRETCHES[b][0]
@@ -393,18 +399,23 @@ def tile_mix_tierg_ls_kernel(tc, g, w4_words, w4_scales, res, ls, out):
         product_q(2, 0, 0, 1)
         product_q(2, 1, 0, 1)
         product_q(2, 0, 2, 3)
+        product_q(2, 1, 2, 3)
         subtract(14)
         subtract(15)
         finish_half(2, 128, BANK)
         quantise_rest(12, 4)
         product_r(2, 0, 0, 1)
         product_r(2, 1, 0, 1)
-        product_q(2, 1, 2, 3)
         product_r(2, 0, 2, 3)
         product_r(2, 1, 2, 3)
-        for n in range(N_TILES):
-            finish(1, n)
-            store_tile(1, n, (nc.scalar, nc.sync)[n % 2])
+        finish(1, 0)
+        store_tile(1, 0, nc.scalar)
+        finish(1, 1)
+        store_tile(1, 1, nc.sync)
+        finish(1, 2)
+        store_tile(1, 2, nc.scalar)
+        finish(1, 3)
+        store_tile(1, 3, nc.sync)
         finish(2, 0)
         store_tile(2, 0, nc.scalar)
         finish(2, 1)

@@ -22,23 +22,21 @@ K_PASS = P * PACK
 BANK = 512
 STRIP = BANK // PACK
 PIECE = 2 * STRIP
+HALF = T // 2
 PASSES = K // K_PASS
-HALVES = T // BANK
-CHUNKS = PASSES * HALVES
-PIECES = 2 * CHUNKS
-STRIPS = 2 * PIECES
+STRIPS = PASSES * T // STRIP
 N_TILES = N // P
+QUAD = 32
 PAIR = 2
 LINE = 4
-G_GROUPS = ((0,), (1,), (2,), (3,), (4,), (5,), (6,), (7,))
-REST_GROUPS = ((0,), (1,), (2,), (3,), (4,), (5,), (6, 7))
-LAST_BANK = 3
-LOADS = ((0,), (1, 2), (3,), (4, 5), (6, 7), (8, 9), (10, 11), (12, 13), (14, 15))
 BF16_ONE = 0x3F80
-STRETCHES = ((0, BANK, (0, 1, 2, 3)), (BANK, PIECE, (6, 7)), (BANK + PIECE, PIECE, (0, 1)))
-PIECE_AT = tuple(
-    (a, t0 + lo) for t0, width, banks in STRETCHES for a in range(PASSES) for lo in range(0, width, PIECE)
-)
+LOADS = ((0,), (1, 2), (3,), (4, 5), (6, 7), (8, 9), (10, 11), (12, 13), (14, 15))
+STRETCHES = ((0, HALF, (0, 1, 2, 3)), (HALF, PIECE, (0, 3)), (HALF + PIECE, PIECE, (4, 5)))
+STRIP_AT = tuple((a, t0 + lo) for t0, width, banks in STRETCHES for a in range(PASSES) for lo in range(0, width, STRIP))
+VALUE_BANKS = tuple(4 + s % 4 for s in range(STRIPS))
+WORD_GROUPS = tuple((s, s + 1) for s in range(0, STRIPS, 2))
+REST_GROUPS = ((0, 1), (2, 3), (4, 5), (6, 7), (8, 9), (10, 11), (12, 13, 14, 15))
+RES_LOADS = ((0, 2, HALF, HALF), (2, 2, HALF, HALF))
 
 
 def tile_mix_tierg_ls_kernel(tc, g, w4_words, w4_scales, res, ls, out):
@@ -48,44 +46,47 @@ def tile_mix_tierg_ls_kernel(tc, g, w4_words, w4_scales, res, ls, out):
         psum = ctx.enter_context(tc.psum_pool(name="psum", bufs=1))
         ctx.enter_context(tc.manual_schedule())
 
-        def tiles(name, count, shape, dtype):
-            return [sb.tile(shape, dtype, name="%s%d" % (name, i), align_bytes=64) for i in range(count)]
+        def tile(name, shape, dtype, tag=None):
+            return sb.tile(shape, dtype, name=name, tag=tag or name, align_bytes=64)
 
         g_rows = {}
         for strips in LOADS:
-            tile = sb.tile([P, PACK, len(strips) * STRIP], F32, name="g_rows%d" % strips[0], align_bytes=64)
+            rows = tile("g_rows%d" % strips[0], [P, PACK, len(strips) * STRIP], F32)
             for s in strips:
-                g_rows[s] = (tile, strips[0])
-        def word_tiles(name, groups):
-            found = {}
-            for group in groups:
-                full = "%s%d" % (name, group[0])
-                tile = sb.tile([P, len(group) * PIECE * PACK], BF16, name=full, tag=full, align_bytes=64)
-                for i in group:
-                    found[i] = (tile, group[0])
-            return found
-
-        g_words = word_tiles("g_words", G_GROUPS)
-        rest_words = word_tiles("rest_words", REST_GROUPS)
-        q_codes = sb.tile([P, PIECES * PIECE], U32, name="q_codes", align_bytes=64)
-        q_scales = sb.tile([P, PIECES * PIECE], U8, name="q_scales", align_bytes=64)
-        r_codes = sb.tile([P, PIECES * PIECE], U32, name="r_codes", align_bytes=64)
-        r_scales = sb.tile([P, PIECES * PIECE], U8, name="r_scales", align_bytes=64)
-        w_words = tiles("w_words", PASSES, [P, 2 * N], U8)
-        w_scales = sb.tile([P, PASSES, N], U8, name="w_scales", align_bytes=64)
-        ls_cols = sb.tile([P, N_TILES], F32, name="ls_cols", align_bytes=64)
-        res_half = sb.tile([P, N_TILES * BANK], F32, name="res_half", align_bytes=64)
-        scaled = sb.tile([P, N_TILES * BANK], F32, name="scaled", align_bytes=64)
-        res_quarter = tiles("res_quarter", 2, [P, N_TILES, PIECE], F32)
-        out_quarter = tiles("out_quarter", 4, [P, 2, PIECE], F32)
-        ramp = sb.tile([P, 2 * P], I32, name="ramp", align_bytes=64)
-        eye_pairs = sb.tile([P, PACK, 2 * P], I32, name="eye_pairs", align_bytes=64)
-        eye_codes = sb.tile([P, PACK * P], U32, name="eye_codes", align_bytes=64)
-        eye_scales = sb.tile([P, PACK * P], U8, name="eye_scales", align_bytes=64)
+                g_rows[s] = (rows, strips[0])
+        g_words = {}
+        for group in WORD_GROUPS:
+            words = tile("g_words%d" % group[0], [P, len(group) * BANK], BF16)
+            for s in group:
+                g_words[s] = (words, group[0])
+        rest_words = {}
+        for group in REST_GROUPS:
+            words = tile("rest_words%d" % group[0], [P, len(group) * BANK], BF16)
+            for s in group:
+                rest_words[s] = (words, group[0])
+        q_codes = tile("q_codes", [P, STRIPS * STRIP], U32)
+        q_scales = tile("q_scales", [P, STRIPS * STRIP], U8)
+        r_codes = tile("r_codes", [P, STRIPS * STRIP], U32)
+        r_scales = tile("r_scales", [P, STRIPS * STRIP], U8)
+        w_words = [tile("w_words%d" % a, [P, 2 * N], U8) for a in range(PASSES)]
+        w_scales = tile("w_scales", [P, PASSES, N], U8)
+        ls_rows = tile("ls_rows", [P, N_TILES * QUAD], F32)
+        ls_cols = tile("ls_cols", [P, N_TILES * QUAD], F32)
+        res_at = {}
+        for i, (n0, count, t0, width) in enumerate(RES_LOADS):
+            rows = tile("res%d" % i, [P, count, width], F32)
+            for n in range(n0, n0 + count):
+                for t in range(t0, t0 + width, STRIP):
+                    res_at[(n, t)] = (rows, n0, t0)
+        res_half = tile("res_half", [P, N_TILES * HALF], F32)
+        scaled = tile("scaled", [P, N_TILES * HALF], F32)
+        ramp = tile("ramp", [P, 2 * P], I32)
+        eye_pairs = tile("eye_pairs", [P, PACK, 2 * P], I32)
+        eye_codes = tile("eye_codes", [P, PACK * P], U32)
+        eye_scales = tile("eye_scales", [P, PACK * P], U8)
 
         nc.gpsimd.iota(ramp[:], pattern=[[1, 2 * P]], base=0, channel_multiplier=-2)
-
-        nc.vector.memset(w_scales[:].rearrange("p a n -> p (a n)").bitcast(I32), 0)
+        nc.vector.memset(ls_rows[:], 0.0)
         for j in range(PACK):
             nc.vector.tensor_scalar(
                 out=eye_pairs[:, j, :],
@@ -95,15 +96,19 @@ def tile_mix_tierg_ls_kernel(tc, g, w4_words, w4_scales, res, ls, out):
                 op0=ALU.is_equal,
                 op1=ALU.mult,
             )
+        nc.vector.memset(w_scales[:].rearrange("p a n -> p (a n)").bitcast(I32), 0)
         nc.vector.quantize_mx(
             out=eye_codes[:].bitcast(E4M3),
             scales=eye_scales[:],
             in_=eye_pairs[:].rearrange("p j w -> p (j w)").bitcast(BF16),
         )
 
-        warm_bank = psum.tile([P, BANK], F32, name="warm_bank", tag="bank0")
+        values = {}
+        sums = {}
+        results = {}
 
         def warm_tensor(passes):
+            warm_bank = psum.tile([P, BANK], F32, name="warm_bank", tag="bank0")
             for count in range(passes):
                 nc.tensor.matmul_mx(
                     out=warm_bank[:],
@@ -115,95 +120,109 @@ def tile_mix_tierg_ls_kernel(tc, g, w4_words, w4_scales, res, ls, out):
                     stop=True,
                 )
 
-        values = {}
-        sums = {}
-        shared = {}
-
         def load_g(i):
             strips = LOADS[i]
-            a, t0 = PIECE_AT[strips[0] // 2]
-            t0 = t0 + (strips[0] % 2) * STRIP
+            a, t0 = STRIP_AT[strips[0]]
             rows = g[a * K_PASS : (a + 1) * K_PASS, t0 : t0 + len(strips) * STRIP]
             nc.sync.dma_start(out=g_rows[strips[0]][0][:], in_=rows.rearrange("(p j) w -> p j w", j=PACK))
 
         def load_words(a):
             nc.sync.dma_start(out=w_words[a][:], in_=w4_words[a])
 
-        def load_scales():
+        def load_scales(queue):
             for r in range(4):
-                nc.sync.dma_start(
+                queue.dma_start(
                     out=w_scales[r:P:32, :, :].bitcast(I32),
                     in_=w4_scales[:, r:16:4, :].rearrange("a q n -> q a n").bitcast(I32),
                 )
 
-        def load_ls():
-            with nc.allow_non_contiguous_dma("ls[128 c + p] goes to partition p"):
-                nc.sync.dma_start(out=ls_cols[:], in_=ls.rearrange("(c p) -> p c", p=P))
+        def load_ls(queue):
+            queue.dma_start(
+                out=ls_rows[0:P:QUAD, :].rearrange("q (c i) -> q c i", i=QUAD),
+                in_=ls.rearrange("(c q i) -> q c i", c=N_TILES, i=QUAD),
+            )
+
+        def turn_ls():
+            nc.vector.transpose(out=ls_cols[:], in_=ls_rows[:])
+
+        def ls_of(n):
+            return ls_cols[:, n * QUAD : n * QUAD + 1]
+
+        def load_res(i):
+            n0, count, t0, width = RES_LOADS[i]
+            rows = res[n0 * P : (n0 + count) * P, t0 : t0 + width]
+            nc.sync.dma_start(out=res_at[(n0, t0)][0][:], in_=rows.rearrange("(c p) w -> p c w", p=P))
 
         def load_res_half(n):
-            nc.sync.dma_start(out=res_half[:, n * BANK : (n + 1) * BANK], in_=res[n * P : (n + 1) * P, 0:BANK])
+            nc.sync.dma_start(out=res_half[:, n * HALF : (n + 1) * HALF], in_=res[n * P : (n + 1) * P, 0:HALF])
 
-        def load_res_quarter(b):
-            t0 = STRETCHES[b][0]
-            nc.sync.dma_start(out=res_quarter[b - 1][:], in_=res[:, t0 : t0 + PIECE].rearrange("(c p) w -> p c w", p=P))
+        def res_of(n, t, width):
+            if t < HALF:
+                return res_half[:, n * HALF + t : n * HALF + t + width]
+            rows, n0, t0 = res_at[(n, t)]
+            return rows[:, n - n0, t - t0 : t - t0 + width]
 
-        def as_words(words, s, count):
-            tile, first = words[s // 2]
-            lo = (s - 2 * first) * STRIP * PACK
-            return tile[:, lo : lo + count * STRIP * PACK]
+        def g_as_words(s, count):
+            words, first = g_words[s]
+            return words[:, (s - first) * BANK : (s - first + count) * BANK]
 
-        def walk_words(words, run=PAIR):
+        def rest_as_words(s, count):
+            words, first = rest_words[s]
+            return words[:, (s - first) * BANK : (s - first + count) * BANK]
+
+        def walk_words(words, run):
             return words.rearrange("p (c i j) -> p c j i", i=run, j=PACK)
 
-        def walk_rows(rows, run=PAIR):
+        def walk_rows(rows, run):
             return rows.rearrange("p j (c i) -> p c j i", i=run)
 
         def rows_of(s, count):
-            tile, first = g_rows[s]
-            return tile[:, :, (s - first) * STRIP : (s - first + count) * STRIP]
+            rows, first = g_rows[s]
+            return rows[:, :, (s - first) * STRIP : (s - first + count) * STRIP]
 
         def strip_cols(rows, s, count):
             return rows[:, s * STRIP : (s + count) * STRIP]
 
-        def round_g(copy, s, count):
-            copy(out=walk_words(as_words(g_words, s, count)), in_=walk_rows(rows_of(s, count)))
+        def round_g(copy, s, count=1):
+            copy(out=walk_words(g_as_words(s, count), PAIR), in_=walk_rows(rows_of(s, count), PAIR))
 
-        def quantise_g(s, count):
+        def quantise_g(s, count=1):
             nc.vector.quantize_mx(
                 out=strip_cols(q_codes, s, count).bitcast(E5M2),
                 scales=strip_cols(q_scales, s, count),
-                in_=as_words(g_words, s, count),
+                in_=g_as_words(s, count),
             )
 
-        def quantise_rest(s, count):
+        def quantise_rest(s, count=2):
             nc.vector.quantize_mx(
                 out=strip_cols(r_codes, s, count).bitcast(E4M3),
                 scales=strip_cols(r_scales, s, count),
-                in_=as_words(rest_words, s, count),
+                in_=rest_as_words(s, count),
             )
 
-        def recover(s):
-            bank = LAST_BANK if s == STRIPS - 1 else 4 + s % (4 if s < STRIPS // 2 else 2)
-            values[s] = psum.tile([P, PACK, STRIP], F32, name="values%d" % s, tag="bank%d" % bank)
-            for j in range(PACK):
-                cols = slice(j * P, (j + 1) * P)
-                nc.tensor.matmul_mx(
-                    out=values[s][:, j, :],
-                    lhsT=eye_codes[:, cols].bitcast(E4M3),
-                    lhsT_scale=eye_scales[:, cols],
-                    rhs=strip_cols(q_codes, s, 1).bitcast(E5M2),
-                    rhs_scale=strip_cols(q_scales, s, 1),
-                    start=True,
-                    stop=True,
+        def recover(*strips):
+            for s in strips:
+                values[s] = psum.tile([P, PACK, STRIP], F32, name="values%d" % s, tag="bank%d" % VALUE_BANKS[s])
+                for j in range(PACK):
+                    cols = slice(j * P, (j + 1) * P)
+                    nc.tensor.matmul_mx(
+                        out=values[s][:, j, :],
+                        lhsT=eye_codes[:, cols].bitcast(E4M3),
+                        lhsT_scale=eye_scales[:, cols],
+                        rhs=strip_cols(q_codes, s, 1).bitcast(E5M2),
+                        rhs_scale=strip_cols(q_scales, s, 1),
+                        start=True,
+                        stop=True,
+                    )
+
+        def subtract(*strips):
+            for s in strips:
+                nc.vector.tensor_tensor(
+                    out=walk_words(rest_as_words(s, 1), LINE),
+                    in0=walk_rows(rows_of(s, 1), LINE),
+                    in1=walk_rows(values[s][:], LINE),
+                    op=ALU.subtract,
                 )
-
-        def subtract(s):
-            nc.vector.tensor_tensor(
-                out=walk_words(as_words(rest_words, s, 1), LINE),
-                in0=walk_rows(rows_of(s, 1), LINE),
-                in1=walk_rows(values[s][:], LINE),
-                op=ALU.subtract,
-            )
 
         def sum_of(b, n):
             t0, width, banks = STRETCHES[b]
@@ -213,214 +232,158 @@ def tile_mix_tierg_ls_kernel(tc, g, w4_words, w4_scales, res, ls, out):
                 sums[(b, n // share)] = psum.tile([P, share, width], F32, name=name, tag="bank%d" % banks[n // share])
             return sums[(b, n // share)][:, n % share, :]
 
-        def product(codes, scales, fmt, b, a, n, first, last, part=None):
+        passes_done = {}
+
+        def product(tier, b, a, n_tiles, lo=0, hi=None):
+            codes, scales, fmt = ((q_codes, q_scales, E5M2), (r_codes, r_scales, E4M3))[tier]
             t0, width, banks = STRETCHES[b]
             share = BANK // width
-            start = 0 if part is None else part * PIECE
-            width = width if part is None else PIECE
-            lo = PIECE_AT.index((a, t0)) * PIECE + start
-            nc.tensor.matmul_mx(
-                out=sum_of(b, n)[:, start : start + width],
-                lhsT=w_words[a][:, 2 * P * n : 2 * P * (n + 1)].bitcast(E2M1),
-                lhsT_scale=w_scales[:, a, P * n : P * (n + 1)],
-                rhs=codes[:, lo : lo + width].bitcast(fmt),
-                rhs_scale=scales[:, lo : lo + width],
-                start=first and n % share == 0,
-                stop=last and n % share == share - 1,
-            )
-
-        def product_q(b, a, *n_tiles):
+            hi = width if hi is None else hi
+            first = STRIP_AT.index((a, t0 + lo)) * STRIP
             for n in n_tiles:
-                product(q_codes, q_scales, E5M2, b, a, n, a == 0, False)
-
-        def product_r(b, a, *n_tiles):
-            for n in n_tiles:
-                product(r_codes, r_scales, E4M3, b, a, n, False, a == PASSES - 1)
-
-        def product_r_piece(a, part, *n_tiles):
-            for n in n_tiles:
-                product(r_codes, r_scales, E4M3, 0, a, n, False, a == PASSES - 1 and part == 1, part)
-
-        def scale(n, width=BANK):
-            nc.scalar.activation(
-                out=scaled[:, n * BANK : n * BANK + width],
-                in_=sum_of(0, n)[:, 0:width],
-                func=ACT.Copy,
-                scale=ls_cols[:, n : n + 1],
-            )
-
-        def store_half(result, lo, hi):
-            for n in range(lo // BANK, (hi - 1) // BANK + 1):
-                first, last = max(lo, n * BANK), min(hi, (n + 1) * BANK)
-                nc.sync.dma_start(
-                    out=out[n * P : (n + 1) * P, first - n * BANK : last - n * BANK],
-                    in_=result[:, first - lo : last - lo],
+                done = passes_done.get((b, n // share), 0)
+                passes_done[(b, n // share)] = done + hi - lo
+                nc.tensor.matmul_mx(
+                    out=sum_of(b, n)[:, lo:hi],
+                    lhsT=w_words[a][:, 2 * P * n : 2 * P * (n + 1)].bitcast(E2M1),
+                    lhsT_scale=w_scales[:, a, P * n : P * (n + 1)],
+                    rhs=codes[:, first : first + hi - lo].bitcast(fmt),
+                    rhs_scale=scales[:, first : first + hi - lo],
+                    start=done == 0,
+                    stop=done + hi - lo == 2 * PASSES * BANK,
                 )
 
-        def add_res(lo, hi, slot):
-            whole = (hi + BANK - 1) // BANK * BANK
-            result = sb.tile([P, whole - lo], F32, name="added%d" % lo, tag=slot, align_bytes=64)
-            nc.gpsimd.tensor_tensor(out=result[:, 0 : hi - lo], in0=scaled[:, lo:hi], in1=res_half[:, lo:hi], op=ALU.add)
-            store_half(result, lo, lo + BANK)
-            if hi < whole:
-                shared[hi // BANK] = result[:, whole - BANK - lo : whole - lo]
+        def result_of(key, width, tag=None):
+            if key not in results:
+                results[key] = tile("out_%s" % key, [P, width], F32, tag=tag)
+            return results[key]
 
-        def finish_half(n, lo=0, hi=BANK):
-            if n not in shared:
-                shared[n] = sb.tile([P, BANK], F32, name="out_half%d" % n, align_bytes=64)[:]
+        def scale(b, n, lo, hi, at):
+            nc.scalar.activation(out=scaled[:, at : at + hi - lo], in_=sum_of(b, n)[:, lo:hi], func=ACT.Copy, scale=ls_of(n))
+
+        def add_res(dst, at, src):
+            nc.gpsimd.tensor_tensor(out=dst, in0=at, in1=src, op=ALU.add)
+
+        def finish(b, n, dst, lo=0, hi=None):
+            t0, width, banks = STRETCHES[b]
+            hi = width if hi is None else hi
             nc.vector.scalar_tensor_tensor(
-                out=shared[n][:, lo:hi],
-                in0=sum_of(0, n)[:, lo:hi],
-                scalar=ls_cols[:, n : n + 1],
-                in1=res_half[:, n * BANK + lo : n * BANK + hi],
-                op0=ALU.mult,
-                op1=ALU.add,
-            )
-            store_half(shared[n], n * BANK, (n + 1) * BANK)
-
-        def store_tile(b, n, queue):
-            t0 = STRETCHES[b][0]
-            queue.dma_start(
-                out=out[n * P : (n + 1) * P, t0 : t0 + PIECE], in_=out_quarter[2 * (b - 1) + n // 2][:, n % 2, :]
-            )
-
-        def finish(b, n):
-            nc.vector.scalar_tensor_tensor(
-                out=out_quarter[2 * (b - 1) + n // 2][:, n % 2, :],
-                in0=sum_of(b, n),
-                scalar=ls_cols[:, n : n + 1],
-                in1=res_quarter[b - 1][:, n, :],
+                out=dst,
+                in0=sum_of(b, n)[:, lo:hi],
+                scalar=ls_of(n),
+                in1=res_of(n, t0 + lo, hi - lo),
                 op0=ALU.mult,
                 op1=ALU.add,
             )
 
-        def store(b, pair, queue):
-            t0 = STRETCHES[b][0]
-            rows = out[2 * pair * P : 2 * (pair + 1) * P, t0 : t0 + PIECE]
-            queue.dma_start(out=rows.rearrange("(c p) w -> p c w", p=P), in_=out_quarter[2 * (b - 1) + pair][:])
+        def store(queue, n, t0, src):
+            queue.dma_start(out=out[n * P : (n + 1) * P, t0 : t0 + src.shape[1]], in_=src)
+
 
         load_g(0)
         load_g(1)
+        load_ls(nc.sync)
         load_g(2)
         load_g(3)
         load_words(0)
-        load_scales()
+        load_scales(nc.sync)
         load_g(4)
         load_g(5)
         load_words(1)
         load_g(6)
         load_g(7)
-        load_ls()
         load_g(8)
-        for n in (0, 3, 1, 2):
-            load_res_half(n)
-        load_res_quarter(1)
-        load_res_quarter(2)
-
+        for n in (0, 3, 1, 2): load_res_half(n)
+        for i in range(len(RES_LOADS)): load_res(i)
         warm_tensor(2)
-        round_g(nc.vector.tensor_copy, 0, 1)
-        quantise_g(0, 1)
+        round_g(nc.vector.tensor_copy, 0)
+        quantise_g(0)
         recover(0)
-        round_g(nc.vector.tensor_copy, 1, 1)
-        for s in range(2, 12):
-            round_g(nc.scalar.copy, s, 1)
+        round_g(nc.vector.tensor_copy, 1)
+        turn_ls()
+        for s in range(2, 10): round_g(nc.scalar.copy, s)
+        round_g(nc.scalar.copy, 10, 2)
         round_g(nc.scalar.copy, 12, 2)
-        quantise_g(1, 1)
+        quantise_g(1)
         recover(1)
-        quantise_g(2, 1)
+        quantise_g(2)
         recover(2)
         subtract(0)
-        quantise_g(3, 1)
+        quantise_g(3)
         recover(3)
         subtract(1)
-        product_q(0, 0, 0, 1)
+        product(0, 0, 0, (0, 1))
         subtract(2)
-        quantise_g(4, 1)
+        quantise_g(4)
         recover(4)
-        quantise_rest(0, 2)
-        product_q(0, 0, 2, 3)
+        quantise_rest(0)
+        product(0, 0, 0, (2, 3))
         subtract(3)
-        quantise_g(5, 1)
+        quantise_g(5)
         recover(5)
-        product_r_piece(0, 0, 0, 1)
+        product(1, 0, 0, (0, 1), 0, PIECE)
         subtract(4)
-        quantise_g(6, 1)
+        quantise_g(6)
         recover(6)
-        quantise_rest(2, 2)
-        product_r_piece(0, 0, 2, 3)
-        product_r_piece(0, 1, 0, 1)
+        quantise_rest(2)
+        product(1, 0, 0, (2, 3), 0, PIECE)
+        product(1, 0, 0, (0, 1), PIECE, HALF)
         subtract(5)
-        quantise_g(7, 1)
+        quantise_g(7)
         recover(7)
-        product_r_piece(0, 1, 2, 3)
+        product(1, 0, 0, (2, 3), PIECE, HALF)
+        product(0, 0, 1, (0,))
         subtract(6)
-        quantise_g(8, 1)
+        quantise_g(8)
         recover(8)
-        quantise_rest(4, 2)
-        product_q(0, 1, 0, 1)
+        quantise_rest(4)
+        product(0, 0, 1, (1, 2))
         subtract(7)
-        quantise_g(9, 1)
+        quantise_g(9)
         recover(9)
-        product_q(0, 1, 3, 2)
+        product(0, 0, 1, (3,))
+
         subtract(8)
-        quantise_g(10, 1)
-        recover(10)
-        quantise_rest(6, 2)
-        product_r(0, 1, 0, 1)
+        quantise_rest(6)
+        quantise_g(10, 2)
+        product(1, 0, 1, (0, 1))
+        recover(10, 11)
+        product(1, 0, 1, (3, 2))
         subtract(9)
-        quantise_g(11, 1)
-        recover(11)
-        product_r(0, 1, 3)
-        scale(0)
-        round_g(nc.scalar.copy, 14, 2)
-        scale(1)
-        subtract(10)
         quantise_g(12, 2)
-        recover(12)
-        add_res(0, BANK, "g_words6")
-        quantise_rest(8, 2)
-        product_r(0, 1, 2)
-        scale(2, 128)
-        product_q(1, 0, 0, 1)
-        subtract(11)
-        recover(13)
-        product_q(1, 0, 2, 3)
-        product_q(1, 1, 0, 1, 2, 3)
-        subtract(12)
-        finish_half(3)
+        recover(12, 13)
+        quantise_rest(8)
+        scale(0, 0, 0, HALF, 0)
+        round_g(nc.scalar.copy, 14, 2)
+        scale(0, 1, 0, HALF, HALF)
+        scale(0, 2, 0, 320, 2 * HALF)
+        add_res(result_of("a0", HALF, "g_words12")[:], scaled[:, 0:HALF], res_of(0, 0, HALF))
+        store(nc.sync, 0, 0, result_of("a0", HALF)[:])
+        product(0, 1, 0, (0, 1))
+        product(1, 1, 0, (0, 1))
+        product(0, 1, 1, (0, 1))
+        subtract(10, 11)
+        finish(0, 3, result_of("a3", HALF)[:])
+        store(nc.sync, 3, 0, result_of("a3", HALF)[:])
         quantise_g(14, 2)
-        recover(14)
-        recover(15)
-        add_res(BANK, 2 * BANK + 128, "g_words7")
-        quantise_rest(10, 2)
-        subtract(13)
-        product_r(1, 0, 0, 1, 2, 3)
-        product_r(1, 1, 0, 1, 2, 3)
-        product_q(2, 0, 0, 1)
-        product_q(2, 1, 0, 1)
-        product_q(2, 0, 2, 3)
-        product_q(2, 1, 2, 3)
-        subtract(14)
-        subtract(15)
-        finish_half(2, 128, BANK)
+        product(0, 1, 0, (2, 3))
+        recover(14, 15)
+        quantise_rest(10)
+        add_res(result_of("a1", 2 * HALF, "g_words14")[:, 0:HALF + 320], scaled[:, HALF:2 * HALF + 320], res_of(1, 0, HALF + 320))
+        store(nc.sync, 1, 0, result_of("a1", 2 * HALF)[:, 0:HALF])
+        product(1, 1, 1, (0, 1))
+        product(1, 1, 0, (2, 3))
+        product(0, 1, 1, (2, 3))
+        product(1, 1, 1, (2, 3))
+        subtract(13, 12, 15, 14)
+        product(0, 2, 0, (0, 1, 2, 3))
+        product(0, 2, 1, (0, 1, 2, 3))
+        finish(0, 2, result_of("a1", 2 * HALF)[:, HALF + 320:2 * HALF], 320, HALF)
+        store(nc.sync, 2, 0, result_of("a1", 2 * HALF)[:, HALF:2 * HALF])
         quantise_rest(12, 4)
-        product_r(2, 0, 0, 1)
-        product_r(2, 1, 0, 1)
-        product_r(2, 0, 2, 3)
-        product_r(2, 1, 2, 3)
-        finish(1, 0)
-        store_tile(1, 0, nc.scalar)
-        finish(1, 1)
-        store_tile(1, 1, nc.sync)
-        finish(1, 2)
-        store_tile(1, 2, nc.scalar)
-        finish(1, 3)
-        store_tile(1, 3, nc.sync)
-        finish(2, 0)
-        store_tile(2, 0, nc.scalar)
-        finish(2, 1)
-        store_tile(2, 1, nc.sync)
-        finish(2, 2)
-        store_tile(2, 2, nc.scalar)
-        finish(2, 3)
-        store_tile(2, 3, nc.sync)
+        product(1, 2, 0, (0, 1))
+        product(1, 2, 1, (0, 1))
+        product(1, 2, 0, (2, 3))
+        product(1, 2, 1, (2, 3))
+        for n in (3, 2, 1, 0): finish(1, n, result_of("b%d" % n, PIECE)[:]); store(nc.sync if n % 2 == 0 else nc.scalar, n, HALF, result_of("b%d" % n, PIECE)[:])
+        for n in range(4): finish(2, n, result_of("c%d" % n, PIECE)[:]); store(nc.sync if n % 2 else nc.scalar, n, HALF + PIECE, result_of("c%d" % n, PIECE)[:])

@@ -87,35 +87,41 @@ def tile_mix_tierg_ls_kernel(tc, g, w4_words, w4_scales, res, ls, out):
 
         nc.gpsimd.iota(ramp[:], pattern=[[1, 2 * P]], base=0, channel_multiplier=-2)
         nc.vector.memset(ls_rows[:], 0.0)
-        for j in range(PACK):
-            nc.vector.tensor_scalar(
-                out=eye_pairs[:, j, :],
-                in0=ramp[:],
-                scalar1=float(j // 2),
-                scalar2=float(BF16_ONE << (16 * (j % 2))),
-                op0=ALU.is_equal,
-                op1=ALU.mult,
+
+        def mark_eye(*rows):
+            for j in rows:
+                nc.vector.tensor_scalar(
+                    out=eye_pairs[:, j, :],
+                    in0=ramp[:],
+                    scalar1=float(j // 2),
+                    scalar2=float(BF16_ONE << (16 * (j % 2))),
+                    op0=ALU.is_equal,
+                    op1=ALU.mult,
+                )
+
+        def zero_scales():
+            nc.vector.memset(w_scales[:].rearrange("p a n -> p (a n)").bitcast(I32), 0)
+
+        def quantise_eye(j, count):
+            nc.vector.quantize_mx(
+                out=eye_codes[:, j * P : (j + count) * P].bitcast(E4M3),
+                scales=eye_scales[:, j * P : (j + count) * P],
+                in_=eye_pairs[:, j : j + count, :].rearrange("p j w -> p (j w)").bitcast(BF16),
             )
-        nc.vector.memset(w_scales[:].rearrange("p a n -> p (a n)").bitcast(I32), 0)
-        nc.vector.quantize_mx(
-            out=eye_codes[:].bitcast(E4M3),
-            scales=eye_scales[:],
-            in_=eye_pairs[:].rearrange("p j w -> p (j w)").bitcast(BF16),
-        )
 
         values = {}
         sums = {}
         results = {}
 
-        def warm_tensor(passes):
+        def warm_tensor(passes, width=BANK):
             warm_bank = psum.tile([P, BANK], F32, name="warm_bank", tag="bank0")
             for count in range(passes):
                 nc.tensor.matmul_mx(
-                    out=warm_bank[:],
+                    out=warm_bank[:, 0:width],
                     lhsT=eye_codes[:, 0:P].bitcast(E4M3),
                     lhsT_scale=eye_scales[:, 0:P],
-                    rhs=eye_codes[:].bitcast(E5M2),
-                    rhs_scale=eye_scales[:],
+                    rhs=eye_codes[:, 0:width].bitcast(E5M2),
+                    rhs_scale=eye_scales[:, 0:width],
                     start=True,
                     stop=True,
                 )
@@ -185,6 +191,10 @@ def tile_mix_tierg_ls_kernel(tc, g, w4_words, w4_scales, res, ls, out):
 
         def round_g(copy, s, count=1):
             copy(out=walk_words(g_as_words(s, count), PAIR), in_=walk_rows(rows_of(s, count), PAIR))
+
+        def round_part(copy, s, lo, hi):
+            words = g_as_words(s, 1)[:, lo * PACK : hi * PACK]
+            copy(out=walk_words(words, PAIR), in_=walk_rows(rows_of(s, 1)[:, :, lo:hi], PAIR))
 
         def quantise_g(s, count=1):
             nc.vector.quantize_mx(
@@ -279,6 +289,10 @@ def tile_mix_tierg_ls_kernel(tc, g, w4_words, w4_scales, res, ls, out):
         def store(queue, n, t0, src):
             queue.dma_start(out=out[n * P : (n + 1) * P, t0 : t0 + src.shape[1]], in_=src)
 
+        mark_eye(0, 1)
+        zero_scales()
+        quantise_eye(0, 2)
+        mark_eye(2, 3)
 
         load_g(0)
         load_g(1)
@@ -295,8 +309,10 @@ def tile_mix_tierg_ls_kernel(tc, g, w4_words, w4_scales, res, ls, out):
         load_g(8)
         for n in (0, 3, 1, 2): load_res_half(n)
         for i in range(len(RES_LOADS)): load_res(i)
-        warm_tensor(2)
+        warm_tensor(4, PIECE)
+
         round_g(nc.vector.tensor_copy, 0)
+        quantise_eye(2, 2)
         quantise_g(0)
         recover(0)
         round_g(nc.vector.tensor_copy, 1)
@@ -356,7 +372,7 @@ def tile_mix_tierg_ls_kernel(tc, g, w4_words, w4_scales, res, ls, out):
         scale(0, 0, 0, HALF, 0)
         round_g(nc.scalar.copy, 14, 2)
         scale(0, 1, 0, HALF, HALF)
-        scale(0, 2, 0, 320, 2 * HALF)
+        scale(0, 2, 0, 256, 2 * HALF)
         add_res(result_of("a0", HALF, "g_words12")[:], scaled[:, 0:HALF], res_of(0, 0, HALF))
         store(nc.sync, 0, 0, result_of("a0", HALF)[:])
         product(0, 1, 0, (0, 1))
@@ -369,7 +385,7 @@ def tile_mix_tierg_ls_kernel(tc, g, w4_words, w4_scales, res, ls, out):
         product(0, 1, 0, (2, 3))
         recover(14, 15)
         quantise_rest(10)
-        add_res(result_of("a1", 2 * HALF, "g_words14")[:, 0:HALF + 320], scaled[:, HALF:2 * HALF + 320], res_of(1, 0, HALF + 320))
+        add_res(result_of("a1", 2 * HALF, "g_words14")[:, 0:HALF + 256], scaled[:, HALF:2 * HALF + 256], res_of(1, 0, HALF + 256))
         store(nc.sync, 1, 0, result_of("a1", 2 * HALF)[:, 0:HALF])
         product(1, 1, 1, (0, 1))
         product(1, 1, 0, (2, 3))
@@ -378,7 +394,7 @@ def tile_mix_tierg_ls_kernel(tc, g, w4_words, w4_scales, res, ls, out):
         subtract(13, 12, 15, 14)
         product(0, 2, 0, (0, 1, 2, 3))
         product(0, 2, 1, (0, 1, 2, 3))
-        finish(0, 2, result_of("a1", 2 * HALF)[:, HALF + 320:2 * HALF], 320, HALF)
+        finish(0, 2, result_of("a1", 2 * HALF)[:, HALF + 256:2 * HALF], 256, HALF)
         store(nc.sync, 2, 0, result_of("a1", 2 * HALF)[:, HALF:2 * HALF])
         quantise_rest(12, 4)
         product(1, 2, 0, (0, 1))

@@ -113,19 +113,6 @@ def tile_mix_tierg_ls_kernel(tc, g, w4_words, w4_scales, res, ls, out):
         sums = {}
         results = {}
 
-        def warm_tensor(passes, width=BANK):
-            warm_bank = psum.tile([P, BANK], F32, name="warm_bank", tag="bank0")
-            for count in range(passes):
-                nc.tensor.matmul_mx(
-                    out=warm_bank[:, 0:width],
-                    lhsT=eye_codes[:, 0:P].bitcast(E4M3),
-                    lhsT_scale=eye_scales[:, 0:P],
-                    rhs=eye_codes[:, 0:width].bitcast(E5M2),
-                    rhs_scale=eye_scales[:, 0:width],
-                    start=True,
-                    stop=True,
-                )
-
         def load_g(i):
             strips = LOADS[i]
             a, t0 = STRIP_AT[strips[0]]
@@ -309,7 +296,6 @@ def tile_mix_tierg_ls_kernel(tc, g, w4_words, w4_scales, res, ls, out):
         load_g(8)
         for n in (0, 3, 1, 2): load_res_half(n)
         for i in range(len(RES_LOADS)): load_res(i)
-        warm_tensor(4, PIECE)
 
         round_g(nc.vector.tensor_copy, 0)
         quantise_eye(2, 2)

from contextlib import ExitStack

import concourse.mybir as mybir

K, N, T = 1024, 512, 1024
FLOPS = 2 * 2 * K * N * T

F32 = mybir.dt.float32
BF16 = mybir.dt.bfloat16
U32 = mybir.dt.uint32
I32 = mybir.dt.int32
U8 = mybir.dt.uint8
E4M3 = mybir.dt.float8_e4m3fn_x4
E5M2 = mybir.dt.float8_e5m2_x4
E2M1 = mybir.dt.float4_e2m1fn_x4
ALU = mybir.AluOpType
ACT = mybir.ActivationFunctionType

P = 128
PACK = 4
K_PASS = P * PACK
BANK = 512
STRIP = BANK // PACK
PIECE = 2 * STRIP
HALF = T // 2
PASSES = K // K_PASS
STRIPS = PASSES * T // STRIP
N_TILES = N // P
QUAD = 32
PAIR = 2
LINE = 4
BF16_ONE = 0x3F80
LOADS = ((0,), (1, 2), (3,), (4, 5), (6, 7), (8, 9), (10, 11), (12, 13), (14, 15))
STRETCHES = ((0, HALF, (0, 1, 2, 3)), (HALF, PIECE, (0, 3)), (HALF + PIECE, PIECE, (4, 5)))
STRIP_AT = tuple((a, t0 + lo) for t0, width, banks in STRETCHES for a in range(PASSES) for lo in range(0, width, STRIP))
VALUE_BANKS = tuple(4 + s % 4 for s in range(STRIPS))
WORD_GROUPS = tuple((s, s + 1) for s in range(0, STRIPS, 2))
REST_GROUPS = ((0, 1), (2, 3), (4, 5), (6, 7), (8, 9), (10, 11), (12, 13, 14, 15))
RES_LOADS = ((0, 2, HALF, HALF), (2, 2, HALF, HALF))


def tile_mix_tierg_ls_kernel(tc, g, w4_words, w4_scales, res, ls, out):
    nc = tc.nc
    with ExitStack() as ctx:
        sb = ctx.enter_context(tc.tile_pool(name="sb", bufs=1))
        psum = ctx.enter_context(tc.psum_pool(name="psum", bufs=1))
        ctx.enter_context(tc.manual_schedule())

        def tile(name, shape, dtype, tag=None):
            return sb.tile(shape, dtype, name=name, tag=tag or name, align_bytes=64)

        g_rows = {}
        for strips in LOADS:
            rows = tile("g_rows%d" % strips[0], [P, PACK, len(strips) * STRIP], F32)
            for s in strips:
                g_rows[s] = (rows, strips[0])
        g_words = {}
        for group in WORD_GROUPS:
            words = tile("g_words%d" % group[0], [P, len(group) * BANK], BF16)
            for s in group:
                g_words[s] = (words, group[0])
        rest_words = {}
        for group in REST_GROUPS:
            words = tile("rest_words%d" % group[0], [P, len(group) * BANK], BF16)
            for s in group:
                rest_words[s] = (words, group[0])
        q_codes = tile("q_codes", [P, STRIPS * STRIP], U32)
        q_scales = tile("q_scales", [P, STRIPS * STRIP], U8)
        r_codes = tile("r_codes", [P, STRIPS * STRIP], U32)
        r_scales = tile("r_scales", [P, STRIPS * STRIP], U8)
        w_words = [tile("w_words%d" % a, [P, 2 * N], U8) for a in range(PASSES)]
        w_scales = tile("w_scales", [P, PASSES, N], U8)
        ls_rows = tile("ls_rows", [P, N_TILES * QUAD], F32)
        ls_cols = tile("ls_cols", [P, N_TILES * QUAD], F32)
        res_at = {}
        for i, (n0, count, t0, width) in enumerate(RES_LOADS):
            rows = tile("res%d" % i, [P, count, width], F32)
            for n in range(n0, n0 + count):
                for t in range(t0, t0 + width, STRIP):
                    res_at[(n, t)] = (rows, n0, t0)
        res_half = tile("res_half", [P, N_TILES * HALF], F32)
        scaled = tile("scaled", [P, N_TILES * HALF], F32)
        ramp = tile("ramp", [P, 2 * P], I32)
        eye_pairs = tile("eye_pairs", [P, PACK, 2 * P], I32)
        eye_codes = tile("eye_codes", [P, PACK * P], U32)
        eye_scales = tile("eye_scales", [P, PACK * P], U8)

        nc.gpsimd.iota(ramp[:], pattern=[[1, 2 * P]], base=0, channel_multiplier=-2)
        nc.vector.memset(ls_rows[:], 0.0)

        def mark_eye(*rows):
            for j in rows:
                nc.vector.tensor_scalar(
                    out=eye_pairs[:, j, :],
                    in0=ramp[:],
                    scalar1=float(j // 2),
                    scalar2=float(BF16_ONE << (16 * (j % 2))),
                    op0=ALU.is_equal,
                    op1=ALU.mult,
                )

        def zero_scales():
            nc.vector.memset(w_scales[:].rearrange("p a n -> p (a n)").bitcast(I32), 0)

        def quantise_eye(j, count):
            nc.vector.quantize_mx(
                out=eye_codes[:, j * P : (j + count) * P].bitcast(E4M3),
                scales=eye_scales[:, j * P : (j + count) * P],
                in_=eye_pairs[:, j : j + count, :].rearrange("p j w -> p (j w)").bitcast(BF16),
            )

        values = {}
        sums = {}
        results = {}

        def load_g(i):
            strips = LOADS[i]
            a, t0 = STRIP_AT[strips[0]]
            rows = g[a * K_PASS : (a + 1) * K_PASS, t0 : t0 + len(strips) * STRIP]
            nc.sync.dma_start(out=g_rows[strips[0]][0][:], in_=rows.rearrange("(p j) w -> p j w", j=PACK))

        def load_words(a):
            nc.sync.dma_start(out=w_words[a][:], in_=w4_words[a])

        def load_scales(queue):
            for r in range(4):
                queue.dma_start(
                    out=w_scales[r:P:32, :, :].bitcast(I32),
                    in_=w4_scales[:, r:16:4, :].rearrange("a q n -> q a n").bitcast(I32),
                )

        def load_ls(queue):
            queue.dma_start(
                out=ls_rows[0:P:QUAD, :].rearrange("q (c i) -> q c i", i=QUAD),
                in_=ls.rearrange("(c q i) -> q c i", c=N_TILES, i=QUAD),
            )

        def turn_ls():
            nc.vector.transpose(out=ls_cols[:], in_=ls_rows[:])

        def ls_of(n):
            return ls_cols[:, n * QUAD : n * QUAD + 1]

        def load_res(i):
            n0, count, t0, width = RES_LOADS[i]
            rows = res[n0 * P : (n0 + count) * P, t0 : t0 + width]
            nc.sync.dma_start(out=res_at[(n0, t0)][0][:], in_=rows.rearrange("(c p) w -> p c w", p=P))

        def load_res_half(n):
            nc.sync.dma_start(out=res_half[:, n * HALF : (n + 1) * HALF], in_=res[n * P : (n + 1) * P, 0:HALF])

        def res_of(n, t, width):
            if t < HALF:
                return res_half[:, n * HALF + t : n * HALF + t + width]
            rows, n0, t0 = res_at[(n, t)]
            return rows[:, n - n0, t - t0 : t - t0 + width]

        def g_as_words(s, count):
            words, first = g_words[s]
            return words[:, (s - first) * BANK : (s - first + count) * BANK]

        def rest_as_words(s, count):
            words, first = rest_words[s]
            return words[:, (s - first) * BANK : (s - first + count) * BANK]

        def walk_words(words, run):
            return words.rearrange("p (c i j) -> p c j i", i=run, j=PACK)

        def walk_rows(rows, run):
            return rows.rearrange("p j (c i) -> p c j i", i=run)

        def rows_of(s, count):
            rows, first = g_rows[s]
            return rows[:, :, (s - first) * STRIP : (s - first + count) * STRIP]

        def strip_cols(rows, s, count):
            return rows[:, s * STRIP : (s + count) * STRIP]

        def round_g(copy, s, count=1):
            copy(out=walk_words(g_as_words(s, count), PAIR), in_=walk_rows(rows_of(s, count), PAIR))

        def round_part(copy, s, lo, hi):
            words = g_as_words(s, 1)[:, lo * PACK : hi * PACK]
            copy(out=walk_words(words, PAIR), in_=walk_rows(rows_of(s, 1)[:, :, lo:hi], PAIR))

        def quantise_g(s, count=1):
            nc.vector.quantize_mx(
                out=strip_cols(q_codes, s, count).bitcast(E5M2),
                scales=strip_cols(q_scales, s, count),
                in_=g_as_words(s, count),
            )

        def quantise_rest(s, count=2):
            nc.vector.quantize_mx(
                out=strip_cols(r_codes, s, count).bitcast(E4M3),
                scales=strip_cols(r_scales, s, count),
                in_=rest_as_words(s, count),
            )

        def recover(*strips):
            for s in strips:
                values[s] = psum.tile([P, PACK, STRIP], F32, name="values%d" % s, tag="bank%d" % VALUE_BANKS[s])
                for j in range(PACK):
                    cols = slice(j * P, (j + 1) * P)
                    nc.tensor.matmul_mx(
                        out=values[s][:, j, :],
                        lhsT=eye_codes[:, cols].bitcast(E4M3),
                        lhsT_scale=eye_scales[:, cols],
                        rhs=strip_cols(q_codes, s, 1).bitcast(E5M2),
                        rhs_scale=strip_cols(q_scales, s, 1),
                        start=True,
                        stop=True,
                    )

        def subtract(*strips):
            for s in strips:
                nc.vector.tensor_tensor(
                    out=walk_words(rest_as_words(s, 1), LINE),
                    in0=walk_rows(rows_of(s, 1), LINE),
                    in1=walk_rows(values[s][:], LINE),
                    op=ALU.subtract,
                )

        def sum_of(b, n):
            t0, width, banks = STRETCHES[b]
            share = BANK // width
            if (b, n // share) not in sums:
                name = "sums%d_%d" % (b, n // share)
                sums[(b, n // share)] = psum.tile([P, share, width], F32, name=name, tag="bank%d" % banks[n // share])
            return sums[(b, n // share)][:, n % share, :]

        passes_done = {}

        def product(tier, b, a, n_tiles, lo=0, hi=None):
            codes, scales, fmt = ((q_codes, q_scales, E5M2), (r_codes, r_scales, E4M3))[tier]
            t0, width, banks = STRETCHES[b]
            share = BANK // width
            hi = width if hi is None else hi
            first = STRIP_AT.index((a, t0 + lo)) * STRIP
            for n in n_tiles:
                done = passes_done.get((b, n // share), 0)
                passes_done[(b, n // share)] = done + hi - lo
                nc.tensor.matmul_mx(
                    out=sum_of(b, n)[:, lo:hi],
                    lhsT=w_words[a][:, 2 * P * n : 2 * P * (n + 1)].bitcast(E2M1),
                    lhsT_scale=w_scales[:, a, P * n : P * (n + 1)],
                    rhs=codes[:, first : first + hi - lo].bitcast(fmt),
                    rhs_scale=scales[:, first : first + hi - lo],
                    start=done == 0,
                    stop=done + hi - lo == 2 * PASSES * BANK,
                )

        def result_of(key, width, tag=None):
            if key not in results:
                results[key] = tile("out_%s" % key, [P, width], F32, tag=tag)
            return results[key]

        def scale(b, n, lo, hi, at):
            nc.scalar.activation(out=scaled[:, at : at + hi - lo], in_=sum_of(b, n)[:, lo:hi], func=ACT.Copy, scale=ls_of(n))

        def add_res(dst, at, src):
            nc.gpsimd.tensor_tensor(out=dst, in0=at, in1=src, op=ALU.add)

        def finish(b, n, dst, lo=0, hi=None):
            t0, width, banks = STRETCHES[b]
            hi = width if hi is None else hi
            nc.vector.scalar_tensor_tensor(
                out=dst,
                in0=sum_of(b, n)[:, lo:hi],
                scalar=ls_of(n),
                in1=res_of(n, t0 + lo, hi - lo),
                op0=ALU.mult,
                op1=ALU.add,
            )

        def store(queue, n, t0, src):
            queue.dma_start(out=out[n * P : (n + 1) * P, t0 : t0 + src.shape[1]], in_=src)

        mark_eye(0, 1)
        zero_scales()
        quantise_eye(0, 2)
        mark_eye(2, 3)

        load_g(0)
        load_g(1)
        load_ls(nc.sync)
        load_g(2)
        load_g(3)
        load_words(0)
        load_scales(nc.sync)
        load_g(4)
        load_g(5)
        load_words(1)
        load_g(6)
        load_g(7)
        load_g(8)
        for n in (0, 3, 1, 2): load_res_half(n)
        for i in range(len(RES_LOADS)): load_res(i)

        round_g(nc.vector.tensor_copy, 0)
        quantise_eye(2, 2)
        quantise_g(0)
        recover(0)
        round_g(nc.vector.tensor_copy, 1)
        turn_ls()
        for s in range(2, 10): round_g(nc.scalar.copy, s)
        round_g(nc.scalar.copy, 10, 2)
        round_g(nc.scalar.copy, 12, 2)
        quantise_g(1)
        recover(1)
        quantise_g(2)
        recover(2)
        subtract(0)
        quantise_g(3)
        recover(3)
        subtract(1)
        product(0, 0, 0, (0, 1))
        subtract(2)
        quantise_g(4)
        recover(4)
        quantise_rest(0)
        product(0, 0, 0, (2, 3))
        subtract(3)
        quantise_g(5)
        recover(5)
        product(1, 0, 0, (0, 1), 0, PIECE)
        subtract(4)
        quantise_g(6)
        recover(6)
        quantise_rest(2)
        product(1, 0, 0, (2, 3), 0, PIECE)
        product(1, 0, 0, (0, 1), PIECE, HALF)
        subtract(5)
        quantise_g(7)
        recover(7)
        product(1, 0, 0, (2, 3), PIECE, HALF)
        product(0, 0, 1, (0,))
        subtract(6)
        quantise_g(8)
        recover(8)
        quantise_rest(4)
        product(0, 0, 1, (1, 2))
        subtract(7)
        quantise_g(9)
        recover(9)
        product(0, 0, 1, (3,))

        subtract(8)
        quantise_rest(6)
        quantise_g(10, 2)
        product(1, 0, 1, (0, 1))
        recover(10, 11)
        product(1, 0, 1, (3, 2))
        subtract(9)
        quantise_g(12, 2)
        recover(12, 13)
        quantise_rest(8)
        scale(0, 0, 0, HALF, 0)
        round_g(nc.scalar.copy, 14, 2)
        scale(0, 1, 0, HALF, HALF)
        scale(0, 2, 0, 256, 2 * HALF)
        add_res(result_of("a0", HALF, "g_words12")[:], scaled[:, 0:HALF], res_of(0, 0, HALF))
        store(nc.sync, 0, 0, result_of("a0", HALF)[:])
        product(0, 1, 0, (0, 1))
        product(1, 1, 0, (0, 1))
        product(0, 1, 1, (0, 1))
        subtract(10, 11)
        finish(0, 3, result_of("a3", HALF)[:])
        store(nc.sync, 3, 0, result_of("a3", HALF)[:])
        quantise_g(14, 2)
        product(0, 1, 0, (2, 3))
        recover(14, 15)
        quantise_rest(10)
        add_res(result_of("a1", 2 * HALF, "g_words14")[:, 0:HALF + 256], scaled[:, HALF:2 * HALF + 256], res_of(1, 0, HALF + 256))
        store(nc.sync, 1, 0, result_of("a1", 2 * HALF)[:, 0:HALF])
        product(1, 1, 1, (0, 1))
        product(1, 1, 0, (2, 3))
        product(0, 1, 1, (2, 3))
        product(1, 1, 1, (2, 3))
        subtract(13, 12, 15, 14)
        product(0, 2, 0, (0, 1, 2, 3))
        product(0, 2, 1, (0, 1, 2, 3))
        finish(0, 2, result_of("a1", 2 * HALF)[:, HALF + 256:2 * HALF], 256, HALF)
        store(nc.sync, 2, 0, result_of("a1", 2 * HALF)[:, HALF:2 * HALF])
        quantise_rest(12, 4)
        product(1, 2, 0, (0, 1))
        product(1, 2, 1, (0, 1))
        product(1, 2, 0, (2, 3))
        product(1, 2, 1, (2, 3))
        for n in (3, 2, 1, 0): finish(1, n, result_of("b%d" % n, PIECE)[:]); store(nc.sync if n % 2 == 0 else nc.scalar, n, HALF, result_of("b%d" % n, PIECE)[:])
        for n in range(4): finish(2, n, result_of("c%d" % n, PIECE)[:]); store(nc.sync if n % 2 else nc.scalar, n, HALF + PIECE, result_of("c%d" % n, PIECE)[:])
